import numpy as np
import ml_dtypes


def mxq(x, axis, fmt="e4m3"):
    dtype, down = {"e4m3": (ml_dtypes.float8_e4m3fn, 7), "e5m2": (ml_dtypes.float8_e5m2, 14)}[fmt]
    v = np.moveaxis(np.asarray(x, np.float32).astype(ml_dtypes.bfloat16).astype(np.float64), axis, -1)
    blocks = v.reshape(v.shape[:-1] + (-1, 32))
    amax = np.abs(blocks).max(-1, keepdims=True)
    byte = np.maximum(np.where(amax > 0, np.frexp(amax)[1] - 1 + 127, 0) - down, 1)
    scale = np.exp2(byte - 127.0)
    codes = (blocks / scale).astype(np.float32).astype(dtype).astype(np.float64)
    return np.moveaxis((codes * scale).reshape(v.shape), -1, axis)


WIDE = False


def mx_kscale(k):
    if not WIDE:
        return np.ones(k)
    levels = np.array([10, -10, 5, -5, 0])
    if k % 512:
        return np.exp2(np.random.permutation(np.resize(levels, k // 32))).repeat(32)
    a = np.empty((k // 512, 16))
    for p in range(k // 512):
        a[p, :8] = np.random.permutation(np.resize(levels, 8))
        for g in range(8):
            far = levels[np.abs(levels - a[p, g]) >= 10]
            a[p, g + 8] = far[np.random.randint(len(far))]
    return np.exp2(a.ravel()).repeat(32)


def f64(x):
    return np.asarray(x).astype(np.float64)


def striped(idx):
    return np.tile(idx.reshape(-1, 16).T, (8, 1)).astype(np.uint16)


def unstriped(offs):
    return offs[:16].T.reshape(-1).astype(np.int64)


E2M1 = np.array([0.0, 0.5, 1.0, 1.5, 2.0, 3.0, 4.0, 6.0, -0.0, -0.5, -1.0, -1.5, -2.0, -3.0, -4.0, -6.0])


def pack_weight(w, fmt):
    k, n = w.shape
    w = f64(np.asarray(w, np.float32).astype(ml_dtypes.bfloat16)).reshape(k // 32, 32, n)
    amax = np.abs(w).max(1)
    if fmt == "e4m3":
        byte = np.frexp(amax)[1] - 1 + 127 - 7
    else:
        mant, ex = np.frexp(amax / 6.0)
        byte = np.where(mant > 0.5, ex, ex - 1) + 127
    byte = np.clip(np.where(amax > 0, byte, 1), 1, 254)
    scaled = (w * np.exp2(127.0 - byte)[:, None, :]).reshape(k, n).astype(np.float32)
    by_word = np.ascontiguousarray(scaled.reshape(k // 512, 128, 4, n).transpose(0, 1, 3, 2))
    if fmt == "e4m3":
        words = by_word.astype(ml_dtypes.float8_e4m3fn).view(np.uint8)
    else:
        c = by_word.astype(ml_dtypes.float4_e2m1fn).view(np.uint8) & 0xF
        words = (c[..., 0::2] | (c[..., 1::2] << 4)).reshape(k // 512, 128, 2 * n)
    return np.ascontiguousarray(words), np.ascontiguousarray(byte.astype(np.uint8).reshape(k // 512, 16, n))


def unpack_weight(words, scales, fmt):
    g, _, n = scales.shape
    words = np.ascontiguousarray(words).reshape(g, 128, n, -1)
    if fmt == "e4m3":
        vals = words.view(ml_dtypes.float8_e4m3fn).astype(np.float64)
    else:
        nib = np.empty((g, 128, n, 4), np.uint8)
        nib[..., 0::2] = words & 0xF
        nib[..., 1::2] = words >> 4
        vals = E2M1[nib]
    vals = vals * np.repeat(np.exp2(scales.astype(np.float64) - 127.0), 8, axis=1)[..., None]
    return vals.transpose(0, 1, 3, 2).reshape(g * 512, n)


def gelu(v):
    return 0.5 * v * (1.0 + np.tanh(np.sqrt(2.0 / np.pi) * (v + 0.044715 * v**3)))


def striped8(idx):
    return np.concatenate([v.reshape(-1, 16).T for v in idx]).astype(np.uint16)


def unstriped8(offs):
    return np.stack([offs[16 * g:16 * g + 16].T.reshape(-1) for g in range(8)]).astype(np.int64)


def runs(v, idx8):
    k = np.arange(v.shape[0])
    return v[k[:, None], idx8[k % 512 // 64]]


def put_heads(h, wgs, idx8, t2):
    r = np.arange(h.shape[0])
    page = np.zeros((h.shape[0], t2))
    page[r[:, None], idx8[r % 512 // 64]] = wgs[r // 4 % 128] * h
    return page


def often(T, S):
    return np.random.permutation(T)[(T * np.random.uniform(0, 1, S) ** 4).astype(np.int64)]


K, H, N, T, S, T2 = 1024, 512, 512, 2048, 1024, 2048

def setup_inputs():
    n = np.random.standard_normal
    s = mx_kscale(K)[:, None]
    u = mx_kscale(H)[:, None]
    tab_words, tab_scales = pack_weight(n((K, T)) * s, "e4m3")
    wa_words, wa_scales = pack_weight(n((K, H)) / np.sqrt(K) * u.T / s, "e2m1")
    wb = n((K, H)) / np.sqrt(K) * u.T / s
    wc_words, wc_scales = pack_weight(n((K, H)) / np.sqrt(K) * u.T / s, "e4m3")
    wd = n((H, N)) / np.sqrt(H) / u
    return {
        "tab_words": tab_words, "tab_scales": tab_scales,
        "offs": striped8(np.stack([often(T, S) for _ in range(8)])),
        "wa_words": wa_words, "wa_scales": wa_scales,
        "wb": wb.astype(np.float32),
        "wc_words": wc_words, "wc_scales": wc_scales,
        "wd": wd.astype(np.float32),
        "usual": n(N).astype(np.float32),
        "wgo": np.repeat(np.random.uniform(0.5, 2.0, (8, S)), 16, axis=0).astype(np.float32),
        "offs2": striped8(np.stack([np.random.permutation(T2)[:S] for _ in range(8)])),
    }

def reference(tab_words, tab_scales, offs, wa_words, wa_scales, wb, wc_words, wc_scales, wd, usual, wgo, offs2):
    v = runs(unpack_weight(tab_words, tab_scales, "e4m3"), unstriped8(offs))
    a = unpack_weight(wa_words, wa_scales, "e2m1").T @ v
    b = mxq(f64(wb), 0, "e4m3").T @ v
    c = unpack_weight(wc_words, wc_scales, "e4m3").T @ v
    top = np.maximum(np.maximum(a, b), c)
    low = np.minimum(np.minimum(a, b), c)
    h = top - low
    y = (mxq(f64(wd), 0, "e4m3").T @ mxq(h, 0, "e4m3")) - f64(usual)[:, None]
    return put_heads(y, f64(wgo), unstriped8(offs2), T2)

@@ -1,0 +1,229 @@
+from contextlib import ExitStack
+
+import concourse.mybir as mybir
+from concourse.masks import make_identity
+
+K, H, N, T, S, T2 = 1024, 512, 512, 2048, 1024, 2048
+FLOPS = 3 * 2 * K * H * S + 2 * H * N * S
+
+F32 = mybir.dt.float32
+BF16 = mybir.dt.bfloat16
+I32 = mybir.dt.int32
+U32 = mybir.dt.uint32
+U16 = mybir.dt.uint16
+U8 = mybir.dt.uint8
+FP8X4 = mybir.dt.float8_e4m3fn_x4
+FP4X4 = mybir.dt.float4_e2m1fn_x4
+ALU = mybir.AluOpType
+ACT = mybir.ActivationFunctionType
+
+P = 128
+TILES = S // P
+CHUNKS = ((0, 2), (2, 4), (4, 8))
+
+
+def tile_list_skill_disagreement_marks_kernel(
+    tc, tab_words, tab_scales, offs, wa_words, wa_scales, wb, wc_words, wc_scales, wd, usual, wgo, offs2, out
+):
+    nc = tc.nc
+    with ExitStack() as ctx:
+        lists = ctx.enter_context(tc.tile_pool(name="lists", bufs=1))
+        keep = ctx.enter_context(tc.tile_pool(name="keep", bufs=1))
+        ring = ctx.enter_context(tc.tile_pool(name="ring", bufs=3))
+        psum = ctx.enter_context(tc.psum_pool(name="psum", bufs=2))
+
+        offs_sb = lists.tile([P, S // 16], U16, name="offs_sb")
+        offs2_sb = lists.tile([P, S // 16], U16, name="offs2_sb")
+        nc.sync.dma_start(offs_sb[:], offs)
+        nc.sync.dma_start(offs2_sb[:], offs2)
+
+        tab_sc = keep.tile([P, T], U8, name="tab_sc", tag="slot_sc", align_bytes=64)
+        nc.vector.memset(tab_sc[:].bitcast(I32), 0)
+        for a in range(2):
+            nc.scalar.dma_start(tab_sc[a:P:8, :].bitcast(I32), tab_scales[a].bitcast(I32))
+        planes = [keep.tile([P, S], U8, name="plane%d" % a, align_bytes=64) for a in range(2)]
+        nc.vector.memset(planes[1][:].bitcast(I32), 0)
+
+        tab_w = [keep.tile([P, T], I32, name="tab_w%d" % a, tag="slot_w%d" % a, align_bytes=64) for a in range(2)]
+        for a in range(2):
+            nc.sync.dma_start(tab_w[a][:], tab_words[a].rearrange("p t i -> p (t i)").bitcast(I32))
+        wa_sb = keep.tile([P, 2, 2 * H], U8, name="wa_sb", align_bytes=64)
+        nc.sync.dma_start(wa_sb[:].bitcast(I32), wa_words.rearrange("a p n -> p a n").bitcast(I32))
+        wc_sb = keep.tile([P, 2, H], I32, name="wc_sb", align_bytes=64)
+        nc.sync.dma_start(wc_sb[:], wc_words.rearrange("a p e i -> p a (e i)").bitcast(I32))
+        wb_rows = wb.rearrange("(a p j) c -> a p j c", a=2, j=4)
+        wb_raw0 = keep.tile([P, 4, H], F32, name="wb_raw0")
+        nc.sync.dma_start(wb_raw0[:], wb_rows[0])
+
+        wa_sc = keep.tile([P, 2, H], U8, name="wa_sc", align_bytes=64)
+        wc_sc = keep.tile([P, 2, H], U8, name="wc_sc", align_bytes=64)
+        for sc, src in ((wa_sc, wa_scales), (wc_sc, wc_scales)):
+            nc.gpsimd.memset(sc[:].bitcast(I32), 0)
+            for d in range(4):
+                nc.gpsimd.dma_start(
+                    sc[32 * d : 32 * d + 4].bitcast(I32),
+                    src[:, 4 * d : 4 * d + 4, :].rearrange("a r e -> r a e").bitcast(I32),
+                )
+        usual_sb = keep.tile([P, 4], F32, name="usual_sb")
+        nc.gpsimd.dma_start(usual_sb[:], usual.rearrange("(p i) -> p i", i=4))
+        ident = keep.tile([P, P], F32, name="ident")
+        make_identity(nc, ident[:])
+        pages = [keep.tile([P, T2], F32, name="page%d" % i) for i in range(4)]
+        neg_usual = keep.tile([P, 4], F32, name="neg_usual")
+        nc.gpsimd.tensor_scalar(neg_usual[:], usual_sb[:], -1.0, 0.0, ALU.mult, ALU.add)
+        for page in pages[:2]:
+            nc.vector.memset(page[:], 0.0)
+        for page in pages[2:]:
+            for half in range(2):
+                nc.gpsimd.memset(page[:, 1024 * half : 1024 * (half + 1)], 0.0)
+
+        picked_sc = keep.tile([P, S], U8, name="picked_sc", align_bytes=64)
+        nc.vector.tensor_copy(picked_sc[:], tab_sc[:].indirect(offs_sb[:]))
+        nc.vector.tensor_copy(planes[0][:].bitcast(I32), picked_sc[:].bitcast(I32))
+        for a in range(2):
+            for r in range(1 - a, 4):
+                nc.scalar.dma_start(planes[a][r:P:32, :].bitcast(I32), picked_sc[8 * r + a : P : 32, :].bitcast(I32))
+        picked = [keep.tile([P, S], U32, name="picked%d" % a, align_bytes=64) for a in range(2)]
+        nc.vector.tensor_copy(picked[0][:], tab_w[0][:].bitcast(U32).indirect(offs_sb[:]))
+        for half in range(2):
+            nc.vector.tensor_copy(
+                picked[1][:, 512 * half : 512 * (half + 1)],
+                tab_w[1][:].bitcast(U32).indirect(offs_sb[:, 32 * half : 32 * (half + 1)]),
+            )
+
+        wb_raw1 = keep.tile([P, 4, H], F32, name="wb_raw1", tag="slot_sc", align_bytes=64)
+        nc.sync.dma_start(wb_raw1[:], wb_rows[1])
+        wd_raw = keep.tile([P, 4, N], F32, name="wd_raw", tag="slot_w0", align_bytes=64)
+        nc.sync.dma_start(wd_raw[:], wd.rearrange("(p j) c -> p j c", j=4))
+        wgo_sb = keep.tile([P, S], F32, name="wgo_sb", tag="slot_w1", align_bytes=64)
+        nc.sync.dma_start(wgo_sb[:], wgo)
+
+        wb_bf = [keep.tile([P, H, 4], BF16, name="wb_bf%d" % a, align_bytes=64) for a in range(2)]
+        wb_q = [keep.tile([P, H], U32, name="wb_q%d" % a, align_bytes=64) for a in range(2)]
+        wb_sc = [keep.tile([P, H], U8, name="wb_sc%d" % a, align_bytes=64) for a in range(2)]
+
+        def prepare_wb(a, raw):
+            nc.scalar.copy(
+                wb_bf[a][:].rearrange("p (c i) j -> p c j i", i=4), raw[:].rearrange("p j (c i) -> p c j i", i=4)
+            )
+            nc.vector.quantize_mx(
+                out=wb_q[a][:].bitcast(FP8X4), scales=wb_sc[a][:], in_=wb_bf[a][:].rearrange("p c j -> p (c j)")
+            )
+
+        def product(k, rhs, rhs_sc):
+            acc = psum.tile([P, H], F32, name="acc", tag="acc", bufs=4)
+            for a in range(2):
+                nc.tensor.matmul_mx(
+                    out=acc[:],
+                    lhsT=picked[a][:, P * k : P * (k + 1)].bitcast(FP8X4),
+                    lhsT_scale=planes[a][:, P * k : P * (k + 1)],
+                    rhs=rhs[a],
+                    rhs_scale=rhs_sc[a],
+                    start=(a == 0),
+                    stop=(a == 1),
+                )
+            return acc[:].rearrange("p (m t) -> p t m", t=4)
+
+        wa_ops = [wa_sb[:, a, :].bitcast(FP4X4) for a in range(2)]
+        wc_ops = [wc_sb[:, a, :].bitcast(FP8X4) for a in range(2)]
+        c_sb, d_sb, rd_sb = [], [], []
+
+        def first(k):
+            c_ps = product(k, wc_ops, [wc_sc[:, a, :] for a in range(2)])
+            a_ps = product(k, wa_ops, [wa_sc[:, a, :] for a in range(2)])
+            c_k = keep.tile([P, 4, P], F32, name="c_k", tag="late" if k == TILES - 1 else "c%d" % k)
+            nc.scalar.copy(c_k[:], c_ps)
+            d_k = keep.tile([P, 4, P], F32, name="d%d" % k)
+            nc.vector.tensor_tensor(d_k[:], a_ps, c_k[:], ALU.subtract)
+            rd_k = keep.tile([P, 4, P], F32, name="rd%d" % k)
+            nc.scalar.activation(rd_k[:], d_k[:], ACT.Relu, scale=-1.0)
+            c_sb.append(c_k)
+            d_sb.append(d_k)
+            rd_sb.append(rd_k)
+
+        def second(k, h_bf, k0):
+            b_ps = product(k, [q[:].bitcast(FP8X4) for q in wb_q], [s[:] for s in wb_sc])
+            u_k = ring.tile([P, 4, P], F32, name="u_k")
+            nc.vector.tensor_tensor(u_k[:], b_ps, c_sb[k][:], ALU.subtract)
+            ru_k = ring.tile([P, 4, P], F32, name="ru_k")
+            nc.scalar.activation(ru_k[:], u_k[:], ACT.Relu, scale=-1.0)
+            m_k = ring.tile([P, 4, P], F32, name="m_k")
+            nc.vector.tensor_tensor(m_k[:], d_sb[k][:], u_k[:], ALU.max)
+            h_ps = psum.tile([P, 4, P], F32, name="h_ps")
+            for t in range(4):
+                for n, term in enumerate((rd_sb[k], m_k, ru_k)):
+                    nc.tensor.matmul(
+                        h_ps[:, t, :], term[:, t, :], ident[:], start=(n == 0), stop=(n == 2), is_transpose=True
+                    )
+            nc.scalar.copy(h_bf[:, P * (k - k0) : P * (k - k0 + 1), :], h_ps[:].rearrange("p t j -> p j t"))
+
+        wd_bf = keep.tile([P, N, 4], BF16, name="wd_bf", align_bytes=64)
+        wd_q = keep.tile([P, N], U32, name="wd_q", align_bytes=64)
+        wd_sc = keep.tile([P, N], U8, name="wd_sc", align_bytes=64)
+
+        def prepare_wd():
+            for i in range(4):
+                nc.scalar.copy(
+                    wd_bf[:, P * i : P * (i + 1), :], wd_raw[:].rearrange("p j (m i) -> p i m j", i=4)[:, i]
+                )
+            nc.vector.quantize_mx(
+                out=wd_q[:].bitcast(FP8X4), scales=wd_sc[:], in_=wd_bf[:].rearrange("p c j -> p (c j)")
+            )
+
+        def quantise(c, h_bf):
+            k0, k1 = CHUNKS[c]
+            w = P * (k1 - k0)
+            h_q = keep.tile([P, w], U32, name="h_q%d" % c, align_bytes=64)
+            h_sc = keep.tile([P, w], U8, name="h_sc%d" % c, align_bytes=64)
+            nc.vector.quantize_mx(out=h_q[:].bitcast(FP8X4), scales=h_sc[:], in_=h_bf[:].rearrange("p c j -> p (c j)"))
+            return h_q, h_sc
+
+        def marks(c, h_q, h_sc):
+            k0, k1 = CHUNKS[c]
+            w = P * (k1 - k0)
+            y_lo = keep.tile([P, 2, w], F32, name="y_lo", tag="late" if c == 1 else "ylo%d" % c)
+            y_hi = keep.tile([P, 2, w], F32, name="y_hi", tag="later" if c == 1 else "yhi%d" % c, align_bytes=64)
+            y_sb = [y_lo[:, 0, :], y_lo[:, 1, :], y_hi[:, 0, :], y_hi[:, 1, :]]
+            per_bank = 512 // w
+            for i0 in range(0, 4, per_bank):
+                y_ps = psum.tile([P, per_bank, w], F32, name="y_ps")
+                for i in range(i0, i0 + per_bank):
+                    nc.tensor.matmul_mx(
+                        out=y_ps[:, i - i0, :],
+                        lhsT=wd_q[:, P * i : P * (i + 1)].bitcast(FP8X4),
+                        lhsT_scale=wd_sc[:, P * i : P * (i + 1)],
+                        rhs=h_q[:].bitcast(FP8X4),
+                        rhs_scale=h_sc[:],
+                        start=True,
+                        stop=True,
+                    )
+                for i in range(i0, i0 + per_bank):
+                    nc.scalar.activation(y_sb[i], y_ps[:, i - i0, :], ACT.Identity, bias=neg_usual[:, i : i + 1])
+            for i in range(4):
+                nc.vector.tensor_tensor(
+                    pages[i][:].indirect(offs2_sb[:, 8 * k0 : 8 * k1]), y_sb[i], wgo_sb[:, P * k0 : P * k1], ALU.mult
+                )
+
+        for k in range(TILES):
+            first(k)
+            if k == 1:
+                prepare_wb(0, wb_raw0)
+            if k == 3:
+                prepare_wb(1, wb_raw1)
+        quantised = []
+        for c, (k0, k1) in enumerate(CHUNKS):
+            h_bf = keep.tile(
+                [P, P * (k1 - k0), 4], BF16, name="h_bf", tag="later" if c == 2 else "h_bf%d" % c, align_bytes=64
+            )
+            for k in range(k0, k1):
+                second(k, h_bf, k0)
+            if c == 0:
+                prepare_wd()
+            quantised.append(quantise(c, h_bf))
+            if c == 0:
+                marks(0, *quantised[0])
+        marks(1, *quantised[1])
+        marks(2, *quantised[2])
+        rows = out.rearrange("(p i) t -> i p t", i=4)
+        for i in range(4):
+            nc.sync.dma_start(rows[i], pages[i][:])

@@ -47,17 +47,15 @@ def tile_list_skill_disagreement_marks_kernel(
         tab_w = [keep.tile([P, T], I32, name="tab_w%d" % a, tag="slot_w%d" % a, align_bytes=64) for a in range(2)]
         for a in range(2):
             nc.sync.dma_start(tab_w[a][:], tab_words[a].rearrange("p t i -> p (t i)").bitcast(I32))
-        wa_sb = keep.tile([P, 2, 2 * H], U8, name="wa_sb", align_bytes=64)
-        nc.sync.dma_start(wa_sb[:].bitcast(I32), wa_words.rearrange("a p n -> p a n").bitcast(I32))
         wc_sb = keep.tile([P, 2, H], I32, name="wc_sb", align_bytes=64)
         nc.sync.dma_start(wc_sb[:], wc_words.rearrange("a p e i -> p a (e i)").bitcast(I32))
+        wa_sb = keep.tile([P, 2, 2 * H], U8, name="wa_sb", align_bytes=64)
+        nc.sync.dma_start(wa_sb[:].bitcast(I32), wa_words.rearrange("a p n -> p a n").bitcast(I32))
         wb_rows = wb.rearrange("(a p j) c -> a p j c", a=2, j=4)
-        wb_raw0 = keep.tile([P, 4, H], F32, name="wb_raw0")
-        nc.sync.dma_start(wb_raw0[:], wb_rows[0])
 
         wa_sc = keep.tile([P, 2, H], U8, name="wa_sc", align_bytes=64)
         wc_sc = keep.tile([P, 2, H], U8, name="wc_sc", align_bytes=64)
-        for sc, src in ((wa_sc, wa_scales), (wc_sc, wc_scales)):
+        for sc, src in ((wc_sc, wc_scales), (wa_sc, wa_scales)):
             nc.gpsimd.memset(sc[:].bitcast(I32), 0)
             for d in range(4):
                 nc.gpsimd.dma_start(
@@ -71,8 +69,6 @@ def tile_list_skill_disagreement_marks_kernel(
         pages = [keep.tile([P, T2], F32, name="page%d" % i) for i in range(4)]
         neg_usual = keep.tile([P, 4], F32, name="neg_usual")
         nc.gpsimd.tensor_scalar(neg_usual[:], usual_sb[:], -1.0, 0.0, ALU.mult, ALU.add)
-        for page in pages[:2]:
-            nc.vector.memset(page[:], 0.0)
         for page in pages[2:]:
             for half in range(2):
                 nc.gpsimd.memset(page[:, 1024 * half : 1024 * (half + 1)], 0.0)
@@ -91,19 +87,22 @@ def tile_list_skill_disagreement_marks_kernel(
                 tab_w[1][:].bitcast(U32).indirect(offs_sb[:, 32 * half : 32 * (half + 1)]),
             )
 
-        wb_raw1 = keep.tile([P, 4, H], F32, name="wb_raw1", tag="slot_sc", align_bytes=64)
-        nc.sync.dma_start(wb_raw1[:], wb_rows[1])
-        wd_raw = keep.tile([P, 4, N], F32, name="wd_raw", tag="slot_w0", align_bytes=64)
+        for page in pages[:2]:
+            for half in range(2):
+                nc.vector.memset(page[:, 1024 * half : 1024 * (half + 1)], 0.0)
+        wd_raw = keep.tile([P, 4, N], F32, name="wd_raw", tag="slot_sc", align_bytes=64)
         nc.sync.dma_start(wd_raw[:], wd.rearrange("(p j) c -> p j c", j=4))
-        wgo_sb = keep.tile([P, S], F32, name="wgo_sb", tag="slot_w1", align_bytes=64)
-        nc.sync.dma_start(wgo_sb[:], wgo)
+        wb_raw0 = keep.tile([P, 4, H], F32, name="wb_raw0", tag="slot_w0", align_bytes=64)
+        nc.sync.dma_start(wb_raw0[:], wb_rows[0])
+        wb_raw1 = keep.tile([P, 4, H], F32, name="wb_raw1", tag="slot_w1", align_bytes=64)
+        nc.sync.dma_start(wb_raw1[:], wb_rows[1])
 
         wb_bf = [keep.tile([P, H, 4], BF16, name="wb_bf%d" % a, align_bytes=64) for a in range(2)]
         wb_q = [keep.tile([P, H], U32, name="wb_q%d" % a, align_bytes=64) for a in range(2)]
         wb_sc = [keep.tile([P, H], U8, name="wb_sc%d" % a, align_bytes=64) for a in range(2)]
 
         def prepare_wb(a, raw):
-            nc.scalar.copy(
+            nc.vector.tensor_copy(
                 wb_bf[a][:].rearrange("p (c i) j -> p c j i", i=4), raw[:].rearrange("p j (c i) -> p c j i", i=4)
             )
             nc.vector.quantize_mx(
@@ -163,8 +162,9 @@ def tile_list_skill_disagreement_marks_kernel(
 
         def prepare_wd():
             for i in range(4):
-                nc.scalar.copy(
-                    wd_bf[:, P * i : P * (i + 1), :], wd_raw[:].rearrange("p j (m i) -> p i m j", i=4)[:, i]
+                nc.gpsimd.tensor_scalar(
+                    wd_bf[:, P * i : P * (i + 1), :], wd_raw[:].rearrange("p j (m i) -> p i m j", i=4)[:, i],
+                    1.0, 0.0, ALU.mult, ALU.add,
                 )
             nc.vector.quantize_mx(
                 out=wd_q[:].bitcast(FP8X4), scales=wd_sc[:], in_=wd_bf[:].rearrange("p c j -> p (c j)")
@@ -204,12 +204,15 @@ def tile_list_skill_disagreement_marks_kernel(
                     pages[i][:].indirect(offs2_sb[:, 8 * k0 : 8 * k1]), y_sb[i], wgo_sb[:, P * k0 : P * k1], ALU.mult
                 )
 
-        for k in range(TILES):
+        for k in range(4):
             first(k)
             if k == 1:
                 prepare_wb(0, wb_raw0)
             if k == 3:
                 prepare_wb(1, wb_raw1)
+        prepare_wd()
+        wgo_sb = keep.tile([P, S], F32, name="wgo_sb", tag="slot_w0", align_bytes=64)
+        nc.sync.dma_start(wgo_sb[:], wgo)
         quantised = []
         for c, (k0, k1) in enumerate(CHUNKS):
             h_bf = keep.tile(
@@ -217,8 +220,8 @@ def tile_list_skill_disagreement_marks_kernel(
             )
             for k in range(k0, k1):
                 second(k, h_bf, k0)
-            if c == 0:
-                prepare_wd()
+                if k < 4:
+                    first(k + 4)
             quantised.append(quantise(c, h_bf))
             if c == 0:
                 marks(0, *quantised[0])

@@ -19,7 +19,8 @@ ACT = mybir.ActivationFunctionType
 
 P = 128
 TILES = S // P
-CHUNKS = ((0, 2), (2, 4), (4, 8))
+HALF = S // 2
+CHUNKS = ((0, 1), (1, 2), (2, 3), (3, 4), (4, 5), (5, 6), (6, 8))
 
 
 def tile_list_skill_disagreement_marks_kernel(
@@ -29,88 +30,79 @@ def tile_list_skill_disagreement_marks_kernel(
     with ExitStack() as ctx:
         lists = ctx.enter_context(tc.tile_pool(name="lists", bufs=1))
         keep = ctx.enter_context(tc.tile_pool(name="keep", bufs=1))
+        arena = ctx.enter_context(tc.tile_pool(name="arena", bufs=1))
         ring = ctx.enter_context(tc.tile_pool(name="ring", bufs=3))
         psum = ctx.enter_context(tc.psum_pool(name="psum", bufs=2))
+
+        def placed(shape, dtype, name, offset):
+            return arena.tile(shape, dtype, name=name, offset=offset, align_bytes=64)
 
         offs_sb = lists.tile([P, S // 16], U16, name="offs_sb")
         offs2_sb = lists.tile([P, S // 16], U16, name="offs2_sb")
         nc.sync.dma_start(offs_sb[:], offs)
         nc.sync.dma_start(offs2_sb[:], offs2)
+        warm = keep.tile([P, 2], F32, name="warm")
+        nc.vector.memset(warm[:, 0:1], 0.0)
+        nc.scalar.activation(warm[:, 1:2], warm[:, 0:1], ACT.Relu)
 
-        tab_sc = keep.tile([P, T], U8, name="tab_sc", tag="slot_sc", align_bytes=64)
-        nc.vector.memset(tab_sc[:].bitcast(I32), 0)
-        for a in range(2):
-            nc.scalar.dma_start(tab_sc[a:P:8, :].bitcast(I32), tab_scales[a].bitcast(I32))
-        planes = [keep.tile([P, S], U8, name="plane%d" % a, align_bytes=64) for a in range(2)]
-        nc.vector.memset(planes[1][:].bitcast(I32), 0)
-
-        tab_w = [keep.tile([P, T], I32, name="tab_w%d" % a, tag="slot_w%d" % a, align_bytes=64) for a in range(2)]
+        tab_sc = placed([P, T], U8, "tab_sc", 4096)
+        nc.gpsimd.memset(tab_sc[:].bitcast(I32), 0)
+        sc_rows = tab_scales.bitcast(I32)
+        for r in range(2):
+            nc.sync.dma_start(tab_sc[r:P:16, :].bitcast(I32), sc_rows[0].rearrange("(g r) t -> r g t", r=2)[r])
+        nc.sync.dma_start(tab_sc[4:P:8, :].bitcast(I32), sc_rows[1])
+        tab_w = [placed([P, T], I32, "tab_w%d" % a, (12288, 23552)[a]) for a in range(2)]
         for a in range(2):
             nc.sync.dma_start(tab_w[a][:], tab_words[a].rearrange("p t i -> p (t i)").bitcast(I32))
         wc_sb = keep.tile([P, 2, H], I32, name="wc_sb", align_bytes=64)
         nc.sync.dma_start(wc_sb[:], wc_words.rearrange("a p e i -> p a (e i)").bitcast(I32))
-        wa_sb = keep.tile([P, 2, 2 * H], U8, name="wa_sb", align_bytes=64)
-        nc.sync.dma_start(wa_sb[:].bitcast(I32), wa_words.rearrange("a p n -> p a n").bitcast(I32))
-        wb_rows = wb.rearrange("(a p j) c -> a p j c", a=2, j=4)
+        planes = [keep.tile([P, S], U8, name="plane%d" % a, align_bytes=64) for a in range(2)]
+        nc.vector.memset(planes[1][:].bitcast(I32), 0)
 
-        wa_sc = keep.tile([P, 2, H], U8, name="wa_sc", align_bytes=64)
-        wc_sc = keep.tile([P, 2, H], U8, name="wc_sc", align_bytes=64)
-        for sc, src in ((wc_sc, wc_scales), (wa_sc, wa_scales)):
-            nc.gpsimd.memset(sc[:].bitcast(I32), 0)
+        def load_scales(engine, queue, sc, src):
+            engine.memset(sc[:].bitcast(I32), 0)
             for d in range(4):
-                nc.gpsimd.dma_start(
+                queue.dma_start(
                     sc[32 * d : 32 * d + 4].bitcast(I32),
                     src[:, 4 * d : 4 * d + 4, :].rearrange("a r e -> r a e").bitcast(I32),
                 )
-        usual_sb = keep.tile([P, 4], F32, name="usual_sb")
-        nc.gpsimd.dma_start(usual_sb[:], usual.rearrange("(p i) -> p i", i=4))
-        ident = keep.tile([P, P], F32, name="ident")
-        make_identity(nc, ident[:])
-        pages = [keep.tile([P, T2], F32, name="page%d" % i) for i in range(4)]
-        neg_usual = keep.tile([P, 4], F32, name="neg_usual")
-        nc.gpsimd.tensor_scalar(neg_usual[:], usual_sb[:], -1.0, 0.0, ALU.mult, ALU.add)
-        for page in pages[2:]:
-            for half in range(2):
-                nc.gpsimd.memset(page[:, 1024 * half : 1024 * (half + 1)], 0.0)
+
+        wc_sc = keep.tile([P, 2, H], U8, name="wc_sc", align_bytes=64)
+        load_scales(nc.gpsimd, nc.gpsimd, wc_sc, wc_scales)
+        wa_sc = keep.tile([P, 2, H], U8, name="wa_sc", align_bytes=64)
+        load_scales(nc.vector, nc.scalar, wa_sc, wa_scales)
 
         picked_sc = keep.tile([P, S], U8, name="picked_sc", align_bytes=64)
         nc.vector.tensor_copy(picked_sc[:], tab_sc[:].indirect(offs_sb[:]))
         nc.vector.tensor_copy(planes[0][:].bitcast(I32), picked_sc[:].bitcast(I32))
-        for a in range(2):
-            for r in range(1 - a, 4):
-                nc.scalar.dma_start(planes[a][r:P:32, :].bitcast(I32), picked_sc[8 * r + a : P : 32, :].bitcast(I32))
+        for r in range(2):
+            nc.scalar.dma_start(planes[0][2 + r : P : 32, :].bitcast(I32), picked_sc[16 + r : P : 32, :].bitcast(I32))
+        for r in range(4):
+            nc.scalar.dma_start(planes[1][r:P:32, :].bitcast(I32), picked_sc[8 * r + 4 : P : 32, :].bitcast(I32))
+        wb_rows = wb.rearrange("(a p j) c -> a p j c", a=2, j=4)
+        wb_raw = [placed([P, 4, H], F32, "wb_raw%d" % a, 4096 + 8192 * a) for a in range(2)]
+        nc.sync.dma_start(wb_raw[0][:], wb_rows[0])
+
         picked = [keep.tile([P, S], U32, name="picked%d" % a, align_bytes=64) for a in range(2)]
         nc.vector.tensor_copy(picked[0][:], tab_w[0][:].bitcast(U32).indirect(offs_sb[:]))
+        nc.sync.dma_start(wb_raw[1][:], wb_rows[1])
         for half in range(2):
             nc.vector.tensor_copy(
-                picked[1][:, 512 * half : 512 * (half + 1)],
+                picked[1][:, HALF * half : HALF * (half + 1)],
                 tab_w[1][:].bitcast(U32).indirect(offs_sb[:, 32 * half : 32 * (half + 1)]),
             )
-
-        for page in pages[:2]:
-            for half in range(2):
-                nc.vector.memset(page[:, 1024 * half : 1024 * (half + 1)], 0.0)
-        wd_raw = keep.tile([P, 4, N], F32, name="wd_raw", tag="slot_sc", align_bytes=64)
+        wa_sb = placed([P, 2, 2 * H], U8, "wa_sb", 23552)
+        nc.sync.dma_start(wa_sb[:].bitcast(I32), wa_words.rearrange("a p n -> p a n").bitcast(I32))
+        wgo_sb = placed([P, S], F32, "wgo_sb", 23552 + 2048)
+        nc.sync.dma_start(wgo_sb[:], wgo)
+        usual_sb = placed([P, 4], F32, "usual_sb", 23552 + 6144)
+        nc.sync.dma_start(usual_sb[:], usual.rearrange("(p i) -> p i", i=4))
+        neg_usual = keep.tile([P, 4], F32, name="neg_usual")
+        wd_raw = placed([P, 4, N], F32, "wd_raw", 23552 + 7168)
         nc.sync.dma_start(wd_raw[:], wd.rearrange("(p j) c -> p j c", j=4))
-        wb_raw0 = keep.tile([P, 4, H], F32, name="wb_raw0", tag="slot_w0", align_bytes=64)
-        nc.sync.dma_start(wb_raw0[:], wb_rows[0])
-        wb_raw1 = keep.tile([P, 4, H], F32, name="wb_raw1", tag="slot_w1", align_bytes=64)
-        nc.sync.dma_start(wb_raw1[:], wb_rows[1])
 
-        wb_bf = [keep.tile([P, H, 4], BF16, name="wb_bf%d" % a, align_bytes=64) for a in range(2)]
-        wb_q = [keep.tile([P, H], U32, name="wb_q%d" % a, align_bytes=64) for a in range(2)]
-        wb_sc = [keep.tile([P, H], U8, name="wb_sc%d" % a, align_bytes=64) for a in range(2)]
-
-        def prepare_wb(a, raw):
-            nc.vector.tensor_copy(
-                wb_bf[a][:].rearrange("p (c i) j -> p c j i", i=4), raw[:].rearrange("p j (c i) -> p c j i", i=4)
-            )
-            nc.vector.quantize_mx(
-                out=wb_q[a][:].bitcast(FP8X4), scales=wb_sc[a][:], in_=wb_bf[a][:].rearrange("p c j -> p (c j)")
-            )
-
-        def product(k, rhs, rhs_sc):
-            acc = psum.tile([P, H], F32, name="acc", tag="acc", bufs=4)
+        def product(k, tag, rhs, rhs_sc):
+            acc = psum.tile([P, H], F32, name="acc", tag=tag)
             for a in range(2):
                 nc.tensor.matmul_mx(
                     out=acc[:],
@@ -123,32 +115,81 @@ def tile_list_skill_disagreement_marks_kernel(
                 )
             return acc[:].rearrange("p (m t) -> p t m", t=4)
 
-        wa_ops = [wa_sb[:, a, :].bitcast(FP4X4) for a in range(2)]
-        wc_ops = [wc_sb[:, a, :].bitcast(FP8X4) for a in range(2)]
-        c_sb, d_sb, rd_sb = [], [], []
+        c_sb = []
+        for k in range(TILES):
+            c_ps = product(k, "hy"[k % 2], [wc_sb[:, a, :].bitcast(FP8X4) for a in range(2)], [wc_sc[:, a, :] for a in range(2)])
+            c_k = keep.tile([P, 4, P], F32, name="c_k", tag="c%d" % k)
+            nc.scalar.copy(c_k[:], c_ps)
+            c_sb.append(c_k)
+
+        wb_bf = [placed([P, H, 4], BF16, "wb_bf%d" % a, (0, 49152)[a]) for a in range(2)]
+        wb_q = [keep.tile([P, H], U32, name="wb_q%d" % a, align_bytes=64) for a in range(2)]
+        wb_sc = [keep.tile([P, H], U8, name="wb_sc%d" % a, align_bytes=64) for a in range(2)]
+        for a, raw in enumerate(wb_raw):
+            nc.vector.tensor_copy(
+                wb_bf[a][:], raw[:].rearrange("p j c -> p c j")
+            )
+            nc.vector.quantize_mx(
+                out=wb_q[a][:].bitcast(FP8X4), scales=wb_sc[a][:], in_=wb_bf[a][:].rearrange("p c j -> p (c j)")
+            )
+        ident = placed([P, P], F32, "ident", 49152 + 1024)
+        make_identity(nc, ident[:])
+        pages = [
+            placed([P, T2], F32, "page0", 49152 + 1024 - 8192),
+            placed([P, T2], F32, "page1", 49152 + 2048),
+            placed([P, T2], F32, "page2", 68608 + 2048),
+            placed([P, T2], F32, "page3", 68608 + 1024 - 8192),
+        ]
+
+        def clear(page):
+            for q in range(4):
+                nc.gpsimd.memset(page[:, 512 * q : 512 * (q + 1)], 0.0)
+
+        clear(pages[0])
+        clear(pages[1])
+
+        wd_bf = placed([P, 4, P, 4], BF16, "wd_bf", 68608)
+        wd_q = keep.tile([P, N], U32, name="wd_q", align_bytes=64)
+        wd_sc = keep.tile([P, N], U8, name="wd_sc", align_bytes=64)
+
+        def prepare_wd():
+            nc.vector.tensor_copy(
+                wd_bf[:].rearrange("p i m j -> p m j i"), wd_raw[:].rearrange("p j (m i) -> p m j i", i=4)
+            )
+            nc.scalar.activation(neg_usual[:], usual_sb[:], ACT.Identity, scale=-1.0)
+            nc.vector.quantize_mx(
+                out=wd_q[:].bitcast(FP8X4), scales=wd_sc[:], in_=wd_bf[:].rearrange("p i m j -> p (i m j)")
+            )
+
+        d_sb, rd_sb = [], []
 
         def first(k):
-            c_ps = product(k, wc_ops, [wc_sc[:, a, :] for a in range(2)])
-            a_ps = product(k, wa_ops, [wa_sc[:, a, :] for a in range(2)])
-            c_k = keep.tile([P, 4, P], F32, name="c_k", tag="late" if k == TILES - 1 else "c%d" % k)
-            nc.scalar.copy(c_k[:], c_ps)
-            d_k = keep.tile([P, 4, P], F32, name="d%d" % k)
-            nc.vector.tensor_tensor(d_k[:], a_ps, c_k[:], ALU.subtract)
-            rd_k = keep.tile([P, 4, P], F32, name="rd%d" % k)
+            a_ps = product(k, "a", [wa_sb[:, a, :].bitcast(FP4X4) for a in range(2)], [wa_sc[:, a, :] for a in range(2)])
+            d_k = keep.tile([P, 4, P], F32, name="d_k", tag="d%d" % k)
+            nc.vector.tensor_tensor(d_k[:], a_ps, c_sb[k][:], ALU.subtract)
+            rd_k = ring.tile([P, 4, P], F32, name="rd_k")
             nc.scalar.activation(rd_k[:], d_k[:], ACT.Relu, scale=-1.0)
-            c_sb.append(c_k)
             d_sb.append(d_k)
             rd_sb.append(rd_k)
 
         def second(k, h_bf, k0):
-            b_ps = product(k, [q[:].bitcast(FP8X4) for q in wb_q], [s[:] for s in wb_sc])
-            u_k = ring.tile([P, 4, P], F32, name="u_k")
+            b_ps = product(k, "b", [q[:].bitcast(FP8X4) for q in wb_q], [s[:] for s in wb_sc])
+            if k == 1:
+                u_k = placed([P, 4, P], F32, "u_1", 23552 + 9216)
+            else:
+                u_k = ring.tile([P, 4, P], F32, name="u_k")
             nc.vector.tensor_tensor(u_k[:], b_ps, c_sb[k][:], ALU.subtract)
             ru_k = ring.tile([P, 4, P], F32, name="ru_k")
             nc.scalar.activation(ru_k[:], u_k[:], ACT.Relu, scale=-1.0)
-            m_k = ring.tile([P, 4, P], F32, name="m_k")
+            if k + 1 < TILES:
+                first(k + 1)
+                m_k = ring.tile([P, 4, P], F32, name="m_k")
+            else:
+                m_k = keep.tile([P, 4, P], F32, name="m_last", tag="late")
             nc.vector.tensor_tensor(m_k[:], d_sb[k][:], u_k[:], ALU.max)
-            h_ps = psum.tile([P, 4, P], F32, name="h_ps")
+            if k >= 2:
+                early_pages(P * (k - 2), P * (k - 1), "d%d" % k)
+            h_ps = psum.tile([P, 4, P], F32, name="h_ps", tag="h")
             for t in range(4):
                 for n, term in enumerate((rd_sb[k], m_k, ru_k)):
                     nc.tensor.matmul(
@@ -156,77 +197,63 @@ def tile_list_skill_disagreement_marks_kernel(
                     )
             nc.scalar.copy(h_bf[:, P * (k - k0) : P * (k - k0 + 1), :], h_ps[:].rearrange("p t j -> p j t"))
 
-        wd_bf = keep.tile([P, N, 4], BF16, name="wd_bf", align_bytes=64)
-        wd_q = keep.tile([P, N], U32, name="wd_q", align_bytes=64)
-        wd_sc = keep.tile([P, N], U8, name="wd_sc", align_bytes=64)
+        h_q = keep.tile([P, S], U32, name="h_q", align_bytes=64)
+        h_sc = keep.tile([P, S], U8, name="h_sc", align_bytes=64)
 
-        def prepare_wd():
-            for i in range(4):
-                nc.gpsimd.tensor_scalar(
-                    wd_bf[:, P * i : P * (i + 1), :], wd_raw[:].rearrange("p j (m i) -> p i m j", i=4)[:, i],
-                    1.0, 0.0, ALU.mult, ALU.add,
-                )
-            nc.vector.quantize_mx(
-                out=wd_q[:].bitcast(FP8X4), scales=wd_sc[:], in_=wd_bf[:].rearrange("p c j -> p (c j)")
+        def mark(i, j0, j1, y_ps, y_sb):
+            nc.tensor.matmul_mx(
+                out=y_ps,
+                lhsT=wd_q[:, P * i : P * (i + 1)].bitcast(FP8X4),
+                lhsT_scale=wd_sc[:, P * i : P * (i + 1)],
+                rhs=h_q[:, j0:j1].bitcast(FP8X4),
+                rhs_scale=h_sc[:, j0:j1],
+                start=True,
+                stop=True,
             )
 
-        def quantise(c, h_bf):
-            k0, k1 = CHUNKS[c]
-            w = P * (k1 - k0)
-            h_q = keep.tile([P, w], U32, name="h_q%d" % c, align_bytes=64)
-            h_sc = keep.tile([P, w], U8, name="h_sc%d" % c, align_bytes=64)
-            nc.vector.quantize_mx(out=h_q[:].bitcast(FP8X4), scales=h_sc[:], in_=h_bf[:].rearrange("p c j -> p (c j)"))
-            return h_q, h_sc
+        def shift(i, y_ps, y_sb):
+            nc.scalar.activation(y_sb, y_ps, ACT.Identity, bias=neg_usual[:, i : i + 1])
 
-        def marks(c, h_q, h_sc):
-            k0, k1 = CHUNKS[c]
-            w = P * (k1 - k0)
-            y_lo = keep.tile([P, 2, w], F32, name="y_lo", tag="late" if c == 1 else "ylo%d" % c)
-            y_hi = keep.tile([P, 2, w], F32, name="y_hi", tag="later" if c == 1 else "yhi%d" % c, align_bytes=64)
-            y_sb = [y_lo[:, 0, :], y_lo[:, 1, :], y_hi[:, 0, :], y_hi[:, 1, :]]
-            per_bank = 512 // w
-            for i0 in range(0, 4, per_bank):
-                y_ps = psum.tile([P, per_bank, w], F32, name="y_ps")
-                for i in range(i0, i0 + per_bank):
-                    nc.tensor.matmul_mx(
-                        out=y_ps[:, i - i0, :],
-                        lhsT=wd_q[:, P * i : P * (i + 1)].bitcast(FP8X4),
-                        lhsT_scale=wd_sc[:, P * i : P * (i + 1)],
-                        rhs=h_q[:].bitcast(FP8X4),
-                        rhs_scale=h_sc[:],
-                        start=True,
-                        stop=True,
-                    )
-                for i in range(i0, i0 + per_bank):
-                    nc.scalar.activation(y_sb[i], y_ps[:, i - i0, :], ACT.Identity, bias=neg_usual[:, i : i + 1])
-            for i in range(4):
-                nc.vector.tensor_tensor(
-                    pages[i][:].indirect(offs2_sb[:, 8 * k0 : 8 * k1]), y_sb[i], wgo_sb[:, P * k0 : P * k1], ALU.mult
-                )
+        def put(i, j0, j1, y_sb):
+            nc.vector.tensor_tensor(pages[i][:].indirect(offs2_sb[:, j0 // 16 : j1 // 16]), y_sb, wgo_sb[:, j0:j1], ALU.mult)
 
-        for k in range(4):
-            first(k)
-            if k == 1:
-                prepare_wb(0, wb_raw0)
-            if k == 3:
-                prepare_wb(1, wb_raw1)
-        prepare_wd()
-        wgo_sb = keep.tile([P, S], F32, name="wgo_sb", tag="slot_w0", align_bytes=64)
-        nc.sync.dma_start(wgo_sb[:], wgo)
-        quantised = []
+        def half_page(i, half, bank, slot):
+            y_ps = psum.tile([P, HALF], F32, name="y_half_ps", tag=bank)
+            y_sb = keep.tile([P, HALF], F32, name="y_half", tag=slot)
+            mark(i, HALF * half, HALF * (half + 1), y_ps[:], y_sb[:])
+            shift(i, y_ps[:], y_sb[:])
+            put(i, HALF * half, HALF * (half + 1), y_sb[:])
+
+        def early_pages(j0, j1, slot):
+            y_ps = psum.tile([P, 2, j1 - j0], F32, name="y_ps", tag="y")
+            y_sb = keep.tile([P, 2, j1 - j0], F32, name="y_early", tag=slot)
+            for i in range(2):
+                mark(i, j0, j1, y_ps[:, i, :], y_sb[:, i, :])
+            for i in range(2):
+                shift(i, y_ps[:, i, :], y_sb[:, i, :])
+            for i in range(2):
+                put(i, j0, j1, y_sb[:, i, :])
+
+        first(0)
         for c, (k0, k1) in enumerate(CHUNKS):
-            h_bf = keep.tile(
-                [P, P * (k1 - k0), 4], BF16, name="h_bf", tag="later" if c == 2 else "h_bf%d" % c, align_bytes=64
-            )
+            j0, j1 = P * k0, P * k1
+            h_bf = keep.tile([P, j1 - j0, 4], BF16, name="h_bf%d" % c, align_bytes=64)
             for k in range(k0, k1):
                 second(k, h_bf, k0)
-                if k < 4:
-                    first(k + 4)
-            quantised.append(quantise(c, h_bf))
+            if k1 == TILES:
+                half_page(3, 0, "a", "c7")
             if c == 0:
-                marks(0, *quantised[0])
-        marks(1, *quantised[1])
-        marks(2, *quantised[2])
+                prepare_wd()
+                clear(pages[3])
+                clear(pages[2])
+            nc.vector.quantize_mx(
+                out=h_q[:, j0:j1].bitcast(FP8X4), scales=h_sc[:, j0:j1], in_=h_bf[:].rearrange("p c j -> p (c j)")
+            )
+            if k1 == TILES:
+                half_page(2, 0, "a", "late")
+        early_pages(P * (TILES - 2), S, "y01")
+        half_page(2, 1, "b", "y2b")
+        half_page(3, 1, "b", "y3b")
         rows = out.rearrange("(p i) t -> i p t", i=4)
         for i in range(4):
             nc.sync.dma_start(rows[i], pages[i][:])

@@ -56,21 +56,34 @@ def tile_list_skill_disagreement_marks_kernel(
             nc.sync.dma_start(tab_w[a][:], tab_words[a].rearrange("p t i -> p (t i)").bitcast(I32))
         wc_sb = keep.tile([P, 2, H], I32, name="wc_sb", align_bytes=64)
         nc.sync.dma_start(wc_sb[:], wc_words.rearrange("a p e i -> p a (e i)").bitcast(I32))
+        ident = keep.tile([P, P], F32, name="ident")
+        make_identity(nc, ident[:])
+        pages = [
+            keep.tile([P, T2], F32, name="page0"),
+            keep.tile([P, T2], F32, name="page1"),
+            placed([P, T2], F32, "page2", 68608 + 2048),
+            placed([P, T2], F32, "page3", 49152 + 2048),
+        ]
+
+        def clear(page):
+            for half in range(2):
+                nc.vector.memset(page[:, 1024 * half : 1024 * (half + 1)].bitcast(I32), 0)
+
+        clear(pages[0])
+        clear(pages[1])
         planes = [keep.tile([P, S], U8, name="plane%d" % a, align_bytes=64) for a in range(2)]
         nc.vector.memset(planes[1][:].bitcast(I32), 0)
 
-        def load_scales(engine, queue, sc, src):
-            engine.memset(sc[:].bitcast(I32), 0)
+        def load_scales(sc, src):
+            nc.vector.memset(sc[:].bitcast(I32), 0)
             for d in range(4):
-                queue.dma_start(
+                nc.scalar.dma_start(
                     sc[32 * d : 32 * d + 4].bitcast(I32),
                     src[:, 4 * d : 4 * d + 4, :].rearrange("a r e -> r a e").bitcast(I32),
                 )
 
         wc_sc = keep.tile([P, 2, H], U8, name="wc_sc", align_bytes=64)
-        load_scales(nc.gpsimd, nc.gpsimd, wc_sc, wc_scales)
-        wa_sc = keep.tile([P, 2, H], U8, name="wa_sc", align_bytes=64)
-        load_scales(nc.vector, nc.scalar, wa_sc, wa_scales)
+        load_scales(wc_sc, wc_scales)
 
         picked_sc = keep.tile([P, S], U8, name="picked_sc", align_bytes=64)
         nc.vector.tensor_copy(picked_sc[:], tab_sc[:].indirect(offs_sb[:]))
@@ -80,19 +93,21 @@ def tile_list_skill_disagreement_marks_kernel(
         for r in range(4):
             nc.scalar.dma_start(planes[1][r:P:32, :].bitcast(I32), picked_sc[8 * r + 4 : P : 32, :].bitcast(I32))
         wb_rows = wb.rearrange("(a p j) c -> a p j c", a=2, j=4)
-        wb_raw = [placed([P, 4, H], F32, "wb_raw%d" % a, 4096 + 8192 * a) for a in range(2)]
+        wb_raw = [placed([P, 4, H], F32, "wb_raw%d" % a, (4096, 15360)[a]) for a in range(2)]
         nc.sync.dma_start(wb_raw[0][:], wb_rows[0])
 
         picked = [keep.tile([P, S], U32, name="picked%d" % a, align_bytes=64) for a in range(2)]
         nc.vector.tensor_copy(picked[0][:], tab_w[0][:].bitcast(U32).indirect(offs_sb[:]))
         nc.sync.dma_start(wb_raw[1][:], wb_rows[1])
+        wa_sb = placed([P, 2, 2 * H], U8, "wa_sb", 12288 + 1024)
+        nc.sync.dma_start(wa_sb[:].bitcast(I32), wa_words.rearrange("a p n -> p a n").bitcast(I32))
+        wa_sc = placed([P, 2, H], U8, "wa_sc", 12288)
+        load_scales(wa_sc, wa_scales)
         for half in range(2):
             nc.vector.tensor_copy(
                 picked[1][:, HALF * half : HALF * (half + 1)],
                 tab_w[1][:].bitcast(U32).indirect(offs_sb[:, 32 * half : 32 * (half + 1)]),
             )
-        wa_sb = placed([P, 2, 2 * H], U8, "wa_sb", 23552)
-        nc.sync.dma_start(wa_sb[:].bitcast(I32), wa_words.rearrange("a p n -> p a n").bitcast(I32))
         wgo_sb = placed([P, S], F32, "wgo_sb", 23552 + 2048)
         nc.sync.dma_start(wgo_sb[:], wgo)
         usual_sb = placed([P, 4], F32, "usual_sb", 23552 + 6144)
@@ -132,21 +147,6 @@ def tile_list_skill_disagreement_marks_kernel(
             nc.vector.quantize_mx(
                 out=wb_q[a][:].bitcast(FP8X4), scales=wb_sc[a][:], in_=wb_bf[a][:].rearrange("p c j -> p (c j)")
             )
-        ident = placed([P, P], F32, "ident", 49152 + 1024)
-        make_identity(nc, ident[:])
-        pages = [
-            placed([P, T2], F32, "page0", 49152 + 1024 - 8192),
-            placed([P, T2], F32, "page1", 49152 + 2048),
-            placed([P, T2], F32, "page2", 68608 + 2048),
-            placed([P, T2], F32, "page3", 68608 + 1024 - 8192),
-        ]
-
-        def clear(page):
-            for q in range(4):
-                nc.gpsimd.memset(page[:, 512 * q : 512 * (q + 1)], 0.0)
-
-        clear(pages[0])
-        clear(pages[1])
 
         wd_bf = placed([P, 4, P, 4], BF16, "wd_bf", 68608)
         wd_q = keep.tile([P, N], U32, name="wd_q", align_bytes=64)
@@ -154,7 +154,7 @@ def tile_list_skill_disagreement_marks_kernel(
 
         def prepare_wd():
             nc.vector.tensor_copy(
-                wd_bf[:].rearrange("p i m j -> p m j i"), wd_raw[:].rearrange("p j (m i) -> p m j i", i=4)
+                wd_bf[:].rearrange("p i m j -> p m i j"), wd_raw[:].rearrange("p j (m i) -> p m i j", i=4)
             )
             nc.scalar.activation(neg_usual[:], usual_sb[:], ACT.Identity, scale=-1.0)
             nc.vector.quantize_mx(
@@ -179,13 +179,14 @@ def tile_list_skill_disagreement_marks_kernel(
             else:
                 u_k = ring.tile([P, 4, P], F32, name="u_k")
             nc.vector.tensor_tensor(u_k[:], b_ps, c_sb[k][:], ALU.subtract)
-            ru_k = ring.tile([P, 4, P], F32, name="ru_k")
+            if k + 1 < TILES:
+                ru_k = ring.tile([P, 4, P], F32, name="ru_k")
+            else:
+                ru_k = keep.tile([P, 4, P], F32, name="ru_last", tag="late")
             nc.scalar.activation(ru_k[:], u_k[:], ACT.Relu, scale=-1.0)
             if k + 1 < TILES:
                 first(k + 1)
-                m_k = ring.tile([P, 4, P], F32, name="m_k")
-            else:
-                m_k = keep.tile([P, 4, P], F32, name="m_last", tag="late")
+            m_k = ring.tile([P, 4, P], F32, name="m_k")
             nc.vector.tensor_tensor(m_k[:], d_sb[k][:], u_k[:], ALU.max)
             if k >= 2:
                 early_pages(P * (k - 2), P * (k - 1), "d%d" % k)
@@ -241,11 +242,11 @@ def tile_list_skill_disagreement_marks_kernel(
             for k in range(k0, k1):
                 second(k, h_bf, k0)
             if k1 == TILES:
+                clear(pages[3])
+                clear(pages[2])
                 half_page(3, 0, "a", "c7")
             if c == 0:
                 prepare_wd()
-                clear(pages[3])
-                clear(pages[2])
             nc.vector.quantize_mx(
                 out=h_q[:, j0:j1].bitcast(FP8X4), scales=h_sc[:, j0:j1], in_=h_bf[:].rearrange("p c j -> p (c j)")
             )

@@ -20,7 +20,7 @@ ACT = mybir.ActivationFunctionType
 P = 128
 TILES = S // P
 HALF = S // 2
-CHUNKS = ((0, 1), (1, 2), (2, 3), (3, 4), (4, 5), (5, 6), (6, 8))
+PLAIN = 6
 
 
 def tile_list_skill_disagreement_marks_kernel(
@@ -116,24 +116,27 @@ def tile_list_skill_disagreement_marks_kernel(
         wd_raw = placed([P, 4, N], F32, "wd_raw", 23552 + 7168)
         nc.sync.dma_start(wd_raw[:], wd.rearrange("(p j) c -> p j c", j=4))
 
-        def product(k, tag, rhs, rhs_sc):
+        def product(k, tag, *weights):
             acc = psum.tile([P, H], F32, name="acc", tag=tag)
-            for a in range(2):
+            passes = [(a, codes[a], scales[a]) for codes, scales in weights for a in range(2)]
+            for n, (a, rhs, rhs_sc) in enumerate(passes):
                 nc.tensor.matmul_mx(
                     out=acc[:],
                     lhsT=picked[a][:, P * k : P * (k + 1)].bitcast(FP8X4),
                     lhsT_scale=planes[a][:, P * k : P * (k + 1)],
-                    rhs=rhs[a],
-                    rhs_scale=rhs_sc[a],
-                    start=(a == 0),
-                    stop=(a == 1),
+                    rhs=rhs,
+                    rhs_scale=rhs_sc,
+                    start=(n == 0),
+                    stop=(n == len(passes) - 1),
                 )
             return acc[:].rearrange("p (m t) -> p t m", t=4)
 
+        wa_mx = ([wa_sb[:, a, :].bitcast(FP4X4) for a in range(2)], [wa_sc[:, a, :] for a in range(2)])
+        wc_mx = ([wc_sb[:, a, :].bitcast(FP8X4) for a in range(2)], [wc_sc[:, a, :] for a in range(2)])
         c_sb = []
-        for k in range(TILES):
-            c_ps = product(k, "hy"[k % 2], [wc_sb[:, a, :].bitcast(FP8X4) for a in range(2)], [wc_sc[:, a, :] for a in range(2)])
-            c_k = keep.tile([P, 4, P], F32, name="c_k", tag="c%d" % k)
+        for k in range(PLAIN):
+            c_ps = product(k, "hy"[k % 2], wc_mx)
+            c_k = keep.tile([P, 4, P], F32, name="c%d" % k)
             nc.scalar.copy(c_k[:], c_ps)
             c_sb.append(c_k)
 
@@ -141,9 +144,7 @@ def tile_list_skill_disagreement_marks_kernel(
         wb_q = [keep.tile([P, H], U32, name="wb_q%d" % a, align_bytes=64) for a in range(2)]
         wb_sc = [keep.tile([P, H], U8, name="wb_sc%d" % a, align_bytes=64) for a in range(2)]
         for a, raw in enumerate(wb_raw):
-            nc.vector.tensor_copy(
-                wb_bf[a][:], raw[:].rearrange("p j c -> p c j")
-            )
+            nc.vector.tensor_scalar(wb_bf[a][:], raw[:].rearrange("p j c -> p c j"), -1.0, 0.0, ALU.mult, ALU.add)
             nc.vector.quantize_mx(
                 out=wb_q[a][:].bitcast(FP8X4), scales=wb_sc[a][:], in_=wb_bf[a][:].rearrange("p c j -> p (c j)")
             )
@@ -161,100 +162,108 @@ def tile_list_skill_disagreement_marks_kernel(
                 out=wd_q[:].bitcast(FP8X4), scales=wd_sc[:], in_=wd_bf[:].rearrange("p i m j -> p (i m j)")
             )
 
-        d_sb, rd_sb = [], []
+        nb_mx = ([q[:].bitcast(FP8X4) for q in wb_q], [sc[:] for sc in wb_sc])
+        d_sb, rd_sb, terms = [], [], []
+
+        def relu_of_negative(src, tag):
+            r_k = keep.tile([P, 4, P], F32, name="r_k", tag=tag)
+            nc.scalar.activation(r_k[:], src, ACT.Relu, scale=-1.0)
+            return r_k
 
         def first(k):
-            a_ps = product(k, "a", [wa_sb[:, a, :].bitcast(FP4X4) for a in range(2)], [wa_sc[:, a, :] for a in range(2)])
             d_k = keep.tile([P, 4, P], F32, name="d_k", tag="d%d" % k)
-            nc.vector.tensor_tensor(d_k[:], a_ps, c_sb[k][:], ALU.subtract)
-            rd_k = ring.tile([P, 4, P], F32, name="rd_k")
-            nc.scalar.activation(rd_k[:], d_k[:], ACT.Relu, scale=-1.0)
+            if k < PLAIN:
+                nc.vector.tensor_tensor(d_k[:], c_sb[k][:], product(k, "a", wa_mx), ALU.subtract)
+                rd_sb.append(relu_of_negative(d_k[:], "rd%d" % (k % 3)))
+            else:
+                d_ps = product(k, "a", wc_mx, nb_mx)
+                nc.scalar.copy(d_k[:], d_ps)
+                rd_sb.append(relu_of_negative(d_ps, "rd%d" % (k % 3)))
             d_sb.append(d_k)
-            rd_sb.append(rd_k)
 
-        def second(k, h_bf, k0):
-            b_ps = product(k, "b", [q[:].bitcast(FP8X4) for q in wb_q], [s[:] for s in wb_sc])
-            if k == 1:
-                u_k = placed([P, 4, P], F32, "u_1", 23552 + 9216)
+        def second(k):
+            if k < PLAIN:
+                if k == 1:
+                    u_k = placed([P, 4, P], F32, "u_1", 23552 + 9216)
+                else:
+                    u_k = ring.tile([P, 4, P], F32, name="u_k")
+                nc.vector.tensor_tensor(u_k[:], product(k, "b", nb_mx), c_sb[k][:], ALU.add)
+                u = u_k[:]
             else:
-                u_k = ring.tile([P, 4, P], F32, name="u_k")
-            nc.vector.tensor_tensor(u_k[:], b_ps, c_sb[k][:], ALU.subtract)
-            if k + 1 < TILES:
-                ru_k = ring.tile([P, 4, P], F32, name="ru_k")
-            else:
-                ru_k = keep.tile([P, 4, P], F32, name="ru_last", tag="late")
-            nc.scalar.activation(ru_k[:], u_k[:], ACT.Relu, scale=-1.0)
+                u = product(k, "b", wa_mx, nb_mx)
+            ru_k = relu_of_negative(u, "ru%d" % (k % 3 if k < 5 else k))
             if k + 1 < TILES:
                 first(k + 1)
             m_k = ring.tile([P, 4, P], F32, name="m_k")
-            nc.vector.tensor_tensor(m_k[:], d_sb[k][:], u_k[:], ALU.max)
-            if k >= 2:
-                early_pages(P * (k - 2), P * (k - 1), "d%d" % k)
+            nc.vector.tensor_tensor(m_k[:], u, d_sb[k][:], ALU.max)
+            if k == 5:
+                clear(pages[3])
+                clear(pages[2])
+            if 2 <= k <= 5:
+                early(k - 2, "d%d" % k)
+            terms.append((rd_sb[k], m_k, ru_k))
+
+        def turn(k):
             h_ps = psum.tile([P, 4, P], F32, name="h_ps", tag="h")
             for t in range(4):
-                for n, term in enumerate((rd_sb[k], m_k, ru_k)):
+                for n, term in enumerate(terms[k]):
                     nc.tensor.matmul(
                         h_ps[:, t, :], term[:, t, :], ident[:], start=(n == 0), stop=(n == 2), is_transpose=True
                     )
-            nc.scalar.copy(h_bf[:, P * (k - k0) : P * (k - k0 + 1), :], h_ps[:].rearrange("p t j -> p j t"))
+            return h_ps
 
         h_q = keep.tile([P, S], U32, name="h_q", align_bytes=64)
         h_sc = keep.tile([P, S], U8, name="h_sc", align_bytes=64)
 
-        def mark(i, j0, j1, y_ps, y_sb):
-            nc.tensor.matmul_mx(
-                out=y_ps,
-                lhsT=wd_q[:, P * i : P * (i + 1)].bitcast(FP8X4),
-                lhsT_scale=wd_sc[:, P * i : P * (i + 1)],
-                rhs=h_q[:, j0:j1].bitcast(FP8X4),
-                rhs_scale=h_sc[:, j0:j1],
-                start=True,
-                stop=True,
-            )
+        def place(pieces, bank, slot):
+            width = sum(j1 - j0 for i, j0, j1 in pieces)
+            y_ps = psum.tile([P, width], F32, name="y_ps", tag=bank)
+            y_sb = keep.tile([P, width], F32, name="y_sb", tag=slot)
+            starts = [sum(j1 - j0 for i, j0, j1 in pieces[:n]) for n in range(len(pieces))]
+            cols = [slice(at, at + j1 - j0) for at, (i, j0, j1) in zip(starts, pieces)]
+            for col, (i, j0, j1) in zip(cols, pieces):
+                nc.tensor.matmul_mx(
+                    out=y_ps[:, col],
+                    lhsT=wd_q[:, P * i : P * (i + 1)].bitcast(FP8X4),
+                    lhsT_scale=wd_sc[:, P * i : P * (i + 1)],
+                    rhs=h_q[:, j0:j1].bitcast(FP8X4),
+                    rhs_scale=h_sc[:, j0:j1],
+                    start=True,
+                    stop=True,
+                )
+            for col, (i, j0, j1) in zip(cols, pieces):
+                nc.scalar.activation(y_sb[:, col], y_ps[:, col], ACT.Identity, bias=neg_usual[:, i : i + 1])
+            for col, (i, j0, j1) in zip(cols, pieces):
+                nc.vector.tensor_tensor(
+                    pages[i][:].indirect(offs2_sb[:, j0 // 16 : j1 // 16]), y_sb[:, col], wgo_sb[:, j0:j1], ALU.mult
+                )
 
-        def shift(i, y_ps, y_sb):
-            nc.scalar.activation(y_sb, y_ps, ACT.Identity, bias=neg_usual[:, i : i + 1])
+        extra = {3: [(3, 0, 256)], 4: [(3, 256, 512)], 5: [(2, 0, 256)], 6: [(2, 256, 512)]}
 
-        def put(i, j0, j1, y_sb):
-            nc.vector.tensor_tensor(pages[i][:].indirect(offs2_sb[:, j0 // 16 : j1 // 16]), y_sb, wgo_sb[:, j0:j1], ALU.mult)
-
-        def half_page(i, half, bank, slot):
-            y_ps = psum.tile([P, HALF], F32, name="y_half_ps", tag=bank)
-            y_sb = keep.tile([P, HALF], F32, name="y_half", tag=slot)
-            mark(i, HALF * half, HALF * (half + 1), y_ps[:], y_sb[:])
-            shift(i, y_ps[:], y_sb[:])
-            put(i, HALF * half, HALF * (half + 1), y_sb[:])
-
-        def early_pages(j0, j1, slot):
-            y_ps = psum.tile([P, 2, j1 - j0], F32, name="y_ps", tag="y")
-            y_sb = keep.tile([P, 2, j1 - j0], F32, name="y_early", tag=slot)
-            for i in range(2):
-                mark(i, j0, j1, y_ps[:, i, :], y_sb[:, i, :])
-            for i in range(2):
-                shift(i, y_ps[:, i, :], y_sb[:, i, :])
-            for i in range(2):
-                put(i, j0, j1, y_sb[:, i, :])
+        def early(k, slot):
+            place([(i, P * k, P * (k + 1)) for i in range(2)] + extra.get(k, []), "y", slot)
 
         first(0)
-        for c, (k0, k1) in enumerate(CHUNKS):
-            j0, j1 = P * k0, P * k1
-            h_bf = keep.tile([P, j1 - j0, 4], BF16, name="h_bf%d" % c, align_bytes=64)
-            for k in range(k0, k1):
-                second(k, h_bf, k0)
-            if k1 == TILES:
-                clear(pages[3])
-                clear(pages[2])
-                half_page(3, 0, "a", "c7")
-            if c == 0:
+        for k in range(TILES):
+            if k < PLAIN:
+                second(k)
+            if PLAIN <= k + 1 < TILES:
+                second(k + 1)
+            h_ps = turn(k)
+            h_bf = ring.tile([P, P, 4], BF16, name="h_bf", align_bytes=64)
+            nc.scalar.copy(h_bf[:], h_ps[:].rearrange("p t j -> p j t"))
+            if k == 0:
                 prepare_wd()
             nc.vector.quantize_mx(
-                out=h_q[:, j0:j1].bitcast(FP8X4), scales=h_sc[:, j0:j1], in_=h_bf[:].rearrange("p c j -> p (c j)")
+                out=h_q[:, P * k : P * (k + 1)].bitcast(FP8X4),
+                scales=h_sc[:, P * k : P * (k + 1)],
+                in_=h_bf[:].rearrange("p c j -> p (c j)"),
             )
-            if k1 == TILES:
-                half_page(2, 0, "a", "late")
-        early_pages(P * (TILES - 2), S, "y01")
-        half_page(2, 1, "b", "y2b")
-        half_page(3, 1, "b", "y3b")
+            if k >= 5:
+                early(k - 1, "ru%d" % k)
+        early(TILES - 1, "y_last")
+        place([(2, HALF, S)], "b", "y2b")
+        place([(3, HALF, S)], "b", "y3b")
         rows = out.rearrange("(p i) t -> i p t", i=4)
         for i in range(4):
             nc.sync.dma_start(rows[i], pages[i][:])

@@ -20,7 +20,25 @@ ACT = mybir.ActivationFunctionType
 P = 128
 TILES = S // P
 HALF = S // 2
-PLAIN = 6
+QUARTER = S // 4
+PLAIN = TILES - 2
+AHEAD = 3
+DEPTH = 3
+LAG = 2
+
+TERM = 4 * H
+AT_NEG_WB_BF = (0, 49152)
+AT_TAB_SC = 4096
+AT_TAB_W = (12288, 23552)
+AT_WA_SC = AT_TAB_W[0]
+AT_WA = AT_WA_SC + 2 * H
+AT_WGO = AT_WA + 4 * H
+AT_WD_RAW = AT_TAB_W[1] + 7168
+AT_HELD_U = AT_WD_RAW + TERM
+AT_FIRST_D = AT_NEG_WB_BF[1] - TERM // 2
+AT_PAGE3 = AT_FIRST_D + 2 * TERM
+AT_WD_BF = 68608
+AT_PAGE2 = AT_WD_BF + TERM
 
 
 def tile_list_skill_disagreement_marks_kernel(
@@ -31,7 +49,7 @@ def tile_list_skill_disagreement_marks_kernel(
         lists = ctx.enter_context(tc.tile_pool(name="lists", bufs=1))
         keep = ctx.enter_context(tc.tile_pool(name="keep", bufs=1))
         arena = ctx.enter_context(tc.tile_pool(name="arena", bufs=1))
-        ring = ctx.enter_context(tc.tile_pool(name="ring", bufs=3))
+        ring = ctx.enter_context(tc.tile_pool(name="ring", bufs=DEPTH))
         psum = ctx.enter_context(tc.psum_pool(name="psum", bufs=2))
 
         def placed(shape, dtype, name, offset):
@@ -41,38 +59,38 @@ def tile_list_skill_disagreement_marks_kernel(
         offs2_sb = lists.tile([P, S // 16], U16, name="offs2_sb")
         nc.sync.dma_start(offs_sb[:], offs)
         nc.sync.dma_start(offs2_sb[:], offs2)
-        warm = keep.tile([P, 2], F32, name="warm")
-        nc.vector.memset(warm[:, 0:1], 0.0)
-        nc.scalar.activation(warm[:, 1:2], warm[:, 0:1], ACT.Relu)
+        usual_sb = keep.tile([P, 4], F32, name="usual_sb")
+        nc.scalar.dma_start(usual_sb[:], usual.rearrange("(p i) -> p i", i=4))
+        neg_usual = keep.tile([P, 4], F32, name="neg_usual")
+        nc.scalar.activation(neg_usual[:], usual_sb[:], ACT.Identity, scale=-1.0)
 
-        tab_sc = placed([P, T], U8, "tab_sc", 4096)
+        tab_sc = placed([P, T], U8, "tab_sc", AT_TAB_SC)
         nc.gpsimd.memset(tab_sc[:].bitcast(I32), 0)
         sc_rows = tab_scales.bitcast(I32)
         for r in range(2):
             nc.sync.dma_start(tab_sc[r:P:16, :].bitcast(I32), sc_rows[0].rearrange("(g r) t -> r g t", r=2)[r])
         nc.sync.dma_start(tab_sc[4:P:8, :].bitcast(I32), sc_rows[1])
-        tab_w = [placed([P, T], I32, "tab_w%d" % a, (12288, 23552)[a]) for a in range(2)]
+        tab_w = [placed([P, T], I32, "tab_w%d" % a, AT_TAB_W[a]) for a in range(2)]
         for a in range(2):
             nc.sync.dma_start(tab_w[a][:], tab_words[a].rearrange("p t i -> p (t i)").bitcast(I32))
         wc_sb = keep.tile([P, 2, H], I32, name="wc_sb", align_bytes=64)
         nc.sync.dma_start(wc_sb[:], wc_words.rearrange("a p e i -> p a (e i)").bitcast(I32))
+        wb_rows = wb.rearrange("(a p j) c -> a p j c", a=2, j=4)
+        wb_raw = [keep.tile([P, 4, H], F32, name="wb_raw%d" % a, align_bytes=64) for a in range(2)]
+        for a in range(2):
+            nc.sync.dma_start(wb_raw[a][:], wb_rows[a])
         ident = keep.tile([P, P], F32, name="ident")
         make_identity(nc, ident[:])
         pages = [
             keep.tile([P, T2], F32, name="page0"),
             keep.tile([P, T2], F32, name="page1"),
-            placed([P, T2], F32, "page2", 68608 + 2048),
-            placed([P, T2], F32, "page3", 49152 + 2048),
+            placed([P, T2], F32, "page2", AT_PAGE2),
+            placed([P, T2], F32, "page3", AT_PAGE3),
         ]
 
         def clear(page):
             for half in range(2):
-                nc.vector.memset(page[:, 1024 * half : 1024 * (half + 1)].bitcast(I32), 0)
-
-        clear(pages[0])
-        clear(pages[1])
-        planes = [keep.tile([P, S], U8, name="plane%d" % a, align_bytes=64) for a in range(2)]
-        nc.vector.memset(planes[1][:].bitcast(I32), 0)
+                nc.vector.memset(page[:, T2 // 2 * half : T2 // 2 * (half + 1)].bitcast(I32), 0)
 
         def load_scales(sc, src):
             nc.vector.memset(sc[:].bitcast(I32), 0)
@@ -82,48 +100,49 @@ def tile_list_skill_disagreement_marks_kernel(
                     src[:, 4 * d : 4 * d + 4, :].rearrange("a r e -> r a e").bitcast(I32),
                 )
 
+        clear(pages[0])
+        clear(pages[1])
+        picked_scales = [keep.tile([P, S], U8, name="picked_scales%d" % a, align_bytes=64) for a in range(2)]
+        nc.vector.memset(picked_scales[1][:].bitcast(I32), 0)
         wc_sc = keep.tile([P, 2, H], U8, name="wc_sc", align_bytes=64)
         load_scales(wc_sc, wc_scales)
 
-        picked_sc = keep.tile([P, S], U8, name="picked_sc", align_bytes=64)
-        nc.vector.tensor_copy(picked_sc[:], tab_sc[:].indirect(offs_sb[:]))
-        nc.vector.tensor_copy(planes[0][:].bitcast(I32), picked_sc[:].bitcast(I32))
+        gathered_sc = keep.tile([P, S], U8, name="gathered_sc", align_bytes=64)
+        nc.vector.tensor_copy(gathered_sc[:], tab_sc[:].indirect(offs_sb[:]))
+        nc.vector.tensor_copy(picked_scales[0][:].bitcast(I32), gathered_sc[:].bitcast(I32))
         for r in range(2):
-            nc.scalar.dma_start(planes[0][2 + r : P : 32, :].bitcast(I32), picked_sc[16 + r : P : 32, :].bitcast(I32))
+            nc.scalar.dma_start(
+                picked_scales[0][2 + r : P : 32, :].bitcast(I32), gathered_sc[16 + r : P : 32, :].bitcast(I32)
+            )
         for r in range(4):
-            nc.scalar.dma_start(planes[1][r:P:32, :].bitcast(I32), picked_sc[8 * r + 4 : P : 32, :].bitcast(I32))
-        wb_rows = wb.rearrange("(a p j) c -> a p j c", a=2, j=4)
-        wb_raw = [placed([P, 4, H], F32, "wb_raw%d" % a, (4096, 15360)[a]) for a in range(2)]
-        nc.sync.dma_start(wb_raw[0][:], wb_rows[0])
+            nc.scalar.dma_start(
+                picked_scales[1][r:P:32, :].bitcast(I32), gathered_sc[8 * r + 4 : P : 32, :].bitcast(I32)
+            )
 
-        picked = [keep.tile([P, S], U32, name="picked%d" % a, align_bytes=64) for a in range(2)]
-        nc.vector.tensor_copy(picked[0][:], tab_w[0][:].bitcast(U32).indirect(offs_sb[:]))
-        nc.sync.dma_start(wb_raw[1][:], wb_rows[1])
-        wa_sb = placed([P, 2, 2 * H], U8, "wa_sb", 12288 + 1024)
+        picked_words = [keep.tile([P, S], U32, name="picked_words%d" % a, align_bytes=64) for a in range(2)]
+        nc.vector.tensor_copy(picked_words[0][:], tab_w[0][:].bitcast(U32).indirect(offs_sb[:]))
+        wa_sb = placed([P, 2, 2 * H], U8, "wa_sb", AT_WA)
         nc.sync.dma_start(wa_sb[:].bitcast(I32), wa_words.rearrange("a p n -> p a n").bitcast(I32))
-        wa_sc = placed([P, 2, H], U8, "wa_sc", 12288)
+        wgo_sb = placed([P, S], F32, "wgo_sb", AT_WGO)
+        nc.sync.dma_start(wgo_sb[:], wgo)
+        wa_sc = placed([P, 2, H], U8, "wa_sc", AT_WA_SC)
         load_scales(wa_sc, wa_scales)
         for half in range(2):
             nc.vector.tensor_copy(
-                picked[1][:, HALF * half : HALF * (half + 1)],
-                tab_w[1][:].bitcast(U32).indirect(offs_sb[:, 32 * half : 32 * (half + 1)]),
+                picked_words[1][:, HALF * half : HALF * (half + 1)],
+                tab_w[1][:].bitcast(U32).indirect(offs_sb[:, HALF // 16 * half : HALF // 16 * (half + 1)]),
             )
-        wgo_sb = placed([P, S], F32, "wgo_sb", 23552 + 2048)
-        nc.sync.dma_start(wgo_sb[:], wgo)
-        usual_sb = placed([P, 4], F32, "usual_sb", 23552 + 6144)
-        nc.sync.dma_start(usual_sb[:], usual.rearrange("(p i) -> p i", i=4))
-        neg_usual = keep.tile([P, 4], F32, name="neg_usual")
-        wd_raw = placed([P, 4, N], F32, "wd_raw", 23552 + 7168)
+        wd_raw = placed([P, 4, N], F32, "wd_raw", AT_WD_RAW)
         nc.sync.dma_start(wd_raw[:], wd.rearrange("(p j) c -> p j c", j=4))
 
-        def product(k, tag, *weights):
-            acc = psum.tile([P, H], F32, name="acc", tag=tag)
+        def product(k, bank, *weights):
+            acc = psum.tile([P, H], F32, name="acc", tag=bank)
             passes = [(a, codes[a], scales[a]) for codes, scales in weights for a in range(2)]
             for n, (a, rhs, rhs_sc) in enumerate(passes):
                 nc.tensor.matmul_mx(
                     out=acc[:],
-                    lhsT=picked[a][:, P * k : P * (k + 1)].bitcast(FP8X4),
-                    lhsT_scale=planes[a][:, P * k : P * (k + 1)],
+                    lhsT=picked_words[a][:, P * k : P * (k + 1)].bitcast(FP8X4),
+                    lhsT_scale=picked_scales[a][:, P * k : P * (k + 1)],
                     rhs=rhs,
                     rhs_scale=rhs_sc,
                     start=(n == 0),
@@ -134,93 +153,47 @@ def tile_list_skill_disagreement_marks_kernel(
         wa_mx = ([wa_sb[:, a, :].bitcast(FP4X4) for a in range(2)], [wa_sc[:, a, :] for a in range(2)])
         wc_mx = ([wc_sb[:, a, :].bitcast(FP8X4) for a in range(2)], [wc_sc[:, a, :] for a in range(2)])
         c_sb = []
-        for k in range(PLAIN):
-            c_ps = product(k, "hy"[k % 2], wc_mx)
+
+        def make_c(k, bank):
             c_k = keep.tile([P, 4, P], F32, name="c%d" % k)
-            nc.scalar.copy(c_k[:], c_ps)
+            nc.scalar.copy(c_k[:], product(k, bank, wc_mx))
             c_sb.append(c_k)
 
-        wb_bf = [placed([P, H, 4], BF16, "wb_bf%d" % a, (0, 49152)[a]) for a in range(2)]
-        wb_q = [keep.tile([P, H], U32, name="wb_q%d" % a, align_bytes=64) for a in range(2)]
-        wb_sc = [keep.tile([P, H], U8, name="wb_sc%d" % a, align_bytes=64) for a in range(2)]
-        for a, raw in enumerate(wb_raw):
-            nc.vector.tensor_scalar(wb_bf[a][:], raw[:].rearrange("p j c -> p c j"), -1.0, 0.0, ALU.mult, ALU.add)
-            nc.vector.quantize_mx(
-                out=wb_q[a][:].bitcast(FP8X4), scales=wb_sc[a][:], in_=wb_bf[a][:].rearrange("p c j -> p (c j)")
-            )
+        for k in range(AHEAD):
+            make_c(k, "hy"[k % 2])
 
-        wd_bf = placed([P, 4, P, 4], BF16, "wd_bf", 68608)
+        neg_wb_bf = [placed([P, H, 4], BF16, "neg_wb_bf%d" % a, AT_NEG_WB_BF[a]) for a in range(2)]
+        neg_wb_q = [keep.tile([P, H], U32, name="neg_wb_q%d" % a, align_bytes=64) for a in range(2)]
+        neg_wb_sc = [keep.tile([P, H], U8, name="neg_wb_sc%d" % a, align_bytes=64) for a in range(2)]
+        for a, raw in enumerate(wb_raw):
+            nc.vector.tensor_scalar(neg_wb_bf[a][:], raw[:].rearrange("p j c -> p c j"), -1.0, 0.0, ALU.mult, ALU.add)
+            nc.vector.quantize_mx(
+                out=neg_wb_q[a][:].bitcast(FP8X4),
+                scales=neg_wb_sc[a][:],
+                in_=neg_wb_bf[a][:].rearrange("p c j -> p (c j)"),
+            )
+        neg_wb_mx = ([q[:].bitcast(FP8X4) for q in neg_wb_q], [sc[:] for sc in neg_wb_sc])
+
+        wd_bf = placed([P, 4, P, 4], BF16, "wd_bf", AT_WD_BF)
         wd_q = keep.tile([P, N], U32, name="wd_q", align_bytes=64)
         wd_sc = keep.tile([P, N], U8, name="wd_sc", align_bytes=64)
 
-        def prepare_wd():
+        def quantise_wd():
             nc.vector.tensor_copy(
                 wd_bf[:].rearrange("p i m j -> p m i j"), wd_raw[:].rearrange("p j (m i) -> p m i j", i=4)
             )
-            nc.scalar.activation(neg_usual[:], usual_sb[:], ACT.Identity, scale=-1.0)
             nc.vector.quantize_mx(
                 out=wd_q[:].bitcast(FP8X4), scales=wd_sc[:], in_=wd_bf[:].rearrange("p i m j -> p (i m j)")
             )
-
-        nb_mx = ([q[:].bitcast(FP8X4) for q in wb_q], [sc[:] for sc in wb_sc])
-        d_sb, rd_sb, terms = [], [], []
-
-        def relu_of_negative(src, tag):
-            r_k = keep.tile([P, 4, P], F32, name="r_k", tag=tag)
-            nc.scalar.activation(r_k[:], src, ACT.Relu, scale=-1.0)
-            return r_k
-
-        def first(k):
-            d_k = keep.tile([P, 4, P], F32, name="d_k", tag="d%d" % k)
-            if k < PLAIN:
-                nc.vector.tensor_tensor(d_k[:], c_sb[k][:], product(k, "a", wa_mx), ALU.subtract)
-                rd_sb.append(relu_of_negative(d_k[:], "rd%d" % (k % 3)))
-            else:
-                d_ps = product(k, "a", wc_mx, nb_mx)
-                nc.scalar.copy(d_k[:], d_ps)
-                rd_sb.append(relu_of_negative(d_ps, "rd%d" % (k % 3)))
-            d_sb.append(d_k)
-
-        def second(k):
-            if k < PLAIN:
-                if k == 1:
-                    u_k = placed([P, 4, P], F32, "u_1", 23552 + 9216)
-                else:
-                    u_k = ring.tile([P, 4, P], F32, name="u_k")
-                nc.vector.tensor_tensor(u_k[:], product(k, "b", nb_mx), c_sb[k][:], ALU.add)
-                u = u_k[:]
-            else:
-                u = product(k, "b", wa_mx, nb_mx)
-            ru_k = relu_of_negative(u, "ru%d" % (k % 3 if k < 5 else k))
-            if k + 1 < TILES:
-                first(k + 1)
-            m_k = ring.tile([P, 4, P], F32, name="m_k")
-            nc.vector.tensor_tensor(m_k[:], u, d_sb[k][:], ALU.max)
-            if k == 5:
-                clear(pages[3])
-                clear(pages[2])
-            if 2 <= k <= 5:
-                early(k - 2, "d%d" % k)
-            terms.append((rd_sb[k], m_k, ru_k))
-
-        def turn(k):
-            h_ps = psum.tile([P, 4, P], F32, name="h_ps", tag="h")
-            for t in range(4):
-                for n, term in enumerate(terms[k]):
-                    nc.tensor.matmul(
-                        h_ps[:, t, :], term[:, t, :], ident[:], start=(n == 0), stop=(n == 2), is_transpose=True
-                    )
-            return h_ps
 
         h_q = keep.tile([P, S], U32, name="h_q", align_bytes=64)
         h_sc = keep.tile([P, S], U8, name="h_sc", align_bytes=64)
 
         def place(pieces, bank, slot):
-            width = sum(j1 - j0 for i, j0, j1 in pieces)
-            y_ps = psum.tile([P, width], F32, name="y_ps", tag=bank)
-            y_sb = keep.tile([P, width], F32, name="y_sb", tag=slot)
-            starts = [sum(j1 - j0 for i, j0, j1 in pieces[:n]) for n in range(len(pieces))]
-            cols = [slice(at, at + j1 - j0) for at, (i, j0, j1) in zip(starts, pieces)]
+            widths = [j1 - j0 for i, j0, j1 in pieces]
+            cols = [slice(sum(widths[:n]), sum(widths[: n + 1])) for n in range(len(pieces))]
+            y_ps = psum.tile([P, sum(widths)], F32, name="y_ps", tag=bank)
+            y_sb = keep.tile([P, sum(widths)], F32, name="y_sb", tag=slot)
             for col, (i, j0, j1) in zip(cols, pieces):
                 nc.tensor.matmul_mx(
                     out=y_ps[:, col],
@@ -238,32 +211,87 @@ def tile_list_skill_disagreement_marks_kernel(
                     pages[i][:].indirect(offs2_sb[:, j0 // 16 : j1 // 16]), y_sb[:, col], wgo_sb[:, j0:j1], ALU.mult
                 )
 
-        extra = {3: [(3, 0, 256)], 4: [(3, 256, 512)], 5: [(2, 0, 256)], 6: [(2, 256, 512)]}
+        quarters = [(i, QUARTER * n, QUARTER * (n + 1)) for i in (3, 2) for n in range(2)]
+        extra = {TILES - 1 - len(quarters) + n: [piece] for n, piece in enumerate(quarters)}
 
-        def early(k, slot):
+        def place_tile(k, slot):
             place([(i, P * k, P * (k + 1)) for i in range(2)] + extra.get(k, []), "y", slot)
 
-        first(0)
-        for k in range(TILES):
+        d_sb, rd_sb, terms = [], [], []
+
+        def relu_of_negative(src, tag):
+            r_k = keep.tile([P, 4, P], F32, name="r_k", tag=tag)
+            nc.scalar.activation(r_k[:], src, ACT.Relu, scale=-1.0)
+            return r_k
+
+        def make_d(k):
+            if AHEAD <= k + 1 < PLAIN:
+                make_c(k + 1, "a")
+            if k < LAG:
+                d_k = placed([P, 4, P], F32, "d_first%d" % k, AT_FIRST_D + TERM * k)
+            else:
+                d_k = keep.tile([P, 4, P], F32, name="d_k", tag="d%d" % k)
             if k < PLAIN:
-                second(k)
-            if PLAIN <= k + 1 < TILES:
-                second(k + 1)
-            h_ps = turn(k)
+                nc.vector.tensor_tensor(d_k[:], c_sb[k][:], product(k, "a", wa_mx), ALU.subtract)
+                rd_sb.append(relu_of_negative(d_k[:], "rd%d" % (k % DEPTH)))
+            else:
+                d_ps = product(k, "a", wc_mx, neg_wb_mx)
+                nc.scalar.copy(d_k[:], d_ps)
+                rd_sb.append(relu_of_negative(d_ps, "rd%d" % (k % DEPTH)))
+            d_sb.append(d_k)
+
+        def make_terms(k):
+            if k < PLAIN:
+                if k == LAG:
+                    u_k = placed([P, 4, P], F32, "u_held", AT_HELD_U)
+                else:
+                    u_k = ring.tile([P, 4, P], F32, name="u_k")
+                nc.vector.tensor_tensor(u_k[:], product(k, "b", neg_wb_mx), c_sb[k][:], ALU.add)
+                u = u_k[:]
+            else:
+                u = product(k, "b", wa_mx, neg_wb_mx)
+            ru_k = relu_of_negative(u, "ru%d" % (k % DEPTH if k < PLAIN - 1 else k))
+            if k + 1 < TILES:
+                make_d(k + 1)
+            m_k = ring.tile([P, 4, P], F32, name="m_k")
+            nc.vector.tensor_tensor(m_k[:], u, d_sb[k][:], ALU.max)
+            if k - LAG == min(extra):
+                clear(pages[3])
+                clear(pages[2])
+            if LAG <= k < PLAIN:
+                place_tile(k - LAG, "d%d" % k)
+            terms.append((rd_sb[k], m_k, ru_k))
+
+        def turn(k):
+            h_ps = psum.tile([P, 4, P], F32, name="h_ps", tag="h")
+            for t in range(4):
+                for n, term in enumerate(terms[k]):
+                    nc.tensor.matmul(
+                        h_ps[:, t, :], term[:, t, :], ident[:], start=(n == 0), stop=(n == 2), is_transpose=True
+                    )
             h_bf = ring.tile([P, P, 4], BF16, name="h_bf", align_bytes=64)
             nc.scalar.copy(h_bf[:], h_ps[:].rearrange("p t j -> p j t"))
+            return h_bf
+
+        make_d(0)
+        for k in range(TILES):
+            if k < PLAIN:
+                make_terms(k)
+            if PLAIN <= k + 1 < TILES:
+                make_terms(k + 1)
+            h_bf = turn(k)
             if k == 0:
-                prepare_wd()
+                quantise_wd()
             nc.vector.quantize_mx(
                 out=h_q[:, P * k : P * (k + 1)].bitcast(FP8X4),
                 scales=h_sc[:, P * k : P * (k + 1)],
                 in_=h_bf[:].rearrange("p c j -> p (c j)"),
             )
-            if k >= 5:
-                early(k - 1, "ru%d" % k)
-        early(TILES - 1, "y_last")
-        place([(2, HALF, S)], "b", "y2b")
-        place([(3, HALF, S)], "b", "y3b")
+            if k >= PLAIN - 1:
+                place_tile(k - 1, "ru%d" % k)
+        place_tile(TILES - 1, "y_last")
+        place([(2, HALF, S)], "b", "y_page2")
+        place([(3, HALF, S)], "b", "y_page3")
         rows = out.rearrange("(p i) t -> i p t", i=4)
         for i in range(4):
             nc.sync.dma_start(rows[i], pages[i][:])

@@ -20,25 +20,20 @@ ACT = mybir.ActivationFunctionType
 P = 128
 TILES = S // P
 HALF = S // 2
-QUARTER = S // 4
+PAIR = 2 * P
+PAIRS = TILES // 2
 PLAIN = TILES - 2
-AHEAD = 3
-DEPTH = 3
-LAG = 2
+AHEAD = 4
 
-TERM = 4 * H
-AT_NEG_WB_BF = (0, 49152)
-AT_TAB_SC = 4096
-AT_TAB_W = (12288, 23552)
-AT_WA_SC = AT_TAB_W[0]
-AT_WA = AT_WA_SC + 2 * H
-AT_WGO = AT_WA + 4 * H
-AT_WD_RAW = AT_TAB_W[1] + 7168
-AT_HELD_U = AT_WD_RAW + TERM
-AT_FIRST_D = AT_NEG_WB_BF[1] - TERM // 2
-AT_PAGE3 = AT_FIRST_D + 2 * TERM
-AT_WD_BF = 68608
-AT_PAGE2 = AT_WD_BF + TERM
+PAGE = 4 * T2
+AT_PAGE2 = 0
+AT_TAB0 = PAGE - 64
+AT_WB1 = PAGE
+AT_TAB1 = AT_WB1 + 16 * H + 4 * S
+AT_USUAL = AT_TAB1 + 64
+AT_WD = AT_USUAL + 64
+AT_WGO = AT_USUAL - 4 * S
+AT_WB_BF1 = AT_WD + 16 * N
 
 
 def tile_list_skill_disagreement_marks_kernel(
@@ -49,91 +44,98 @@ def tile_list_skill_disagreement_marks_kernel(
         lists = ctx.enter_context(tc.tile_pool(name="lists", bufs=1))
         keep = ctx.enter_context(tc.tile_pool(name="keep", bufs=1))
         arena = ctx.enter_context(tc.tile_pool(name="arena", bufs=1))
-        ring = ctx.enter_context(tc.tile_pool(name="ring", bufs=DEPTH))
         psum = ctx.enter_context(tc.psum_pool(name="psum", bufs=2))
 
         def placed(shape, dtype, name, offset):
             return arena.tile(shape, dtype, name=name, offset=offset, align_bytes=64)
 
+        def held(shape, dtype, name, tag=None):
+            return keep.tile(shape, dtype, name=name, tag=tag or name, align_bytes=64)
+
         offs_sb = lists.tile([P, S // 16], U16, name="offs_sb")
         offs2_sb = lists.tile([P, S // 16], U16, name="offs2_sb")
-        nc.sync.dma_start(offs_sb[:], offs)
-        nc.sync.dma_start(offs2_sb[:], offs2)
-        usual_sb = keep.tile([P, 4], F32, name="usual_sb")
-        nc.scalar.dma_start(usual_sb[:], usual.rearrange("(p i) -> p i", i=4))
-        neg_usual = keep.tile([P, 4], F32, name="neg_usual")
-        nc.scalar.activation(neg_usual[:], usual_sb[:], ACT.Identity, scale=-1.0)
-
-        tab_sc = placed([P, T], U8, "tab_sc", AT_TAB_SC)
+        tab_sc = held([P, T], U8, "tab_sc")
+        planes = [held([P, S + 2 * H], U8, "plane%d" % a) for a in range(2)]
+        staged = held([P, S + 2 * H], U8, "staged")
+        nc.gpsimd.memset(staged[:, S : S + H].bitcast(I32), 0)
         nc.gpsimd.memset(tab_sc[:].bitcast(I32), 0)
-        sc_rows = tab_scales.bitcast(I32)
-        for r in range(2):
-            nc.sync.dma_start(tab_sc[r:P:16, :].bitcast(I32), sc_rows[0].rearrange("(g r) t -> r g t", r=2)[r])
-        nc.sync.dma_start(tab_sc[4:P:8, :].bitcast(I32), sc_rows[1])
-        tab_w = [placed([P, T], I32, "tab_w%d" % a, AT_TAB_W[a]) for a in range(2)]
-        for a in range(2):
-            nc.sync.dma_start(tab_w[a][:], tab_words[a].rearrange("p t i -> p (t i)").bitcast(I32))
-        wc_sb = keep.tile([P, 2, H], I32, name="wc_sb", align_bytes=64)
-        nc.sync.dma_start(wc_sb[:], wc_words.rearrange("a p e i -> p a (e i)").bitcast(I32))
+        nc.gpsimd.memset(staged[:, S + H :].bitcast(I32), 0)
+        nc.gpsimd.memset(planes[1][:].bitcast(I32), 0)
+
+        nc.sync.dma_start(offs_sb[:], offs)
+
+        def load_scale_rows(dst, src):
+            rows = src.bitcast(I32)
+            for r in range(2):
+                nc.sync.dma_start(dst[r:P:16, :].bitcast(I32), rows[0].rearrange("(g r) t -> r g t", r=2)[r])
+            nc.sync.dma_start(dst[4:P:8, :].bitcast(I32), rows[1])
+
+        tab_w = [placed([P, T], I32, "tab_w%d" % a, (AT_TAB0, AT_TAB1)[a]) for a in range(2)]
         wb_rows = wb.rearrange("(a p j) c -> a p j c", a=2, j=4)
-        wb_raw = [keep.tile([P, 4, H], F32, name="wb_raw%d" % a, align_bytes=64) for a in range(2)]
-        for a in range(2):
-            nc.sync.dma_start(wb_raw[a][:], wb_rows[a])
-        ident = keep.tile([P, P], F32, name="ident")
-        make_identity(nc, ident[:])
-        pages = [
-            keep.tile([P, T2], F32, name="page0"),
-            keep.tile([P, T2], F32, name="page1"),
-            placed([P, T2], F32, "page2", AT_PAGE2),
-            placed([P, T2], F32, "page3", AT_PAGE3),
-        ]
+        wb_raw = [held([P, 4, H], F32, "wb_raw0"), placed([P, 4, H], F32, "wb_raw1", AT_WB1)]
+        wc_sb = held([P, 2, H], I32, "wc_sb")
+        wa_sb = held([P, 2, 2 * H], U8, "wa_sb")
 
-        def clear(page):
-            for half in range(2):
-                nc.vector.memset(page[:, T2 // 2 * half : T2 // 2 * (half + 1)].bitcast(I32), 0)
+        def load_words(a):
+            nc.sync.dma_start(tab_w[a][:], tab_words[a].rearrange("p t i -> p (t i)").bitcast(I32))
 
-        def load_scales(sc, src):
-            nc.vector.memset(sc[:].bitcast(I32), 0)
-            for d in range(4):
-                nc.scalar.dma_start(
-                    sc[32 * d : 32 * d + 4].bitcast(I32),
-                    src[:, 4 * d : 4 * d + 4, :].rearrange("a r e -> r a e").bitcast(I32),
-                )
-
-        clear(pages[0])
-        clear(pages[1])
-        picked_scales = [keep.tile([P, S], U8, name="picked_scales%d" % a, align_bytes=64) for a in range(2)]
-        nc.vector.memset(picked_scales[1][:].bitcast(I32), 0)
-        wc_sc = keep.tile([P, 2, H], U8, name="wc_sc", align_bytes=64)
-        load_scales(wc_sc, wc_scales)
-
-        gathered_sc = keep.tile([P, S], U8, name="gathered_sc", align_bytes=64)
-        nc.vector.tensor_copy(gathered_sc[:], tab_sc[:].indirect(offs_sb[:]))
-        nc.vector.tensor_copy(picked_scales[0][:].bitcast(I32), gathered_sc[:].bitcast(I32))
-        for r in range(2):
-            nc.scalar.dma_start(
-                picked_scales[0][2 + r : P : 32, :].bitcast(I32), gathered_sc[16 + r : P : 32, :].bitcast(I32)
-            )
-        for r in range(4):
-            nc.scalar.dma_start(
-                picked_scales[1][r:P:32, :].bitcast(I32), gathered_sc[8 * r + 4 : P : 32, :].bitcast(I32)
-            )
-
-        picked_words = [keep.tile([P, S], U32, name="picked_words%d" % a, align_bytes=64) for a in range(2)]
-        nc.vector.tensor_copy(picked_words[0][:], tab_w[0][:].bitcast(U32).indirect(offs_sb[:]))
-        wa_sb = placed([P, 2, 2 * H], U8, "wa_sb", AT_WA)
+        load_scale_rows(staged[:, S : S + H], wc_scales)
+        load_scale_rows(tab_sc, tab_scales)
+        load_words(0)
+        nc.sync.dma_start(wc_sb[:], wc_words.rearrange("a p e i -> p a (e i)").bitcast(I32))
         nc.sync.dma_start(wa_sb[:].bitcast(I32), wa_words.rearrange("a p n -> p a n").bitcast(I32))
-        wgo_sb = placed([P, S], F32, "wgo_sb", AT_WGO)
-        nc.sync.dma_start(wgo_sb[:], wgo)
-        wa_sc = placed([P, 2, H], U8, "wa_sc", AT_WA_SC)
-        load_scales(wa_sc, wa_scales)
+        load_scale_rows(staged[:, S + H :], wa_scales)
+        nc.sync.dma_start(offs2_sb[:], offs2)
+        load_words(1)
+        nc.sync.dma_start(wb_raw[0][:], wb_rows[0])
+
+        pages = [held([P, T2], F32, "page0"), held([P, T2], F32, "page1"), placed([P, T2], F32, "page2", AT_PAGE2)]
+        pages.append(pages[0])
+        ident = held([P, P], F32, "ident")
+        make_identity(nc, ident[:])
+        for i in range(2):
+            nc.vector.memset(pages[i][:].bitcast(I32), 0)
+
+        gathered_sc = held([P, S], U8, "gathered_sc")
+        nc.vector.tensor_copy(gathered_sc[:], tab_sc[:].indirect(offs_sb[:]))
+        nc.vector.tensor_copy(staged[:, :S].bitcast(I32), gathered_sc[:].bitcast(I32))
+        nc.vector.tensor_copy(planes[0][:, :S].bitcast(I32), gathered_sc[:].bitcast(I32))
+        nc.gpsimd.tensor_copy(planes[0][:, S:].bitcast(I32), staged[:, S:].bitcast(I32))
+        for r in range(2):
+            nc.scalar.dma_start(planes[0][2 + r : P : 32, :].bitcast(I32), staged[16 + r : P : 32, :].bitcast(I32))
+        for r in range(4):
+            nc.scalar.dma_start(planes[1][r:P:32, :].bitcast(I32), staged[8 * r + 4 : P : 32, :].bitcast(I32))
+
+        picked_words = [held([P, S], U32, "picked_words%d" % a) for a in range(2)]
+        nc.vector.tensor_copy(picked_words[0][:], tab_w[0][:].bitcast(U32).indirect(offs_sb[:]))
+        nc.sync.dma_start(wb_raw[1][:], wb_rows[1])
+        nc.vector.memset(pages[2][:].bitcast(I32), 0)
+
+        neg_wb_bf = [held([P, 4 * H], BF16, "neg_wb_bf0"), placed([P, 4 * H], BF16, "neg_wb_bf1", AT_WB_BF1)]
+        neg_wb_q = [held([P, H], U32, "neg_wb_q%d" % a) for a in range(2)]
+        neg_wb_sc = [held([P, H], U8, "neg_wb_sc%d" % a) for a in range(2)]
+
+        def walk(a):
+            return (
+                neg_wb_bf[a][:].rearrange("p (c i j) -> p c j i", i=4, j=4),
+                wb_raw[a][:].rearrange("p j (c i) -> p c j i", i=4),
+            )
+
+        def quantise_wb(a):
+            nc.vector.quantize_mx(out=neg_wb_q[a][:].bitcast(FP8X4), scales=neg_wb_sc[a][:], in_=neg_wb_bf[a][:])
+
         for half in range(2):
             nc.vector.tensor_copy(
                 picked_words[1][:, HALF * half : HALF * (half + 1)],
                 tab_w[1][:].bitcast(U32).indirect(offs_sb[:, HALF // 16 * half : HALF // 16 * (half + 1)]),
             )
-        wd_raw = placed([P, 4, N], F32, "wd_raw", AT_WD_RAW)
+        wd_raw = placed([P, 4, N], F32, "wd_raw", AT_WD)
         nc.sync.dma_start(wd_raw[:], wd.rearrange("(p j) c -> p j c", j=4))
+        wgo_sb = placed([P, S], F32, "wgo_sb", AT_WGO)
+        nc.sync.dma_start(wgo_sb[:], wgo)
+        usual_sb = placed([P, 4], F32, "usual_sb", AT_USUAL)
+        nc.sync.dma_start(usual_sb[:], usual.rearrange("(p i) -> p i", i=4))
+        nc.vector.tensor_scalar(*walk(0), -1.0, 0.0, ALU.mult, ALU.add)
 
         def product(k, bank, *weights):
             acc = psum.tile([P, H], F32, name="acc", tag=bank)
@@ -142,7 +144,7 @@ def tile_list_skill_disagreement_marks_kernel(
                 nc.tensor.matmul_mx(
                     out=acc[:],
                     lhsT=picked_words[a][:, P * k : P * (k + 1)].bitcast(FP8X4),
-                    lhsT_scale=picked_scales[a][:, P * k : P * (k + 1)],
+                    lhsT_scale=planes[a][:, P * k : P * (k + 1)],
                     rhs=rhs,
                     rhs_scale=rhs_sc,
                     start=(n == 0),
@@ -150,148 +152,168 @@ def tile_list_skill_disagreement_marks_kernel(
                 )
             return acc[:].rearrange("p (m t) -> p t m", t=4)
 
-        wa_mx = ([wa_sb[:, a, :].bitcast(FP4X4) for a in range(2)], [wa_sc[:, a, :] for a in range(2)])
-        wc_mx = ([wc_sb[:, a, :].bitcast(FP8X4) for a in range(2)], [wc_sc[:, a, :] for a in range(2)])
-        c_sb = []
-
-        def make_c(k, bank):
-            c_k = keep.tile([P, 4, P], F32, name="c%d" % k)
-            nc.scalar.copy(c_k[:], product(k, bank, wc_mx))
-            c_sb.append(c_k)
-
-        for k in range(AHEAD):
-            make_c(k, "hy"[k % 2])
-
-        neg_wb_bf = [placed([P, H, 4], BF16, "neg_wb_bf%d" % a, AT_NEG_WB_BF[a]) for a in range(2)]
-        neg_wb_q = [keep.tile([P, H], U32, name="neg_wb_q%d" % a, align_bytes=64) for a in range(2)]
-        neg_wb_sc = [keep.tile([P, H], U8, name="neg_wb_sc%d" % a, align_bytes=64) for a in range(2)]
-        for a, raw in enumerate(wb_raw):
-            nc.vector.tensor_scalar(neg_wb_bf[a][:], raw[:].rearrange("p j c -> p c j"), -1.0, 0.0, ALU.mult, ALU.add)
-            nc.vector.quantize_mx(
-                out=neg_wb_q[a][:].bitcast(FP8X4),
-                scales=neg_wb_sc[a][:],
-                in_=neg_wb_bf[a][:].rearrange("p c j -> p (c j)"),
-            )
+        wc_mx = ([wc_sb[:, a, :].bitcast(FP8X4) for a in range(2)], [sc[:, S : S + H] for sc in planes])
+        wa_mx = ([wa_sb[:, a, :].bitcast(FP4X4) for a in range(2)], [sc[:, S + H :] for sc in planes])
         neg_wb_mx = ([q[:].bitcast(FP8X4) for q in neg_wb_q], [sc[:] for sc in neg_wb_sc])
 
-        wd_bf = placed([P, 4, P, 4], BF16, "wd_bf", AT_WD_BF)
-        wd_q = keep.tile([P, N], U32, name="wd_q", align_bytes=64)
-        wd_sc = keep.tile([P, N], U8, name="wd_sc", align_bytes=64)
+        def terms(name, tags):
+            return [held([P, 2 * H], F32, "%s%d" % (name, n), "%s%d" % (name, n % tags)) for n in range(PAIRS)]
 
-        def quantise_wd():
-            nc.vector.tensor_copy(
-                wd_bf[:].rearrange("p i m j -> p m i j"), wd_raw[:].rearrange("p j (m i) -> p m i j", i=4)
-            )
+        u_sb, m_sb, rd_sb, ru_sb = terms("u", 2), terms("m", 2), terms("rd", 2), terms("ru", 4)
+        d_sb = [placed([P, 2 * H], F32, "d%d" % n, (AT_WB1 + 64, AT_WB_BF1)[n % 2]) for n in range(PAIRS)]
+        c_sb = {}
+
+        def half(term, k):
+            return term[k // 2][:, H * (k % 2) : H * (k % 2 + 1)]
+
+        def slots(ap):
+            return ap.rearrange("p (t m) -> p t m", t=4)
+
+        def relu_neg(dst, src):
+            nc.scalar.activation(dst, src, ACT.Relu, scale=-1.0)
+
+        def make_d(k):
+            c_sb[k] = held([P, H], F32, "c%d" % k)
+            nc.scalar.copy(slots(c_sb[k][:]), product(k, "h" if k < AHEAD else "a", wc_mx))
+            a_ps = product(k, "y" if k == 2 else "a", wa_mx)
+            nc.vector.tensor_tensor(slots(half(d_sb, k)), slots(c_sb[k][:]), a_ps, ALU.subtract)
+
+        def make_u(k):
+            nc.vector.tensor_tensor(slots(half(u_sb, k)), product(k, "b", neg_wb_mx), slots(c_sb[k][:]), ALU.add)
+
+        def paired(k):
+            d_ps = product(k, "a", wc_mx, neg_wb_mx)
+            nc.scalar.copy(slots(half(d_sb, k)), d_ps)
+            relu_neg(slots(half(rd_sb, k)), d_ps)
+            u_ps = product(k, "b", wa_mx, neg_wb_mx)
+            relu_neg(slots(half(ru_sb, k)), u_ps)
+            nc.vector.tensor_tensor(slots(half(m_sb, k)), u_ps, slots(half(d_sb, k)), ALU.max)
+
+        h_q = held([P, S], U32, "h_q")
+        h_sc = held([P, S], U8, "h_sc")
+
+        def turn(n):
+            h_bf = held([P, 4 * PAIR], BF16, "h_bf%d" % n, "h_bf%d" % (n % 2))
+            for k in (2 * n, 2 * n + 1):
+                h_ps = psum.tile([P, 4, P], F32, name="h_ps", tag="h")
+                for t in range(4):
+                    for e, term in enumerate((rd_sb, m_sb, ru_sb)):
+                        nc.tensor.matmul(
+                            h_ps[:, t, :], slots(half(term, k))[:, t, :], ident[:],
+                            start=(e == 0), stop=(e == 2), is_transpose=True,
+                        )
+                nc.scalar.copy(
+                    h_bf[:, H * (k % 2) : H * (k % 2 + 1)].rearrange("p (j t) -> p j t", t=4),
+                    h_ps[:].rearrange("p t j -> p j t"),
+                )
+            return h_bf
+
+        def quantise_h(n, h_bf):
             nc.vector.quantize_mx(
-                out=wd_q[:].bitcast(FP8X4), scales=wd_sc[:], in_=wd_bf[:].rearrange("p i m j -> p (i m j)")
+                out=h_q[:, PAIR * n : PAIR * (n + 1)].bitcast(FP8X4),
+                scales=h_sc[:, PAIR * n : PAIR * (n + 1)],
+                in_=h_bf[:],
             )
 
-        h_q = keep.tile([P, S], U32, name="h_q", align_bytes=64)
-        h_sc = keep.tile([P, S], U8, name="h_sc", align_bytes=64)
+        wd_q = held([P, N], U32, "wd_q")
+        wd_sc = held([P, N], U8, "wd_sc")
 
-        def place(pieces, bank, slot):
+        def marks(i, j0, j1, y_ps, y_sb):
+            nc.tensor.matmul_mx(
+                out=y_ps,
+                lhsT=wd_q[:, P * i : P * (i + 1)].bitcast(FP8X4),
+                lhsT_scale=wd_sc[:, P * i : P * (i + 1)],
+                rhs=h_q[:, j0:j1].bitcast(FP8X4),
+                rhs_scale=h_sc[:, j0:j1],
+                start=True,
+                stop=True,
+            )
+
+        def shift(i, y_ps, y_sb):
+            nc.scalar.activation(y_sb, y_ps, ACT.Identity, bias=neg_usual[:, i : i + 1])
+
+        def scatter(i, j0, j1, y_sb):
+            nc.vector.tensor_tensor(
+                pages[i][:].indirect(offs2_sb[:, j0 // 16 : j1 // 16]), y_sb, wgo_sb[:, j0:j1], ALU.mult
+            )
+
+        def place(pieces, bank, tag):
             widths = [j1 - j0 for i, j0, j1 in pieces]
             cols = [slice(sum(widths[:n]), sum(widths[: n + 1])) for n in range(len(pieces))]
             y_ps = psum.tile([P, sum(widths)], F32, name="y_ps", tag=bank)
-            y_sb = keep.tile([P, sum(widths)], F32, name="y_sb", tag=slot)
+            y_sb = held([P, sum(widths)], F32, "y_sb", tag)
             for col, (i, j0, j1) in zip(cols, pieces):
-                nc.tensor.matmul_mx(
-                    out=y_ps[:, col],
-                    lhsT=wd_q[:, P * i : P * (i + 1)].bitcast(FP8X4),
-                    lhsT_scale=wd_sc[:, P * i : P * (i + 1)],
-                    rhs=h_q[:, j0:j1].bitcast(FP8X4),
-                    rhs_scale=h_sc[:, j0:j1],
-                    start=True,
-                    stop=True,
-                )
+                marks(i, j0, j1, y_ps[:, col], y_sb[:, col])
             for col, (i, j0, j1) in zip(cols, pieces):
-                nc.scalar.activation(y_sb[:, col], y_ps[:, col], ACT.Identity, bias=neg_usual[:, i : i + 1])
+                shift(i, y_ps[:, col], y_sb[:, col])
             for col, (i, j0, j1) in zip(cols, pieces):
-                nc.vector.tensor_tensor(
-                    pages[i][:].indirect(offs2_sb[:, j0 // 16 : j1 // 16]), y_sb[:, col], wgo_sb[:, j0:j1], ALU.mult
-                )
+                scatter(i, j0, j1, y_sb[:, col])
 
-        quarters = [(i, QUARTER * n, QUARTER * (n + 1)) for i in (3, 2) for n in range(2)]
-        extra = {TILES - 1 - len(quarters) + n: [piece] for n, piece in enumerate(quarters)}
+        def piece(i, n, n1=None):
+            return (i, PAIR * n, PAIR * ((n if n1 is None else n1) + 1))
 
-        def place_tile(k, slot):
-            place([(i, P * k, P * (k + 1)) for i in range(2)] + extra.get(k, []), "y", slot)
-
-        d_sb, rd_sb, terms = [], [], []
-
-        def relu_of_negative(src, tag):
-            r_k = keep.tile([P, 4, P], F32, name="r_k", tag=tag)
-            nc.scalar.activation(r_k[:], src, ACT.Relu, scale=-1.0)
-            return r_k
-
-        def make_d(k):
-            if AHEAD <= k + 1 < PLAIN:
-                make_c(k + 1, "a")
-            if k < LAG:
-                d_k = placed([P, 4, P], F32, "d_first%d" % k, AT_FIRST_D + TERM * k)
-            else:
-                d_k = keep.tile([P, 4, P], F32, name="d_k", tag="d%d" % k)
-            if k < PLAIN:
-                nc.vector.tensor_tensor(d_k[:], c_sb[k][:], product(k, "a", wa_mx), ALU.subtract)
-                rd_sb.append(relu_of_negative(d_k[:], "rd%d" % (k % DEPTH)))
-            else:
-                d_ps = product(k, "a", wc_mx, neg_wb_mx)
-                nc.scalar.copy(d_k[:], d_ps)
-                rd_sb.append(relu_of_negative(d_ps, "rd%d" % (k % DEPTH)))
-            d_sb.append(d_k)
-
-        def make_terms(k):
-            if k < PLAIN:
-                if k == LAG:
-                    u_k = placed([P, 4, P], F32, "u_held", AT_HELD_U)
-                else:
-                    u_k = ring.tile([P, 4, P], F32, name="u_k")
-                nc.vector.tensor_tensor(u_k[:], product(k, "b", neg_wb_mx), c_sb[k][:], ALU.add)
-                u = u_k[:]
-            else:
-                u = product(k, "b", wa_mx, neg_wb_mx)
-            ru_k = relu_of_negative(u, "ru%d" % (k % DEPTH if k < PLAIN - 1 else k))
-            if k + 1 < TILES:
-                make_d(k + 1)
-            m_k = ring.tile([P, 4, P], F32, name="m_k")
-            nc.vector.tensor_tensor(m_k[:], u, d_sb[k][:], ALU.max)
-            if k - LAG == min(extra):
-                clear(pages[3])
-                clear(pages[2])
-            if LAG <= k < PLAIN:
-                place_tile(k - LAG, "d%d" % k)
-            terms.append((rd_sb[k], m_k, ru_k))
-
-        def turn(k):
-            h_ps = psum.tile([P, 4, P], F32, name="h_ps", tag="h")
-            for t in range(4):
-                for n, term in enumerate(terms[k]):
-                    nc.tensor.matmul(
-                        h_ps[:, t, :], term[:, t, :], ident[:], start=(n == 0), stop=(n == 2), is_transpose=True
-                    )
-            h_bf = ring.tile([P, P, 4], BF16, name="h_bf", align_bytes=64)
-            nc.scalar.copy(h_bf[:], h_ps[:].rearrange("p t j -> p j t"))
-            return h_bf
-
-        make_d(0)
-        for k in range(TILES):
-            if k < PLAIN:
-                make_terms(k)
-            if PLAIN <= k + 1 < TILES:
-                make_terms(k + 1)
-            h_bf = turn(k)
-            if k == 0:
-                quantise_wd()
-            nc.vector.quantize_mx(
-                out=h_q[:, P * k : P * (k + 1)].bitcast(FP8X4),
-                scales=h_sc[:, P * k : P * (k + 1)],
-                in_=h_bf[:].rearrange("p c j -> p (c j)"),
-            )
-            if k >= PLAIN - 1:
-                place_tile(k - 1, "ru%d" % k)
-        place_tile(TILES - 1, "y_last")
-        place([(2, HALF, S)], "b", "y_page2")
-        place([(3, HALF, S)], "b", "y_page3")
         rows = out.rearrange("(p i) t -> i p t", i=4)
-        for i in range(4):
-            nc.sync.dma_start(rows[i], pages[i][:])
+
+        nc.vector.tensor_scalar(*walk(1), -1.0, 0.0, ALU.mult, ALU.add)
+        quantise_wb(0)
+        quantise_wb(1)
+        make_d(0)
+        make_d(1)
+        relu_neg(rd_sb[0][:], d_sb[0][:])
+        make_d(2)
+        make_d(3)
+        for k in range(2):
+            make_u(k)
+            relu_neg(half(ru_sb, k), half(u_sb, k))
+        for k in range(2):
+            nc.vector.tensor_tensor(half(m_sb, k), half(u_sb, k), half(d_sb, k), ALU.max)
+        neg_usual = held([P, 4], F32, "neg_usual", "c0")
+        nc.scalar.activation(neg_usual[:], usual_sb[:], ACT.Identity, scale=-1.0)
+        relu_neg(rd_sb[1][:], d_sb[1][:])
+        wd_bf = held([P, 4, P, 4], BF16, "wd_bf", "c1")
+        nc.vector.tensor_copy(
+            wd_bf[:].rearrange("p i m j -> p m i j"), wd_raw[:].rearrange("p j (m i) -> p m i j", i=4)
+        )
+        make_u(2)
+        nc.vector.quantize_mx(
+            out=wd_q[:].bitcast(FP8X4), scales=wd_sc[:], in_=wd_bf[:].rearrange("p i m j -> p (i m j)")
+        )
+        make_u(3)
+        h_bf = turn(0)
+        relu_neg(ru_sb[1][:], u_sb[1][:])
+        nc.vector.tensor_tensor(m_sb[1][:], u_sb[1][:], d_sb[1][:], ALU.max)
+        quantise_h(0, h_bf)
+        make_d(4)
+        make_d(5)
+        place([piece(0, 0), piece(1, 0)], "y", "yab0")
+        relu_neg(rd_sb[2][:], d_sb[2][:])
+        make_u(4)
+        make_u(5)
+        h_bf = turn(1)
+        relu_neg(ru_sb[2][:], u_sb[2][:])
+        nc.vector.tensor_tensor(m_sb[2][:], u_sb[2][:], d_sb[2][:], ALU.max)
+        quantise_h(1, h_bf)
+        place([piece(2, 0)], "y", "ru1")
+        place([piece(0, 1), piece(1, 1)], "y", "yab1")
+        paired(6)
+        h_bf = turn(2)
+        paired(7)
+        quantise_h(2, h_bf)
+        place([piece(2, 1)], "y", "ru2")
+        place([piece(0, 2)], "y", "yab0")
+        h_bf = turn(3)
+        quantise_h(3, h_bf)
+        place([piece(2, 2)], "y", "ru3")
+        place([piece(0, 3)], "y", "yab1")
+        nc.sync.dma_start(rows[0], pages[0][:])
+        place([piece(1, 2, 3)], "a", "yb23")
+        nc.sync.dma_start(rows[1], pages[1][:])
+        place([piece(2, 3)], "y", "yc3")
+        nc.sync.dma_start(rows[2], pages[2][:])
+        y_last = held([P, S], F32, "y_last")
+        for n in range(2):
+            y_ps = psum.tile([P, HALF], F32, name="y_ps", tag="b")
+            marks(3, HALF * n, HALF * (n + 1), y_ps[:], None)
+            shift(3, y_ps[:], y_last[:, HALF * n : HALF * (n + 1)])
+        scatter(3, 0, S, y_last[:])
+        nc.sync.dma_start(rows[3], pages[3][:])

@@ -57,35 +57,39 @@ def tile_list_skill_disagreement_marks_kernel(
         tab_sc = held([P, T], U8, "tab_sc")
         planes = [held([P, S + 2 * H], U8, "plane%d" % a) for a in range(2)]
         staged = held([P, S + 2 * H], U8, "staged")
-        nc.gpsimd.memset(staged[:, S : S + H].bitcast(I32), 0)
         nc.gpsimd.memset(tab_sc[:].bitcast(I32), 0)
+        nc.gpsimd.memset(staged[:, S : S + H].bitcast(I32), 0)
         nc.gpsimd.memset(staged[:, S + H :].bitcast(I32), 0)
-        nc.gpsimd.memset(planes[1][:].bitcast(I32), 0)
+        nc.vector.memset(planes[0][:].bitcast(I32), 0)
 
         nc.sync.dma_start(offs_sb[:], offs)
 
-        def load_scale_rows(dst, src):
+        nc.sync.dma_start(offs2_sb[:], offs2)
+
+        def load_scale_rows(dst, src, parts=range(3)):
             rows = src.bitcast(I32)
-            for r in range(2):
-                nc.sync.dma_start(dst[r:P:16, :].bitcast(I32), rows[0].rearrange("(g r) t -> r g t", r=2)[r])
-            nc.sync.dma_start(dst[4:P:8, :].bitcast(I32), rows[1])
+            for r in parts:
+                if r < 2:
+                    nc.sync.dma_start(dst[r:P:16, :].bitcast(I32), rows[1].rearrange("(g r) t -> r g t", r=2)[r])
+                else:
+                    nc.sync.dma_start(dst[4:P:8, :].bitcast(I32), rows[0])
 
         tab_w = [placed([P, T], I32, "tab_w%d" % a, (AT_TAB0, AT_TAB1)[a]) for a in range(2)]
         wb_rows = wb.rearrange("(a p j) c -> a p j c", a=2, j=4)
         wb_raw = [held([P, 4, H], F32, "wb_raw0"), placed([P, 4, H], F32, "wb_raw1", AT_WB1)]
-        wc_sb = held([P, 2, H], I32, "wc_sb")
-        wa_sb = held([P, 2, 2 * H], U8, "wa_sb")
 
         def load_words(a):
             nc.sync.dma_start(tab_w[a][:], tab_words[a].rearrange("p t i -> p (t i)").bitcast(I32))
 
-        load_scale_rows(staged[:, S : S + H], wc_scales)
         load_scale_rows(tab_sc, tab_scales)
+        load_scale_rows(staged[:, S : S + H], wc_scales, range(2))
         load_words(0)
-        nc.sync.dma_start(wc_sb[:], wc_words.rearrange("a p e i -> p a (e i)").bitcast(I32))
-        nc.sync.dma_start(wa_sb[:].bitcast(I32), wa_words.rearrange("a p n -> p a n").bitcast(I32))
+        load_scale_rows(staged[:, S : S + H], wc_scales, [2])
         load_scale_rows(staged[:, S + H :], wa_scales)
-        nc.sync.dma_start(offs2_sb[:], offs2)
+        wc_sb = held([P, 2, H], I32, "wc_sb")
+        nc.sync.dma_start(wc_sb[:], wc_words.rearrange("a p e i -> p a (e i)").bitcast(I32))
+        wa_sb = held([P, 2, 2 * H], U8, "wa_sb")
+        nc.sync.dma_start(wa_sb[:].bitcast(I32), wa_words.rearrange("a p n -> p a n").bitcast(I32))
         load_words(1)
         nc.sync.dma_start(wb_raw[0][:], wb_rows[0])
 
@@ -99,12 +103,11 @@ def tile_list_skill_disagreement_marks_kernel(
         gathered_sc = held([P, S], U8, "gathered_sc")
         nc.vector.tensor_copy(gathered_sc[:], tab_sc[:].indirect(offs_sb[:]))
         nc.vector.tensor_copy(staged[:, :S].bitcast(I32), gathered_sc[:].bitcast(I32))
-        nc.vector.tensor_copy(planes[0][:, :S].bitcast(I32), gathered_sc[:].bitcast(I32))
-        nc.gpsimd.tensor_copy(planes[0][:, S:].bitcast(I32), staged[:, S:].bitcast(I32))
-        for r in range(2):
-            nc.scalar.dma_start(planes[0][2 + r : P : 32, :].bitcast(I32), staged[16 + r : P : 32, :].bitcast(I32))
         for r in range(4):
-            nc.scalar.dma_start(planes[1][r:P:32, :].bitcast(I32), staged[8 * r + 4 : P : 32, :].bitcast(I32))
+            nc.scalar.dma_start(planes[0][r:P:32, :].bitcast(I32), staged[8 * r + 4 : P : 32, :].bitcast(I32))
+        nc.vector.tensor_copy(planes[1][:].bitcast(I32), staged[:].bitcast(I32))
+        for r in range(2):
+            nc.scalar.dma_start(planes[1][2 + r : P : 32, :].bitcast(I32), staged[16 + r : P : 32, :].bitcast(I32))
 
         picked_words = [held([P, S], U32, "picked_words%d" % a) for a in range(2)]
         nc.vector.tensor_copy(picked_words[0][:], tab_w[0][:].bitcast(U32).indirect(offs_sb[:]))
@@ -117,8 +120,8 @@ def tile_list_skill_disagreement_marks_kernel(
 
         def walk(a):
             return (
-                neg_wb_bf[a][:].rearrange("p (c i j) -> p c j i", i=4, j=4),
-                wb_raw[a][:].rearrange("p j (c i) -> p c j i", i=4),
+                neg_wb_bf[a][:].rearrange("p (c j) -> p c j", j=4),
+                wb_raw[a][:].rearrange("p j c -> p c j"),
             )
 
         def quantise_wb(a):

@@ -24,6 +24,7 @@ PAIR = 2 * P
 PAIRS = TILES // 2
 PLAIN = TILES - 2
 AHEAD = 4
+BANKS = {"a": 2, "b": 2, "h": 2, "y0": 1, "y1": 1}
 
 PAGE = 4 * T2
 AT_PAGE2 = 0
@@ -141,7 +142,7 @@ def tile_list_skill_disagreement_marks_kernel(
         nc.vector.tensor_scalar(*walk(0), -1.0, 0.0, ALU.mult, ALU.add)
 
         def product(k, bank, *weights):
-            acc = psum.tile([P, H], F32, name="acc", tag=bank)
+            acc = psum.tile([P, H], F32, name="acc", tag=bank, bufs=BANKS[bank])
             passes = [(a, codes[a], scales[a]) for codes, scales in weights for a in range(2)]
             for n, (a, rhs, rhs_sc) in enumerate(passes):
                 nc.tensor.matmul_mx(
@@ -162,8 +163,10 @@ def tile_list_skill_disagreement_marks_kernel(
         def terms(name, tags):
             return [held([P, 2 * H], F32, "%s%d" % (name, n), "%s%d" % (name, n % tags)) for n in range(PAIRS)]
 
-        u_sb, m_sb, rd_sb, ru_sb = terms("u", 2), terms("m", 2), terms("rd", 2), terms("ru", 4)
+        u_sb, rd_sb, ru_sb = terms("u", 4), terms("rd", 2), terms("ru", 4)
+        m_sb = terms("m", 4)
         d_sb = [placed([P, 2 * H], F32, "d%d" % n, (AT_WB1 + 64, AT_WB_BF1)[n % 2]) for n in range(PAIRS)]
+        d_sb[2] = held([P, 2 * H], F32, "d2")
         c_sb = {}
 
         def half(term, k):
@@ -178,7 +181,7 @@ def tile_list_skill_disagreement_marks_kernel(
         def make_d(k):
             c_sb[k] = held([P, H], F32, "c%d" % k)
             nc.scalar.copy(slots(c_sb[k][:]), product(k, "h" if k < AHEAD else "a", wc_mx))
-            a_ps = product(k, "y" if k == 2 else "a", wa_mx)
+            a_ps = product(k, "y0" if k == 2 else "a", wa_mx)
             nc.vector.tensor_tensor(slots(half(d_sb, k)), slots(c_sb[k][:]), a_ps, ALU.subtract)
 
         def make_u(k):
@@ -195,9 +198,10 @@ def tile_list_skill_disagreement_marks_kernel(
         h_q = held([P, S], U32, "h_q")
         h_sc = held([P, S], U8, "h_sc")
 
-        def turn(n):
-            h_bf = held([P, 4 * PAIR], BF16, "h_bf%d" % n, "h_bf%d" % (n % 2))
-            for k in (2 * n, 2 * n + 1):
+        h_bf = [held([P, 4 * PAIR], BF16, "h_bf%d" % n) for n in range(PAIRS)]
+
+        def turn(*tiles):
+            for k in tiles:
                 h_ps = psum.tile([P, 4, P], F32, name="h_ps", tag="h")
                 for t in range(4):
                     for e, term in enumerate((rd_sb, m_sb, ru_sb)):
@@ -206,16 +210,14 @@ def tile_list_skill_disagreement_marks_kernel(
                             start=(e == 0), stop=(e == 2), is_transpose=True,
                         )
                 nc.scalar.copy(
-                    h_bf[:, H * (k % 2) : H * (k % 2 + 1)].rearrange("p (j t) -> p j t", t=4),
-                    h_ps[:].rearrange("p t j -> p j t"),
+                    half(h_bf, k).rearrange("p (j t) -> p j t", t=4), h_ps[:].rearrange("p t j -> p j t")
                 )
-            return h_bf
 
-        def quantise_h(n, h_bf):
+        def quantise_h(n):
             nc.vector.quantize_mx(
                 out=h_q[:, PAIR * n : PAIR * (n + 1)].bitcast(FP8X4),
                 scales=h_sc[:, PAIR * n : PAIR * (n + 1)],
-                in_=h_bf[:],
+                in_=h_bf[n][:],
             )
 
         wd_q = held([P, N], U32, "wd_q")
@@ -240,17 +242,24 @@ def tile_list_skill_disagreement_marks_kernel(
                 pages[i][:].indirect(offs2_sb[:, j0 // 16 : j1 // 16]), y_sb, wgo_sb[:, j0:j1], ALU.mult
             )
 
-        def place(pieces, bank, tag):
+        def multiply(pieces, bank):
             widths = [j1 - j0 for i, j0, j1 in pieces]
             cols = [slice(sum(widths[:n]), sum(widths[: n + 1])) for n in range(len(pieces))]
-            y_ps = psum.tile([P, sum(widths)], F32, name="y_ps", tag=bank)
-            y_sb = held([P, sum(widths)], F32, "y_sb", tag)
+            y_ps = psum.tile([P, sum(widths)], F32, name="y_ps", tag=bank, bufs=BANKS[bank])
             for col, (i, j0, j1) in zip(cols, pieces):
-                marks(i, j0, j1, y_ps[:, col], y_sb[:, col])
+                marks(i, j0, j1, y_ps[:, col], None)
+            return y_ps, cols, pieces
+
+        def put(made, tag):
+            y_ps, cols, pieces = made
+            y_sb = held([P, cols[-1].stop], F32, "y_sb", tag)
             for col, (i, j0, j1) in zip(cols, pieces):
                 shift(i, y_ps[:, col], y_sb[:, col])
             for col, (i, j0, j1) in zip(cols, pieces):
                 scatter(i, j0, j1, y_sb[:, col])
+
+        def place(pieces, bank, tag):
+            put(multiply(pieces, bank), tag)
 
         def piece(i, n, n1=None):
             return (i, PAIR * n, PAIR * ((n if n1 is None else n1) + 1))
@@ -282,36 +291,40 @@ def tile_list_skill_disagreement_marks_kernel(
             out=wd_q[:].bitcast(FP8X4), scales=wd_sc[:], in_=wd_bf[:].rearrange("p i m j -> p (i m j)")
         )
         make_u(3)
-        h_bf = turn(0)
+        turn(0, 1)
         relu_neg(ru_sb[1][:], u_sb[1][:])
         nc.vector.tensor_tensor(m_sb[1][:], u_sb[1][:], d_sb[1][:], ALU.max)
-        quantise_h(0, h_bf)
+        quantise_h(0)
         make_d(4)
         make_d(5)
-        place([piece(0, 0), piece(1, 0)], "y", "yab0")
+        place([piece(0, 0), piece(1, 0)], "y0", "yab0")
+        late = multiply([piece(2, 0)], "y1")
         relu_neg(rd_sb[2][:], d_sb[2][:])
         make_u(4)
         make_u(5)
-        h_bf = turn(1)
+        turn(2, 3)
         relu_neg(ru_sb[2][:], u_sb[2][:])
         nc.vector.tensor_tensor(m_sb[2][:], u_sb[2][:], d_sb[2][:], ALU.max)
-        quantise_h(1, h_bf)
-        place([piece(2, 0)], "y", "ru1")
-        place([piece(0, 1), piece(1, 1)], "y", "yab1")
+        quantise_h(1)
+        put(late, "ru1")
         paired(6)
-        h_bf = turn(2)
         paired(7)
-        quantise_h(2, h_bf)
-        place([piece(2, 1)], "y", "ru2")
-        place([piece(0, 2)], "y", "yab0")
-        h_bf = turn(3)
-        quantise_h(3, h_bf)
-        place([piece(2, 2)], "y", "ru3")
-        place([piece(0, 3)], "y", "yab1")
+        place([piece(0, 1), piece(1, 1)], "y1", "yab1")
+        late = multiply([piece(2, 1)], "y0")
+        turn(4, 5)
+        quantise_h(2)
+        put(late, "ru2")
+        turn(6)
+        place([piece(0, 2)], "y1", "yab0")
+        late = multiply([piece(2, 2)], "y0")
+        turn(7)
+        quantise_h(3)
+        put(late, "ru3")
+        place([piece(0, 3)], "y1", "yab1")
         nc.sync.dma_start(rows[0], pages[0][:])
-        place([piece(1, 2, 3)], "a", "yb23")
+        place([piece(1, 2, 3)], "y0", "yb23")
         nc.sync.dma_start(rows[1], pages[1][:])
-        place([piece(2, 3)], "y", "yc3")
+        place([piece(2, 3)], "y1", "yc3")
         nc.sync.dma_start(rows[2], pages[2][:])
         y_last = held([P, S], F32, "y_last")
         for n in range(2):

@@ -35,6 +35,8 @@ AT_USUAL = AT_TAB1 + 64
 AT_WD = AT_USUAL + 64
 AT_WGO = AT_USUAL - 4 * S
 AT_WB_BF1 = AT_WD + 16 * N
+AT_WB_BF0 = AT_WB_BF1 + 8 * H
+AT_PAGE3 = AT_WB_BF0 + 8 * H - 64
 
 
 def tile_list_skill_disagreement_marks_kernel(
@@ -95,7 +97,7 @@ def tile_list_skill_disagreement_marks_kernel(
         nc.sync.dma_start(wb_raw[0][:], wb_rows[0])
 
         pages = [held([P, T2], F32, "page0"), held([P, T2], F32, "page1"), placed([P, T2], F32, "page2", AT_PAGE2)]
-        pages.append(pages[0])
+        pages.append(placed([P, T2], F32, "page3", AT_PAGE3))
         ident = held([P, P], F32, "ident")
         make_identity(nc, ident[:])
         for i in range(2):
@@ -115,7 +117,7 @@ def tile_list_skill_disagreement_marks_kernel(
         nc.sync.dma_start(wb_raw[1][:], wb_rows[1])
         nc.vector.memset(pages[2][:].bitcast(I32), 0)
 
-        neg_wb_bf = [held([P, 4 * H], BF16, "neg_wb_bf0"), placed([P, 4 * H], BF16, "neg_wb_bf1", AT_WB_BF1)]
+        neg_wb_bf = [placed([P, 4 * H], BF16, "neg_wb_bf0", AT_WB_BF0), placed([P, 4 * H], BF16, "neg_wb_bf1", AT_WB_BF1)]
         neg_wb_q = [held([P, H], U32, "neg_wb_q%d" % a) for a in range(2)]
         neg_wb_sc = [held([P, H], U8, "neg_wb_sc%d" % a) for a in range(2)]
 
@@ -269,6 +271,7 @@ def tile_list_skill_disagreement_marks_kernel(
         nc.vector.tensor_scalar(*walk(1), -1.0, 0.0, ALU.mult, ALU.add)
         quantise_wb(0)
         quantise_wb(1)
+        nc.vector.memset(pages[3][:].bitcast(I32), 0)
         make_d(0)
         make_d(1)
         relu_neg(rd_sb[0][:], d_sb[0][:])
@@ -298,7 +301,7 @@ def tile_list_skill_disagreement_marks_kernel(
         make_d(4)
         make_d(5)
         place([piece(0, 0), piece(1, 0)], "y0", "yab0")
-        late = multiply([piece(2, 0)], "y1")
+        late = multiply([piece(2, 0), piece(3, 0)], "y1")
         relu_neg(rd_sb[2][:], d_sb[2][:])
         make_u(4)
         make_u(5)
@@ -310,26 +313,18 @@ def tile_list_skill_disagreement_marks_kernel(
         paired(6)
         paired(7)
         place([piece(0, 1), piece(1, 1)], "y1", "yab1")
-        late = multiply([piece(2, 1)], "y0")
+        late = multiply([piece(2, 1), piece(3, 1)], "y0")
         turn(4, 5)
         quantise_h(2)
         put(late, "ru2")
         turn(6)
-        place([piece(0, 2)], "y1", "yab0")
+        place([piece(0, 2), piece(1, 2)], "y1", "yab0")
         late = multiply([piece(2, 2)], "y0")
         turn(7)
         quantise_h(3)
         put(late, "ru3")
-        place([piece(0, 3)], "y1", "yab1")
-        nc.sync.dma_start(rows[0], pages[0][:])
-        place([piece(1, 2, 3)], "y0", "yb23")
-        nc.sync.dma_start(rows[1], pages[1][:])
-        place([piece(2, 3)], "y1", "yc3")
-        nc.sync.dma_start(rows[2], pages[2][:])
-        y_last = held([P, S], F32, "y_last")
-        for n in range(2):
-            y_ps = psum.tile([P, HALF], F32, name="y_ps", tag="b")
-            marks(3, HALF * n, HALF * (n + 1), y_ps[:], None)
-            shift(3, y_ps[:], y_last[:, HALF * n : HALF * (n + 1)])
-        scatter(3, 0, S, y_last[:])
-        nc.sync.dma_start(rows[3], pages[3][:])
+        place([piece(0, 3), piece(1, 3)], "y1", "yab1")
+        place([piece(2, 3)], "y0", "yc3")
+        place([piece(3, 2, 3)], "y1", "yd23")
+        for i in range(4):
+            nc.sync.dma_start(rows[i], pages[i][:])

@@ -24,12 +24,14 @@ PAIR = 2 * P
 PAIRS = TILES // 2
 PLAIN = TILES - 2
 AHEAD = 4
+SCALAR_COLS = 160
 BANKS = {"a": 2, "b": 2, "h": 2, "y0": 1, "y1": 1}
 
 PAGE = 4 * T2
 AT_PAGE2 = 0
-AT_TAB0 = PAGE - 64
-AT_WB1 = PAGE
+AT_GATHERED = PAGE - 64
+AT_TAB0 = AT_GATHERED + S
+AT_WB1 = AT_TAB0
 AT_TAB1 = AT_WB1 + 16 * H + 4 * S
 AT_USUAL = AT_TAB1 + 64
 AT_WD = AT_USUAL + 64
@@ -37,6 +39,7 @@ AT_WGO = AT_USUAL - 4 * S
 AT_WB_BF1 = AT_WD + 16 * N
 AT_WB_BF0 = AT_WB_BF1 + 8 * H
 AT_PAGE3 = AT_WB_BF0 + 8 * H - 64
+AT_W_ROWS = AT_PAGE3 + PAGE
 
 
 def tile_list_skill_disagreement_marks_kernel(
@@ -61,8 +64,8 @@ def tile_list_skill_disagreement_marks_kernel(
         planes = [held([P, S + 2 * H], U8, "plane%d" % a) for a in range(2)]
         staged = held([P, S + 2 * H], U8, "staged")
         nc.gpsimd.memset(tab_sc[:].bitcast(I32), 0)
-        nc.gpsimd.memset(staged[:, S : S + H].bitcast(I32), 0)
-        nc.gpsimd.memset(staged[:, S + H :].bitcast(I32), 0)
+        w_rows = placed([P, 2 * H], U8, "w_rows", AT_W_ROWS)
+        nc.gpsimd.memset(w_rows[:].bitcast(I32), 0)
         nc.vector.memset(planes[0][:].bitcast(I32), 0)
 
         nc.sync.dma_start(offs_sb[:], offs)
@@ -85,10 +88,10 @@ def tile_list_skill_disagreement_marks_kernel(
             nc.sync.dma_start(tab_w[a][:], tab_words[a].rearrange("p t i -> p (t i)").bitcast(I32))
 
         load_scale_rows(tab_sc, tab_scales)
-        load_scale_rows(staged[:, S : S + H], wc_scales, range(2))
+        load_scale_rows(w_rows[:, :H], wc_scales, range(2))
         load_words(0)
-        load_scale_rows(staged[:, S : S + H], wc_scales, [2])
-        load_scale_rows(staged[:, S + H :], wa_scales)
+        load_scale_rows(w_rows[:, :H], wc_scales, [2])
+        load_scale_rows(w_rows[:, H:], wa_scales)
         wc_sb = held([P, 2, H], I32, "wc_sb")
         nc.sync.dma_start(wc_sb[:], wc_words.rearrange("a p e i -> p a (e i)").bitcast(I32))
         wa_sb = held([P, 2, 2 * H], U8, "wa_sb")
@@ -103,8 +106,9 @@ def tile_list_skill_disagreement_marks_kernel(
         for i in range(2):
             nc.vector.memset(pages[i][:].bitcast(I32), 0)
 
-        gathered_sc = held([P, S], U8, "gathered_sc")
+        gathered_sc = placed([P, S], U8, "gathered_sc", AT_GATHERED)
         nc.vector.tensor_copy(gathered_sc[:], tab_sc[:].indirect(offs_sb[:]))
+        nc.vector.tensor_copy(staged[:, S:].bitcast(I32), w_rows[:].bitcast(I32))
         nc.vector.tensor_copy(staged[:, :S].bitcast(I32), gathered_sc[:].bitcast(I32))
         for r in range(4):
             nc.scalar.dma_start(planes[0][r:P:32, :].bitcast(I32), staged[8 * r + 4 : P : 32, :].bitcast(I32))
@@ -112,7 +116,7 @@ def tile_list_skill_disagreement_marks_kernel(
         for r in range(2):
             nc.scalar.dma_start(planes[1][2 + r : P : 32, :].bitcast(I32), staged[16 + r : P : 32, :].bitcast(I32))
 
-        picked_words = [held([P, S], U32, "picked_words%d" % a) for a in range(2)]
+        picked_words = [placed([P, S], U32, "picked_words0", AT_W_ROWS), held([P, S], U32, "picked_words1")]
         nc.vector.tensor_copy(picked_words[0][:], tab_w[0][:].bitcast(U32).indirect(offs_sb[:]))
         nc.sync.dma_start(wb_raw[1][:], wb_rows[1])
         nc.vector.memset(pages[2][:].bitcast(I32), 0)
@@ -121,10 +125,10 @@ def tile_list_skill_disagreement_marks_kernel(
         neg_wb_q = [held([P, H], U32, "neg_wb_q%d" % a) for a in range(2)]
         neg_wb_sc = [held([P, H], U8, "neg_wb_sc%d" % a) for a in range(2)]
 
-        def walk(a):
+        def walk(a, c0=0, c1=H):
             return (
-                neg_wb_bf[a][:].rearrange("p (c j) -> p c j", j=4),
-                wb_raw[a][:].rearrange("p j c -> p c j"),
+                neg_wb_bf[a][:, 4 * c0 : 4 * c1].rearrange("p (c j) -> p c j", j=4),
+                wb_raw[a][:, :, c0:c1].rearrange("p j c -> p c j"),
             )
 
         def quantise_wb(a):
@@ -168,6 +172,7 @@ def tile_list_skill_disagreement_marks_kernel(
         u_sb, rd_sb, ru_sb = terms("u", 4), terms("rd", 2), terms("ru", 4)
         m_sb = terms("m", 4)
         d_sb = [placed([P, 2 * H], F32, "d%d" % n, (AT_WB1 + 64, AT_WB_BF1)[n % 2]) for n in range(PAIRS)]
+        d_sb[0] = held([P, 2 * H], F32, "d0")
         d_sb[2] = held([P, 2 * H], F32, "d2")
         c_sb = {}
 
@@ -268,7 +273,8 @@ def tile_list_skill_disagreement_marks_kernel(
 
         rows = out.rearrange("(p i) t -> i p t", i=4)
 
-        nc.vector.tensor_scalar(*walk(1), -1.0, 0.0, ALU.mult, ALU.add)
+        nc.scalar.activation(*walk(1, 0, SCALAR_COLS), ACT.Copy, scale=-1.0)
+        nc.vector.tensor_scalar(*walk(1, SCALAR_COLS, H), -1.0, 0.0, ALU.mult, ALU.add)
         quantise_wb(0)
         quantise_wb(1)
         nc.vector.memset(pages[3][:].bitcast(I32), 0)

@@ -30,13 +30,13 @@ BANKS = {"a": 2, "b": 2, "h": 2, "y0": 1, "y1": 1}
 PAGE = 4 * T2
 AT_PAGE2 = 0
 AT_GATHERED = PAGE - 64
-AT_TAB0 = AT_GATHERED + S
-AT_WB1 = AT_TAB0
-AT_TAB1 = AT_WB1 + 16 * H + 4 * S
-AT_USUAL = AT_TAB1 + 64
-AT_WD = AT_USUAL + 64
-AT_WGO = AT_USUAL - 4 * S
-AT_WB_BF1 = AT_WD + 16 * N
+AT_WD = AT_GATHERED + S
+AT_TAB0 = AT_WD + 16 * N - 64
+AT_USUAL = AT_TAB0 + 64
+AT_WGO = AT_USUAL + 64
+AT_WB1 = AT_TAB0 + 4 * T - 64
+AT_TAB1 = AT_WB1 + 16 * H
+AT_WB_BF1 = AT_TAB1 + 4 * T
 AT_WB_BF0 = AT_WB_BF1 + 8 * H
 AT_PAGE3 = AT_WB_BF0 + 8 * H - 64
 AT_W_ROWS = AT_PAGE3 + PAGE
@@ -139,12 +139,12 @@ def tile_list_skill_disagreement_marks_kernel(
                 picked_words[1][:, HALF * half : HALF * (half + 1)],
                 tab_w[1][:].bitcast(U32).indirect(offs_sb[:, HALF // 16 * half : HALF // 16 * (half + 1)]),
             )
+        usual_sb = placed([P, 4], F32, "usual_sb", AT_USUAL)
+        nc.sync.dma_start(usual_sb[:], usual.rearrange("(p i) -> p i", i=4))
         wd_raw = placed([P, 4, N], F32, "wd_raw", AT_WD)
         nc.sync.dma_start(wd_raw[:], wd.rearrange("(p j) c -> p j c", j=4))
         wgo_sb = placed([P, S], F32, "wgo_sb", AT_WGO)
         nc.sync.dma_start(wgo_sb[:], wgo)
-        usual_sb = placed([P, 4], F32, "usual_sb", AT_USUAL)
-        nc.sync.dma_start(usual_sb[:], usual.rearrange("(p i) -> p i", i=4))
         nc.vector.tensor_scalar(*walk(0), -1.0, 0.0, ALU.mult, ALU.add)
 
         def product(k, bank, *weights):
@@ -288,10 +288,8 @@ def tile_list_skill_disagreement_marks_kernel(
             relu_neg(half(ru_sb, k), half(u_sb, k))
         for k in range(2):
             nc.vector.tensor_tensor(half(m_sb, k), half(u_sb, k), half(d_sb, k), ALU.max)
-        neg_usual = held([P, 4], F32, "neg_usual", "c0")
-        nc.scalar.activation(neg_usual[:], usual_sb[:], ACT.Identity, scale=-1.0)
         relu_neg(rd_sb[1][:], d_sb[1][:])
-        wd_bf = held([P, 4, P, 4], BF16, "wd_bf", "c1")
+        wd_bf = held([P, 4, P, 4], BF16, "wd_bf", "u0")
         nc.vector.tensor_copy(
             wd_bf[:].rearrange("p i m j -> p m i j"), wd_raw[:].rearrange("p j (m i) -> p m i j", i=4)
         )
@@ -299,6 +297,8 @@ def tile_list_skill_disagreement_marks_kernel(
         nc.vector.quantize_mx(
             out=wd_q[:].bitcast(FP8X4), scales=wd_sc[:], in_=wd_bf[:].rearrange("p i m j -> p (i m j)")
         )
+        neg_usual = held([P, 4], F32, "neg_usual", "u0")
+        nc.scalar.activation(neg_usual[:], usual_sb[:], ACT.Identity, scale=-1.0)
         make_u(3)
         turn(0, 1)
         relu_neg(ru_sb[1][:], u_sb[1][:])

@@ -37,9 +37,7 @@ AT_WGO = AT_USUAL + 64
 AT_WB1 = AT_TAB0 + 4 * T - 64
 AT_TAB1 = AT_WB1 + 16 * H
 AT_WB_BF1 = AT_TAB1 + 4 * T
-AT_WB_BF0 = AT_WB_BF1 + 8 * H
-AT_PAGE3 = AT_WB_BF0 + 8 * H - 64
-AT_W_ROWS = AT_PAGE3 + PAGE
+AT_W_ROWS = AT_WB_BF1 + 8 * H
 
 
 def tile_list_skill_disagreement_marks_kernel(
@@ -100,7 +98,7 @@ def tile_list_skill_disagreement_marks_kernel(
         nc.sync.dma_start(wb_raw[0][:], wb_rows[0])
 
         pages = [held([P, T2], F32, "page0"), held([P, T2], F32, "page1"), placed([P, T2], F32, "page2", AT_PAGE2)]
-        pages.append(placed([P, T2], F32, "page3", AT_PAGE3))
+        pages.append(pages[0])
         ident = held([P, P], F32, "ident")
         make_identity(nc, ident[:])
         for i in range(2):
@@ -121,7 +119,7 @@ def tile_list_skill_disagreement_marks_kernel(
         nc.sync.dma_start(wb_raw[1][:], wb_rows[1])
         nc.vector.memset(pages[2][:].bitcast(I32), 0)
 
-        neg_wb_bf = [placed([P, 4 * H], BF16, "neg_wb_bf0", AT_WB_BF0), placed([P, 4 * H], BF16, "neg_wb_bf1", AT_WB_BF1)]
+        neg_wb_bf = [held([P, 4 * H], BF16, "neg_wb_bf0"), placed([P, 4 * H], BF16, "neg_wb_bf1", AT_WB_BF1)]
         neg_wb_q = [held([P, H], U32, "neg_wb_q%d" % a) for a in range(2)]
         neg_wb_sc = [held([P, H], U8, "neg_wb_sc%d" % a) for a in range(2)]
 
@@ -277,7 +275,6 @@ def tile_list_skill_disagreement_marks_kernel(
         nc.vector.tensor_scalar(*walk(1, SCALAR_COLS, H), -1.0, 0.0, ALU.mult, ALU.add)
         quantise_wb(0)
         quantise_wb(1)
-        nc.vector.memset(pages[3][:].bitcast(I32), 0)
         make_d(0)
         make_d(1)
         relu_neg(rd_sb[0][:], d_sb[0][:])
@@ -307,7 +304,7 @@ def tile_list_skill_disagreement_marks_kernel(
         make_d(4)
         make_d(5)
         place([piece(0, 0), piece(1, 0)], "y0", "yab0")
-        late = multiply([piece(2, 0), piece(3, 0)], "y1")
+        late = multiply([piece(2, 0)], "y1")
         relu_neg(rd_sb[2][:], d_sb[2][:])
         make_u(4)
         make_u(5)
@@ -319,18 +316,26 @@ def tile_list_skill_disagreement_marks_kernel(
         paired(6)
         paired(7)
         place([piece(0, 1), piece(1, 1)], "y1", "yab1")
-        late = multiply([piece(2, 1), piece(3, 1)], "y0")
+        late = multiply([piece(2, 1)], "y0")
         turn(4, 5)
         quantise_h(2)
         put(late, "ru2")
         turn(6)
-        place([piece(0, 2), piece(1, 2)], "y1", "yab0")
+        place([piece(0, 2)], "y1", "yab0")
         late = multiply([piece(2, 2)], "y0")
         turn(7)
         quantise_h(3)
         put(late, "ru3")
-        place([piece(0, 3), piece(1, 3)], "y1", "yab1")
-        place([piece(2, 3)], "y0", "yc3")
-        place([piece(3, 2, 3)], "y1", "yd23")
-        for i in range(4):
-            nc.sync.dma_start(rows[i], pages[i][:])
+        place([piece(0, 3)], "y1", "yab1")
+        nc.sync.dma_start(rows[0], pages[0][:])
+        place([piece(1, 2, 3)], "y0", "yb23")
+        nc.sync.dma_start(rows[1], pages[1][:])
+        place([piece(2, 3)], "y1", "yc3")
+        nc.sync.dma_start(rows[2], pages[2][:])
+        y_last = held([P, S], F32, "y_last")
+        for n in range(2):
+            y_ps = psum.tile([P, HALF], F32, name="y_ps", tag="b")
+            marks(3, HALF * n, HALF * (n + 1), y_ps[:], None)
+            shift(3, y_ps[:], y_last[:, HALF * n : HALF * (n + 1)])
+        scatter(3, 0, S, y_last[:])
+        nc.sync.dma_start(rows[3], pages[3][:])

@@ -20,24 +20,22 @@ ACT = mybir.ActivationFunctionType
 P = 128
 TILES = S // P
 HALF = S // 2
-PAIR = 2 * P
-PAIRS = TILES // 2
-PLAIN = TILES - 2
-AHEAD = 4
-SCALAR_COLS = 160
-BANKS = {"a": 2, "b": 2, "h": 2, "y0": 1, "y1": 1}
+PLAIN = 4
+TURNED = 6
+AHEAD = 3
+SCALAR_COLS = 224
+BANKS = {"mm": 4, "h": 2, "y": 2}
+DEPTH = 4
 
-PAGE = 4 * T2
-AT_PAGE2 = 0
-AT_GATHERED = PAGE - 64
-AT_WD = AT_GATHERED + S
-AT_TAB0 = AT_WD + 16 * N - 64
-AT_USUAL = AT_TAB0 + 64
-AT_WGO = AT_USUAL + 64
-AT_WB1 = AT_TAB0 + 4 * T - 64
-AT_TAB1 = AT_WB1 + 16 * H
-AT_WB_BF1 = AT_TAB1 + 4 * T
-AT_W_ROWS = AT_WB_BF1 + 8 * H
+AT_TAB1 = 0
+AT_GATHERED = AT_TAB1 + 4 * T - 64
+AT_WB1 = AT_GATHERED + S - 64
+AT_WD = AT_WB1 + 16 * H
+AT_STAGED = AT_WD + 16 * N - 64
+AT_WGO = AT_STAGED + S + 2 * H - 64
+AT_PAGE2 = AT_WGO + 4 * S
+AT_TAB0 = AT_PAGE2 + 2 * T2
+AT_PAGE3 = AT_PAGE2 + 4 * T2
 
 
 def tile_list_skill_disagreement_marks_kernel(
@@ -47,135 +45,160 @@ def tile_list_skill_disagreement_marks_kernel(
     with ExitStack() as ctx:
         lists = ctx.enter_context(tc.tile_pool(name="lists", bufs=1))
         keep = ctx.enter_context(tc.tile_pool(name="keep", bufs=1))
+        ring = ctx.enter_context(tc.tile_pool(name="ring", bufs=DEPTH))
         arena = ctx.enter_context(tc.tile_pool(name="arena", bufs=1))
         psum = ctx.enter_context(tc.psum_pool(name="psum", bufs=2))
 
         def placed(shape, dtype, name, offset):
             return arena.tile(shape, dtype, name=name, offset=offset, align_bytes=64)
 
-        def held(shape, dtype, name, tag=None):
-            return keep.tile(shape, dtype, name=name, tag=tag or name, align_bytes=64)
+        def held(shape, dtype, name):
+            return keep.tile(shape, dtype, name=name, align_bytes=64)
+
+        def term(name):
+            return ring.tile([P, H], F32, name=name, align_bytes=64)
 
         offs_sb = lists.tile([P, S // 16], U16, name="offs_sb")
         offs2_sb = lists.tile([P, S // 16], U16, name="offs2_sb")
         tab_sc = held([P, T], U8, "tab_sc")
         planes = [held([P, S + 2 * H], U8, "plane%d" % a) for a in range(2)]
-        staged = held([P, S + 2 * H], U8, "staged")
-        nc.gpsimd.memset(tab_sc[:].bitcast(I32), 0)
-        w_rows = placed([P, 2 * H], U8, "w_rows", AT_W_ROWS)
-        nc.gpsimd.memset(w_rows[:].bitcast(I32), 0)
-        nc.vector.memset(planes[0][:].bitcast(I32), 0)
+        nc.vector.memset(tab_sc[:].bitcast(I32), 0)
+        staged = placed([P, S + 2 * H], U8, "staged", AT_STAGED)
+        zero = held([P, 1], U32, "zero")
+        nc.vector.memset(zero[:], 0)
+        for plane in planes:
+            nc.scalar.copy(plane[:].bitcast(U32), zero[:].to_broadcast([P, (S + 2 * H) // 4]))
+
+        def load_scale_rows(dst, src):
+            nc.sync.dma_start(dst[0:P:4, :].bitcast(I32), src.bitcast(I32).rearrange("a q t -> q a t"))
 
         nc.sync.dma_start(offs_sb[:], offs)
-
+        load_scale_rows(staged[:, S : S + H], wc_scales)
+        load_scale_rows(staged[:, S + H :], wa_scales)
         nc.sync.dma_start(offs2_sb[:], offs2)
+        usual_sb = held([P, 4], F32, "usual_sb")
+        nc.sync.dma_start(usual_sb[:], usual.rearrange("(p i) -> p i", i=4))
+        load_scale_rows(tab_sc, tab_scales)
 
-        def load_scale_rows(dst, src, parts=range(3)):
-            rows = src.bitcast(I32)
-            for r in parts:
-                if r < 2:
-                    nc.sync.dma_start(dst[r:P:16, :].bitcast(I32), rows[1].rearrange("(g r) t -> r g t", r=2)[r])
-                else:
-                    nc.sync.dma_start(dst[4:P:8, :].bitcast(I32), rows[0])
-
-        tab_w = [placed([P, T], I32, "tab_w%d" % a, (AT_TAB0, AT_TAB1)[a]) for a in range(2)]
-        wb_rows = wb.rearrange("(a p j) c -> a p j c", a=2, j=4)
-        wb_raw = [held([P, 4, H], F32, "wb_raw0"), placed([P, 4, H], F32, "wb_raw1", AT_WB1)]
+        tab_w = [placed([P, T], I32, "tab_w0", AT_TAB0), placed([P, T], I32, "tab_w1", AT_TAB1)]
+        wb_rows = wb.rearrange("(a p j) c -> a p (j c)", a=2, j=4)
+        wb_raw0 = held([P, 4 * H], F32, "wb_raw0")
 
         def load_words(a):
             nc.sync.dma_start(tab_w[a][:], tab_words[a].rearrange("p t i -> p (t i)").bitcast(I32))
 
-        load_scale_rows(tab_sc, tab_scales)
-        load_scale_rows(w_rows[:, :H], wc_scales, range(2))
         load_words(0)
-        load_scale_rows(w_rows[:, :H], wc_scales, [2])
-        load_scale_rows(w_rows[:, H:], wa_scales)
+        nc.sync.dma_start(wb_raw0[:], wb_rows[0])
         wc_sb = held([P, 2, H], I32, "wc_sb")
         nc.sync.dma_start(wc_sb[:], wc_words.rearrange("a p e i -> p a (e i)").bitcast(I32))
-        wa_sb = held([P, 2, 2 * H], U8, "wa_sb")
-        nc.sync.dma_start(wa_sb[:].bitcast(I32), wa_words.rearrange("a p n -> p a n").bitcast(I32))
-        load_words(1)
-        nc.sync.dma_start(wb_raw[0][:], wb_rows[0])
+        wa_sb = held([P, 2, H // 2], I32, "wa_sb")
+        nc.sync.dma_start(wa_sb[:], wa_words.rearrange("a p n -> p a n").bitcast(I32))
 
-        pages = [held([P, T2], F32, "page0"), held([P, T2], F32, "page1"), placed([P, T2], F32, "page2", AT_PAGE2)]
-        pages.append(pages[0])
+        pages = [held([P, T2], F32, "page%d" % i) for i in range(2)]
         ident = held([P, P], F32, "ident")
         make_identity(nc, ident[:])
         for i in range(2):
             nc.vector.memset(pages[i][:].bitcast(I32), 0)
+        neg_usual = held([P, 4], F32, "neg_usual")
+        nc.scalar.activation(neg_usual[:], usual_sb[:], ACT.Identity, scale=-1.0)
 
         gathered_sc = placed([P, S], U8, "gathered_sc", AT_GATHERED)
         nc.vector.tensor_copy(gathered_sc[:], tab_sc[:].indirect(offs_sb[:]))
-        nc.vector.tensor_copy(staged[:, S:].bitcast(I32), w_rows[:].bitcast(I32))
         nc.vector.tensor_copy(staged[:, :S].bitcast(I32), gathered_sc[:].bitcast(I32))
-        for r in range(4):
-            nc.scalar.dma_start(planes[0][r:P:32, :].bitcast(I32), staged[8 * r + 4 : P : 32, :].bitcast(I32))
-        nc.vector.tensor_copy(planes[1][:].bitcast(I32), staged[:].bitcast(I32))
-        for r in range(2):
-            nc.scalar.dma_start(planes[1][2 + r : P : 32, :].bitcast(I32), staged[16 + r : P : 32, :].bitcast(I32))
 
-        picked_words = [placed([P, S], U32, "picked_words0", AT_W_ROWS), held([P, S], U32, "picked_words1")]
+        def move(a, r):
+            nc.sync.dma_start(planes[a][r:P:32, :].bitcast(I32), staged[8 * r + 4 * a : P : 32, :].bitcast(I32))
+
+        wb_raw1 = placed([P, 4 * H], F32, "wb_raw1", AT_WB1)[:]
+        wd_raw = placed([P, 4 * N], F32, "wd_raw", AT_WD)[:]
+        wgo_sb = placed([P, S], F32, "wgo_sb", AT_WGO)[:]
+        moves = [(a, r) for a in range(2) for r in range(4)]
+        for a, r in moves[:3]:
+            move(a, r)
+        load_words(1)
+        for a, r in moves[3:]:
+            move(a, r)
+        nc.sync.dma_start(wb_raw1, wb_rows[1])
+        nc.sync.dma_start(wd_raw, wd.rearrange("(p j) c -> p (j c)", j=4))
+        nc.sync.dma_start(wgo_sb, wgo)
+
+        picked_words = [held([P, S], U32, "picked_words%d" % a) for a in range(2)]
         nc.vector.tensor_copy(picked_words[0][:], tab_w[0][:].bitcast(U32).indirect(offs_sb[:]))
-        nc.sync.dma_start(wb_raw[1][:], wb_rows[1])
-        nc.vector.memset(pages[2][:].bitcast(I32), 0)
-
-        neg_wb_bf = [held([P, 4 * H], BF16, "neg_wb_bf0"), placed([P, 4 * H], BF16, "neg_wb_bf1", AT_WB_BF1)]
-        neg_wb_q = [held([P, H], U32, "neg_wb_q%d" % a) for a in range(2)]
-        neg_wb_sc = [held([P, H], U8, "neg_wb_sc%d" % a) for a in range(2)]
-
-        def walk(a, c0=0, c1=H):
-            return (
-                neg_wb_bf[a][:, 4 * c0 : 4 * c1].rearrange("p (c j) -> p c j", j=4),
-                wb_raw[a][:, :, c0:c1].rearrange("p j c -> p c j"),
-            )
-
-        def quantise_wb(a):
-            nc.vector.quantize_mx(out=neg_wb_q[a][:].bitcast(FP8X4), scales=neg_wb_sc[a][:], in_=neg_wb_bf[a][:])
-
+        for i, at in ((2, AT_PAGE2), (3, AT_PAGE3)):
+            pages.append(placed([P, T2], F32, "page%d" % i, at))
+            nc.vector.memset(pages[i][:].bitcast(I32), 0)
         for half in range(2):
             nc.vector.tensor_copy(
                 picked_words[1][:, HALF * half : HALF * (half + 1)],
                 tab_w[1][:].bitcast(U32).indirect(offs_sb[:, HALF // 16 * half : HALF // 16 * (half + 1)]),
             )
-        usual_sb = placed([P, 4], F32, "usual_sb", AT_USUAL)
-        nc.sync.dma_start(usual_sb[:], usual.rearrange("(p i) -> p i", i=4))
-        wd_raw = placed([P, 4, N], F32, "wd_raw", AT_WD)
-        nc.sync.dma_start(wd_raw[:], wd.rearrange("(p j) c -> p j c", j=4))
-        wgo_sb = placed([P, S], F32, "wgo_sb", AT_WGO)
-        nc.sync.dma_start(wgo_sb[:], wgo)
-        nc.vector.tensor_scalar(*walk(0), -1.0, 0.0, ALU.mult, ALU.add)
 
-        def product(k, bank, *weights):
-            acc = psum.tile([P, H], F32, name="acc", tag=bank, bufs=BANKS[bank])
-            passes = [(a, codes[a], scales[a]) for codes, scales in weights for a in range(2)]
-            for n, (a, rhs, rhs_sc) in enumerate(passes):
-                nc.tensor.matmul_mx(
-                    out=acc[:],
-                    lhsT=picked_words[a][:, P * k : P * (k + 1)].bitcast(FP8X4),
-                    lhsT_scale=planes[a][:, P * k : P * (k + 1)],
-                    rhs=rhs,
-                    rhs_scale=rhs_sc,
-                    start=(n == 0),
-                    stop=(n == len(passes) - 1),
-                )
+        wb_raw = [wb_raw0[:], wb_raw1]
+        neg_wb_bf = [held([P, 4 * H], BF16, "neg_wb_bf%d" % a) for a in range(2)]
+        neg_wb_q = [held([P, H], U32, "neg_wb_q%d" % a) for a in range(2)]
+        neg_wb_sc = [held([P, H], U8, "neg_wb_sc%d" % a) for a in range(2)]
+
+        def walk(a, c0, c1):
+            return (
+                neg_wb_bf[a][:, 4 * c0 : 4 * c1].rearrange("p (c j) -> p c j", j=4),
+                wb_raw[a].rearrange("p (j c) -> p c j", j=4)[:, c0:c1, :],
+            )
+
+        def quantise_wb(a):
+            nc.vector.quantize_mx(out=neg_wb_q[a][:].bitcast(FP8X4), scales=neg_wb_sc[a][:], in_=neg_wb_bf[a][:])
+
+        nc.scalar.activation(*walk(0, 0, H), ACT.Copy, scale=-1.0)
+        quantise_wb(0)
+
+        def wc_mx(a, c0=0, c1=H):
+            return wc_sb[:, a, c0:c1].bitcast(FP8X4), planes[a][:, S + c0 : S + c1]
+
+        def wa_mx(a, c0=0, c1=H):
+            return wa_sb[:, a, c0 // 2 : c1 // 2].bitcast(FP4X4), planes[a][:, S + H + c0 : S + H + c1]
+
+        def neg_wb_mx(a, c0=0, c1=H):
+            return neg_wb_q[a][:, c0:c1].bitcast(FP8X4), neg_wb_sc[a][:, c0:c1]
+
+        def picked_mx(a, k):
+            return picked_words[a][:, P * k : P * (k + 1)].bitcast(FP8X4), planes[a][:, P * k : P * (k + 1)]
+
+        def mx_pass(acc, stationary, moving, start, stop):
+            nc.tensor.matmul_mx(
+                out=acc, lhsT=stationary[0], lhsT_scale=stationary[1], rhs=moving[0], rhs_scale=moving[1],
+                start=start, stop=stop,
+            )
+
+        def bank_tile(bank):
+            return psum.tile([P, H], F32, name="acc", tag=bank, bufs=BANKS[bank])
+
+        def by_slot(acc):
             return acc[:].rearrange("p (m t) -> p t m", t=4)
 
-        wc_mx = ([wc_sb[:, a, :].bitcast(FP8X4) for a in range(2)], [sc[:, S : S + H] for sc in planes])
-        wa_mx = ([wa_sb[:, a, :].bitcast(FP4X4) for a in range(2)], [sc[:, S + H :] for sc in planes])
-        neg_wb_mx = ([q[:].bitcast(FP8X4) for q in neg_wb_q], [sc[:] for sc in neg_wb_sc])
+        def product(k, bank, *weights):
+            acc = bank_tile(bank)
+            passes = [(a, weight) for weight in weights for a in range(2)]
+            for n, (a, weight) in enumerate(passes):
+                mx_pass(acc[:], picked_mx(a, k), weight(a), n == 0, n == len(passes) - 1)
+            return by_slot(acc)
 
-        def terms(name, tags):
-            return [held([P, 2 * H], F32, "%s%d" % (name, n), "%s%d" % (name, n % tags)) for n in range(PAIRS)]
+        def product_by_rows(k, weight, name):
+            acc = bank_tile("mm")
+            for i in range(4):
+                for a in range(2):
+                    mx_pass(acc[:, P * i : P * (i + 1)], weight(a, P * i, P * (i + 1)), picked_mx(a, k), a == 0, a == 1)
+            rows_sb = term(name)
+            nc.scalar.copy(rows_sb[:], acc[:])
+            return rows_sb
 
-        u_sb, rd_sb, ru_sb = terms("u", 4), terms("rd", 2), terms("ru", 4)
-        m_sb = terms("m", 4)
-        d_sb = [placed([P, 2 * H], F32, "d%d" % n, (AT_WB1 + 64, AT_WB_BF1)[n % 2]) for n in range(PAIRS)]
-        d_sb[0] = held([P, 2 * H], F32, "d0")
-        d_sb[2] = held([P, 2 * H], F32, "d2")
-        c_sb = {}
-
-        def half(term, k):
-            return term[k // 2][:, H * (k % 2) : H * (k % 2 + 1)]
+        def turned_sum(first, second):
+            acc = bank_tile("mm")
+            for i in range(4):
+                for e, rows_sb in enumerate((first, second)):
+                    nc.tensor.matmul(
+                        acc[:, P * i : P * (i + 1)], rows_sb[:, P * i : P * (i + 1)], ident[:],
+                        start=(e == 0), stop=(e == 1), is_transpose=True,
+                    )
+            return by_slot(acc)
 
         def slots(ap):
             return ap.rearrange("p (t m) -> p t m", t=4)
@@ -183,159 +206,155 @@ def tile_list_skill_disagreement_marks_kernel(
         def relu_neg(dst, src):
             nc.scalar.activation(dst, src, ACT.Relu, scale=-1.0)
 
-        def make_d(k):
-            c_sb[k] = held([P, H], F32, "c%d" % k)
-            nc.scalar.copy(slots(c_sb[k][:]), product(k, "h" if k < AHEAD else "a", wc_mx))
-            a_ps = product(k, "y0" if k == 2 else "a", wa_mx)
-            nc.vector.tensor_tensor(slots(half(d_sb, k)), slots(c_sb[k][:]), a_ps, ALU.subtract)
+        c_sb, d_sb, summands, by_rows = {}, {}, {}, {}
 
-        def make_u(k):
-            nc.vector.tensor_tensor(slots(half(u_sb, k)), product(k, "b", neg_wb_mx), slots(c_sb[k][:]), ALU.add)
+        def take_d(k, d_ps):
+            d_sb[k], rd = term("d"), term("rd")
+            nc.scalar.copy(slots(d_sb[k][:]), d_ps)
+            relu_neg(slots(rd[:]), d_ps)
+            summands[k] = [rd]
 
-        def paired(k):
-            d_ps = product(k, "a", wc_mx, neg_wb_mx)
-            nc.scalar.copy(slots(half(d_sb, k)), d_ps)
-            relu_neg(slots(half(rd_sb, k)), d_ps)
-            u_ps = product(k, "b", wa_mx, neg_wb_mx)
-            relu_neg(slots(half(ru_sb, k)), u_ps)
-            nc.vector.tensor_tensor(slots(half(m_sb, k)), u_ps, slots(half(d_sb, k)), ALU.max)
+        def row_part(k, n):
+            weight, name = ((neg_wb_mx, "nb"), (wc_mx, "c"), (wa_mx, "u"))[n]
+            by_rows.setdefault(k, []).append(product_by_rows(k, weight, name))
+
+        def first_part(k):
+            if k < PLAIN:
+                bank = "h" if k == AHEAD - 1 else "mm"
+                c_sb[k] = placed([P, H], F32, "c%d" % k, AT_WB1 + 4 * H * k) if k < PLAIN else term("c")
+                d_sb[k], rd = term("d"), term("rd")
+                nc.scalar.copy(slots(c_sb[k][:]), product(k, bank, wc_mx))
+                nc.vector.tensor_tensor(slots(d_sb[k][:]), slots(c_sb[k][:]), product(k, bank, wa_mx), ALU.subtract)
+                relu_neg(rd[:], d_sb[k][:])
+                summands[k] = [rd]
+            elif k >= TURNED:
+                take_d(k, turned_sum(by_rows[k][0], by_rows[k][1]))
+            else:
+                take_d(k, product(k, "mm", wc_mx, neg_wb_mx))
+
+        def second_part(k):
+            ru, top = term("ru"), term("top")
+            if k < PLAIN:
+                u = term("u")
+                nc.vector.tensor_tensor(slots(u[:]), product(k, "y" if k < AHEAD - 1 else "mm", neg_wb_mx), slots(c_sb[k][:]), ALU.add)
+                relu_neg(ru[:], u[:])
+                nc.vector.tensor_tensor(top[:], u[:], d_sb[k][:], ALU.max)
+            else:
+                if k >= TURNED:
+                    u_ps = turned_sum(by_rows[k][0], by_rows[k][2])
+                else:
+                    u_ps = product(k, "mm", wa_mx, neg_wb_mx)
+                relu_neg(slots(ru[:]), u_ps)
+                nc.vector.tensor_tensor(slots(top[:]), u_ps, slots(d_sb[k][:]), ALU.max)
+            summands[k].extend([ru, top])
 
         h_q = held([P, S], U32, "h_q")
         h_sc = held([P, S], U8, "h_sc")
 
-        h_bf = [held([P, 4 * PAIR], BF16, "h_bf%d" % n) for n in range(PAIRS)]
-
-        def turn(*tiles):
-            for k in tiles:
-                h_ps = psum.tile([P, 4, P], F32, name="h_ps", tag="h")
-                for t in range(4):
-                    for e, term in enumerate((rd_sb, m_sb, ru_sb)):
-                        nc.tensor.matmul(
-                            h_ps[:, t, :], slots(half(term, k))[:, t, :], ident[:],
-                            start=(e == 0), stop=(e == 2), is_transpose=True,
-                        )
-                nc.scalar.copy(
-                    half(h_bf, k).rearrange("p (j t) -> p j t", t=4), h_ps[:].rearrange("p t j -> p j t")
-                )
-
-        def quantise_h(n):
+        def turn(k):
+            h_ps = psum.tile([P, 4, P], F32, name="h_ps", tag="h", bufs=BANKS["h"])
+            for t in range(4):
+                for e, summand in enumerate(summands[k]):
+                    nc.tensor.matmul(
+                        h_ps[:, t, :], slots(summand[:])[:, t, :], ident[:],
+                        start=(e == 0), stop=(e == 2), is_transpose=True,
+                    )
+            h_bf = ring.tile([P, 4 * P], BF16, name="h_bf", align_bytes=64)
+            nc.scalar.copy(h_bf[:].rearrange("p (j t) -> p j t", t=4), h_ps[:].rearrange("p t j -> p j t"))
             nc.vector.quantize_mx(
-                out=h_q[:, PAIR * n : PAIR * (n + 1)].bitcast(FP8X4),
-                scales=h_sc[:, PAIR * n : PAIR * (n + 1)],
-                in_=h_bf[n][:],
+                out=h_q[:, P * k : P * (k + 1)].bitcast(FP8X4), scales=h_sc[:, P * k : P * (k + 1)], in_=h_bf[:]
             )
 
+        wd_bf = held([P, 4, P, 4], BF16, "wd_bf")
         wd_q = held([P, N], U32, "wd_q")
         wd_sc = held([P, N], U8, "wd_sc")
 
-        def marks(i, j0, j1, y_ps, y_sb):
-            nc.tensor.matmul_mx(
-                out=y_ps,
-                lhsT=wd_q[:, P * i : P * (i + 1)].bitcast(FP8X4),
-                lhsT_scale=wd_sc[:, P * i : P * (i + 1)],
-                rhs=h_q[:, j0:j1].bitcast(FP8X4),
-                rhs_scale=h_sc[:, j0:j1],
-                start=True,
-                stop=True,
+        def prepare_wd(i0, i1):
+            (nc.vector.tensor_copy if i0 == 0 else nc.scalar.copy)(
+                wd_bf[:, i0:i1].rearrange("p i m j -> p m i j"),
+                wd_raw.rearrange("p (j m i) -> p m i j", j=4, i=4)[:, :, i0:i1, :],
             )
-
-        def shift(i, y_ps, y_sb):
-            nc.scalar.activation(y_sb, y_ps, ACT.Identity, bias=neg_usual[:, i : i + 1])
-
-        def scatter(i, j0, j1, y_sb):
-            nc.vector.tensor_tensor(
-                pages[i][:].indirect(offs2_sb[:, j0 // 16 : j1 // 16]), y_sb, wgo_sb[:, j0:j1], ALU.mult
+            nc.vector.quantize_mx(
+                out=wd_q[:, P * i0 : P * i1].bitcast(FP8X4),
+                scales=wd_sc[:, P * i0 : P * i1],
+                in_=wd_bf[:, i0:i1].rearrange("p i m j -> p (i m j)"),
             )
-
-        def multiply(pieces, bank):
-            widths = [j1 - j0 for i, j0, j1 in pieces]
-            cols = [slice(sum(widths[:n]), sum(widths[: n + 1])) for n in range(len(pieces))]
-            y_ps = psum.tile([P, sum(widths)], F32, name="y_ps", tag=bank, bufs=BANKS[bank])
-            for col, (i, j0, j1) in zip(cols, pieces):
-                marks(i, j0, j1, y_ps[:, col], None)
-            return y_ps, cols, pieces
-
-        def put(made, tag):
-            y_ps, cols, pieces = made
-            y_sb = held([P, cols[-1].stop], F32, "y_sb", tag)
-            for col, (i, j0, j1) in zip(cols, pieces):
-                shift(i, y_ps[:, col], y_sb[:, col])
-            for col, (i, j0, j1) in zip(cols, pieces):
-                scatter(i, j0, j1, y_sb[:, col])
-
-        def place(pieces, bank, tag):
-            put(multiply(pieces, bank), tag)
-
-        def piece(i, n, n1=None):
-            return (i, PAIR * n, PAIR * ((n if n1 is None else n1) + 1))
 
         rows = out.rearrange("(p i) t -> i p t", i=4)
 
+        def place(pieces):
+            width = sum(P * (k1 - k0) for i, k0, k1 in pieces)
+            y_ps = psum.tile([P, width], F32, name="y_ps", tag="y", bufs=BANKS["y"])
+            y_sb = ring.tile([P, width], F32, name="y_sb", align_bytes=64)
+            starts = [sum(P * (k1 - k0) for i, k0, k1 in pieces[:n]) for n in range(len(pieces))]
+            for at, (i, k0, k1) in zip(starts, pieces):
+                for k in range(k0, k1, 2):
+                    j0, j1 = P * k, P * min(k + 2, k1)
+                    nc.tensor.matmul_mx(
+                        out=y_ps[:, at + j0 - P * k0 : at + j1 - P * k0],
+                        lhsT=wd_q[:, P * i : P * (i + 1)].bitcast(FP8X4),
+                        lhsT_scale=wd_sc[:, P * i : P * (i + 1)],
+                        rhs=h_q[:, j0:j1].bitcast(FP8X4),
+                        rhs_scale=h_sc[:, j0:j1],
+                        start=True,
+                        stop=True,
+                    )
+            for at, (i, k0, k1) in zip(starts, pieces):
+                col = slice(at, at + P * (k1 - k0))
+                nc.scalar.activation(y_sb[:, col], y_ps[:, col], ACT.Identity, bias=neg_usual[:, i : i + 1])
+            for at, (i, k0, k1) in zip(starts, pieces):
+                j0, j1 = P * k0, P * k1
+                nc.vector.tensor_tensor(
+                    pages[i][:].indirect(offs2_sb[:, j0 // 16 : j1 // 16]),
+                    y_sb[:, at : at + j1 - j0],
+                    wgo_sb[:, j0:j1],
+                    ALU.mult,
+                )
+                if k1 == TILES:
+                    nc.sync.dma_start(rows[i], pages[i][:])
+
         nc.scalar.activation(*walk(1, 0, SCALAR_COLS), ACT.Copy, scale=-1.0)
         nc.vector.tensor_scalar(*walk(1, SCALAR_COLS, H), -1.0, 0.0, ALU.mult, ALU.add)
-        quantise_wb(0)
         quantise_wb(1)
-        make_d(0)
-        make_d(1)
-        relu_neg(rd_sb[0][:], d_sb[0][:])
-        make_d(2)
-        make_d(3)
-        for k in range(2):
-            make_u(k)
-            relu_neg(half(ru_sb, k), half(u_sb, k))
-        for k in range(2):
-            nc.vector.tensor_tensor(half(m_sb, k), half(u_sb, k), half(d_sb, k), ALU.max)
-        relu_neg(rd_sb[1][:], d_sb[1][:])
-        wd_bf = held([P, 4, P, 4], BF16, "wd_bf", "u0")
-        nc.vector.tensor_copy(
-            wd_bf[:].rearrange("p i m j -> p m i j"), wd_raw[:].rearrange("p j (m i) -> p m i j", i=4)
-        )
-        make_u(2)
-        nc.vector.quantize_mx(
-            out=wd_q[:].bitcast(FP8X4), scales=wd_sc[:], in_=wd_bf[:].rearrange("p i m j -> p (i m j)")
-        )
-        neg_usual = held([P, 4], F32, "neg_usual", "u0")
-        nc.scalar.activation(neg_usual[:], usual_sb[:], ACT.Identity, scale=-1.0)
-        make_u(3)
-        turn(0, 1)
-        relu_neg(ru_sb[1][:], u_sb[1][:])
-        nc.vector.tensor_tensor(m_sb[1][:], u_sb[1][:], d_sb[1][:], ALU.max)
-        quantise_h(0)
-        make_d(4)
-        make_d(5)
-        place([piece(0, 0), piece(1, 0)], "y0", "yab0")
-        late = multiply([piece(2, 0)], "y1")
-        relu_neg(rd_sb[2][:], d_sb[2][:])
-        make_u(4)
-        make_u(5)
-        turn(2, 3)
-        relu_neg(ru_sb[2][:], u_sb[2][:])
-        nc.vector.tensor_tensor(m_sb[2][:], u_sb[2][:], d_sb[2][:], ALU.max)
-        quantise_h(1)
-        put(late, "ru1")
-        paired(6)
-        paired(7)
-        place([piece(0, 1), piece(1, 1)], "y1", "yab1")
-        late = multiply([piece(2, 1)], "y0")
-        turn(4, 5)
-        quantise_h(2)
-        put(late, "ru2")
+        first_part(0)
+        first_part(1)
+        second_part(0)
+        first_part(2)
+        second_part(1)
+        prepare_wd(0, 2)
+        second_part(2)
+        turn(0)
+        prepare_wd(2, 4)
+        first_part(3)
+        second_part(3)
+        turn(1)
+        place([(0, 0, 1), (1, 0, 1)])
+        first_part(4)
+        second_part(4)
+        turn(2)
+        place([(2, 0, 2), (3, 0, 2)])
+        row_part(6, 0)
+        first_part(5)
+        row_part(6, 1)
+        turn(3)
+        place([(0, 1, 3), (1, 1, 3)])
+        second_part(5)
+        row_part(6, 2)
+        turn(4)
+        row_part(7, 0)
+        place([(2, 2, 4), (3, 2, 4)])
+        first_part(6)
+        second_part(6)
+        row_part(7, 1)
+        row_part(7, 2)
+        turn(5)
+        place([(0, 3, 5), (1, 3, 5)])
+        first_part(7)
+        second_part(7)
         turn(6)
-        place([piece(0, 2)], "y1", "yab0")
-        late = multiply([piece(2, 2)], "y0")
+        place([(2, 4, 6)])
         turn(7)
-        quantise_h(3)
-        put(late, "ru3")
-        place([piece(0, 3)], "y1", "yab1")
-        nc.sync.dma_start(rows[0], pages[0][:])
-        place([piece(1, 2, 3)], "y0", "yb23")
-        nc.sync.dma_start(rows[1], pages[1][:])
-        place([piece(2, 3)], "y1", "yc3")
-        nc.sync.dma_start(rows[2], pages[2][:])
-        y_last = held([P, S], F32, "y_last")
-        for n in range(2):
-            y_ps = psum.tile([P, HALF], F32, name="y_ps", tag="b")
-            marks(3, HALF * n, HALF * (n + 1), y_ps[:], None)
-            shift(3, y_ps[:], y_last[:, HALF * n : HALF * (n + 1)])
-        scatter(3, 0, S, y_last[:])
-        nc.sync.dma_start(rows[3], pages[3][:])
+        place([(0, 5, 7)])
+        place([(0, 7, 8), (2, 6, 8)])
+        place([(1, 5, 8)])
+        place([(3, 4, 8)])

@@ -183,20 +183,23 @@ def tile_list_skill_disagreement_marks_kernel(
 
         def product_by_rows(k, weight, name):
             acc = bank_tile("mm")
-            for i in range(4):
-                for a in range(2):
-                    mx_pass(acc[:, P * i : P * (i + 1)], weight(a, P * i, P * (i + 1)), picked_mx(a, k), a == 0, a == 1)
+            for a in range(2):
+                for i in range(4):
+                    mx_pass(
+                        acc[:, P * i : P * (i + 1)], weight(a, P * i, P * (i + 1)), picked_mx(a, k),
+                        a == 0 and i == 0, a == 1 and i == 3,
+                    )
             rows_sb = term(name)
             nc.scalar.copy(rows_sb[:], acc[:])
             return rows_sb
 
         def turned_sum(first, second):
             acc = bank_tile("mm")
-            for i in range(4):
-                for e, rows_sb in enumerate((first, second)):
+            for e, rows_sb in enumerate((first, second)):
+                for i in range(4):
                     nc.tensor.matmul(
                         acc[:, P * i : P * (i + 1)], rows_sb[:, P * i : P * (i + 1)], ident[:],
-                        start=(e == 0), stop=(e == 1), is_transpose=True,
+                        start=(e == 0 and i == 0), stop=(e == 1 and i == 3), is_transpose=True,
                     )
             return by_slot(acc)
 
@@ -253,11 +256,11 @@ def tile_list_skill_disagreement_marks_kernel(
 
         def turn(k):
             h_ps = psum.tile([P, 4, P], F32, name="h_ps", tag="h", bufs=BANKS["h"])
-            for t in range(4):
-                for e, summand in enumerate(summands[k]):
+            for e, summand in enumerate(summands[k]):
+                for t in range(4):
                     nc.tensor.matmul(
                         h_ps[:, t, :], slots(summand[:])[:, t, :], ident[:],
-                        start=(e == 0), stop=(e == 2), is_transpose=True,
+                        start=(e == 0 and t == 0), stop=(e == 2 and t == 3), is_transpose=True,
                     )
             h_bf = ring.tile([P, 4 * P], BF16, name="h_bf", align_bytes=64)
             nc.scalar.copy(h_bf[:].rearrange("p (j t) -> p j t", t=4), h_ps[:].rearrange("p t j -> p j t"))

@@ -20,10 +20,11 @@ ACT = mybir.ActivationFunctionType
 P = 128
 TILES = S // P
 HALF = S // 2
-PLAIN = 4
+PLAIN = 3
+SHARED = 3 * H // 4
 TURNED = 6
 AHEAD = 3
-SCALAR_COLS = 224
+SCALAR_COLS = 288
 BANKS = {"mm": 4, "h": 2, "y": 2}
 DEPTH = 4
 
@@ -181,6 +182,15 @@ def tile_list_skill_disagreement_marks_kernel(
                 mx_pass(acc[:], picked_mx(a, k), weight(a), n == 0, n == len(passes) - 1)
             return by_slot(acc)
 
+        def mostly_less_b(k, weight):
+            acc = bank_tile("mm")
+            for a in range(2):
+                mx_pass(acc[:], picked_mx(a, k), weight(a), a == 0, False)
+            for c0, c1 in ((0, H // 2), (H // 2, SHARED)):
+                for a in range(2):
+                    mx_pass(acc[:, c0:c1], picked_mx(a, k), neg_wb_mx(a, c0, c1), False, a == 1 and c1 == SHARED)
+            return by_slot(acc)
+
         def product_by_rows(k, weight, name):
             acc = bank_tile("mm")
             for a in range(2):
@@ -230,6 +240,9 @@ def tile_list_skill_disagreement_marks_kernel(
                 nc.vector.tensor_tensor(slots(d_sb[k][:]), slots(c_sb[k][:]), product(k, bank, wa_mx), ALU.subtract)
                 relu_neg(rd[:], d_sb[k][:])
                 summands[k] = [rd]
+            elif k == PLAIN:
+                d_sb[k] = term("d")
+                nc.scalar.copy(slots(d_sb[k][:]), mostly_less_b(k, wc_mx))
             elif k >= TURNED:
                 take_d(k, turned_sum(by_rows[k][0], by_rows[k][1]))
             else:
@@ -242,6 +255,21 @@ def tile_list_skill_disagreement_marks_kernel(
                 nc.vector.tensor_tensor(slots(u[:]), product(k, "y" if k < AHEAD - 1 else "mm", neg_wb_mx), slots(c_sb[k][:]), ALU.add)
                 relu_neg(ru[:], u[:])
                 nc.vector.tensor_tensor(top[:], u[:], d_sb[k][:], ALU.max)
+            elif k == PLAIN:
+                cut = SHARED // 4
+                rest = bank_tile("mm")
+                for a in range(2):
+                    mx_pass(rest[:, SHARED:], picked_mx(a, k), neg_wb_mx(a, SHARED, H), a == 0, a == 1)
+                u_ps = mostly_less_b(k, wa_mx)
+                d, u, rd = slots(d_sb[k][:]), slots(term("u")[:]), term("rd")
+                nc.vector.tensor_tensor(u[:, :, cut:], by_slot(rest)[:, :, cut:], d[:, :, cut:], ALU.add)
+                nc.vector.tensor_tensor(d[:, :, cut:], d[:, :, cut:], u_ps[:, :, cut:], ALU.subtract)
+                relu_neg(slots(ru[:])[:, :, :cut], u_ps[:, :, :cut])
+                relu_neg(slots(ru[:])[:, :, cut:], u[:, :, cut:])
+                relu_neg(rd[:], d_sb[k][:])
+                nc.vector.tensor_tensor(slots(top[:])[:, :, :cut], u_ps[:, :, :cut], d[:, :, :cut], ALU.max)
+                nc.vector.tensor_tensor(slots(top[:])[:, :, cut:], u[:, :, cut:], d[:, :, cut:], ALU.max)
+                summands[k] = [rd]
             else:
                 if k >= TURNED:
                     u_ps = turned_sum(by_rows[k][0], by_rows[k][2])
@@ -313,8 +341,11 @@ def tile_list_skill_disagreement_marks_kernel(
                     wgo_sb[:, j0:j1],
                     ALU.mult,
                 )
-                if k1 == TILES:
+                if k1 == TILES and i < 3:
                     nc.sync.dma_start(rows[i], pages[i][:])
+                elif k1 == TILES:
+                    for queue, c0 in ((nc.sync, 0), (nc.scalar, T2 // 2)):
+                        queue.dma_start(rows[i][:, c0 : c0 + T2 // 2], pages[i][:, c0 : c0 + T2 // 2])
 
         nc.scalar.activation(*walk(1, 0, SCALAR_COLS), ACT.Copy, scale=-1.0)
         nc.vector.tensor_scalar(*walk(1, SCALAR_COLS, H), -1.0, 0.0, ALU.mult, ALU.add)
@@ -355,9 +386,9 @@ def tile_list_skill_disagreement_marks_kernel(
         first_part(7)
         second_part(7)
         turn(6)
-        place([(2, 4, 6)])
+        place([(2, 4, 6), (1, 5, 6)])
         turn(7)
         place([(0, 5, 7)])
-        place([(0, 7, 8), (2, 6, 8)])
-        place([(1, 5, 8)])
+        place([(0, 7, 8), (1, 6, 8)])
+        place([(2, 6, 8)])
         place([(3, 4, 8)])

@@ -19,24 +19,25 @@ ACT = mybir.ActivationFunctionType
 
 P = 128
 TILES = S // P
-HALF = S // 2
-PLAIN = 3
 SHARED = 3 * H // 4
-TURNED = 6
-AHEAD = 3
-SCALAR_COLS = 288
-BANKS = {"mm": 4, "h": 2, "y": 2}
+ROW = S + 2 * H
+EDGE = 64
+SCALAR_COLS = 352
+BANKS, BANK_BYTES = 8, 2048
+MOSTLY = 4
 DEPTH = 4
 
-AT_TAB1 = 0
-AT_GATHERED = AT_TAB1 + 4 * T - 64
-AT_WB1 = AT_GATHERED + S - 64
-AT_WD = AT_WB1 + 16 * H
-AT_STAGED = AT_WD + 16 * N - 64
-AT_WGO = AT_STAGED + S + 2 * H - 64
-AT_PAGE2 = AT_WGO + 4 * S
-AT_TAB0 = AT_PAGE2 + 2 * T2
-AT_PAGE3 = AT_PAGE2 + 4 * T2
+AT_WB_BF0 = 0
+AT_TAB_SC = AT_WB_BF0 + 8 * H - EDGE
+AT_PAGE3 = AT_TAB_SC + T - EDGE
+AT_GATHERED = AT_PAGE3 + 4 * T2
+AT_WB_BF1 = AT_GATHERED + S - EDGE
+AT_WGO = AT_WB_BF1 + 8 * H
+AT_STAGED = AT_WGO + 4 * S - EDGE
+AT_WD = AT_STAGED + 2 * ROW - EDGE
+AT_H0 = AT_WD + 16 * N
+AT_WD_BF1 = AT_H0 + 8 * P - EDGE
+LAST_FIRST = (("ru", "rd", "top"), ("rd", "ru", "top"), ("top", "ru", "rd"))
 
 
 def tile_list_skill_disagreement_marks_kernel(
@@ -48,7 +49,7 @@ def tile_list_skill_disagreement_marks_kernel(
         keep = ctx.enter_context(tc.tile_pool(name="keep", bufs=1))
         ring = ctx.enter_context(tc.tile_pool(name="ring", bufs=DEPTH))
         arena = ctx.enter_context(tc.tile_pool(name="arena", bufs=1))
-        psum = ctx.enter_context(tc.psum_pool(name="psum", bufs=2))
+        psum = ctx.enter_context(tc.psum_pool(name="psum", bufs=1))
 
         def placed(shape, dtype, name, offset):
             return arena.tile(shape, dtype, name=name, offset=offset, align_bytes=64)
@@ -61,81 +62,58 @@ def tile_list_skill_disagreement_marks_kernel(
 
         offs_sb = lists.tile([P, S // 16], U16, name="offs_sb")
         offs2_sb = lists.tile([P, S // 16], U16, name="offs2_sb")
-        tab_sc = held([P, T], U8, "tab_sc")
-        planes = [held([P, S + 2 * H], U8, "plane%d" % a) for a in range(2)]
+        tab_sc = placed([P, T], U8, "tab_sc", AT_TAB_SC)
         nc.vector.memset(tab_sc[:].bitcast(I32), 0)
-        staged = placed([P, S + 2 * H], U8, "staged", AT_STAGED)
+        plane = held([P, 2 * ROW], U8, "plane")
+        staged = placed([P, 2 * ROW], U8, "staged", AT_STAGED)
         zero = held([P, 1], U32, "zero")
         nc.vector.memset(zero[:], 0)
-        for plane in planes:
-            nc.scalar.copy(plane[:].bitcast(U32), zero[:].to_broadcast([P, (S + 2 * H) // 4]))
+        nc.scalar.copy(plane[:].bitcast(U32), zero[:].to_broadcast([P, 2 * ROW // 4]))
 
-        def load_scale_rows(dst, src):
-            nc.sync.dma_start(dst[0:P:4, :].bitcast(I32), src.bitcast(I32).rearrange("a q t -> q a t"))
+        def load_weight_scales(c0, src):
+            nc.sync.dma_start(
+                staged[0:P:8, :].bitcast(I32).rearrange("q (a c) -> q a c", a=2)[:, :, c0 // 4 : (c0 + H) // 4],
+                src.bitcast(I32).rearrange("a q t -> q a t"),
+            )
 
         nc.sync.dma_start(offs_sb[:], offs)
-        load_scale_rows(staged[:, S : S + H], wc_scales)
-        load_scale_rows(staged[:, S + H :], wa_scales)
+        load_weight_scales(S, wc_scales)
+        load_weight_scales(S + H, wa_scales)
         nc.sync.dma_start(offs2_sb[:], offs2)
         usual_sb = held([P, 4], F32, "usual_sb")
         nc.sync.dma_start(usual_sb[:], usual.rearrange("(p i) -> p i", i=4))
-        load_scale_rows(tab_sc, tab_scales)
+        nc.sync.dma_start(tab_sc[0:P:4, :].bitcast(I32), tab_scales.bitcast(I32).rearrange("a q t -> q a t"))
 
-        tab_w = [placed([P, T], I32, "tab_w0", AT_TAB0), placed([P, T], I32, "tab_w1", AT_TAB1)]
+        tab_w = [held([P, T], I32, "tab_w%d" % a) for a in range(2)]
         wb_rows = wb.rearrange("(a p j) c -> a p (j c)", a=2, j=4)
-        wb_raw0 = held([P, 4 * H], F32, "wb_raw0")
+        wb_raw = [held([P, 4 * H], F32, "wb_raw%d" % a)[:] for a in range(2)]
 
         def load_words(a):
             nc.sync.dma_start(tab_w[a][:], tab_words[a].rearrange("p t i -> p (t i)").bitcast(I32))
 
+        nc.sync.dma_start(wb_raw[0], wb_rows[0])
         load_words(0)
-        nc.sync.dma_start(wb_raw0[:], wb_rows[0])
+        load_words(1)
+        nc.sync.dma_start(wb_raw[1], wb_rows[1])
         wc_sb = held([P, 2, H], I32, "wc_sb")
         nc.sync.dma_start(wc_sb[:], wc_words.rearrange("a p e i -> p a (e i)").bitcast(I32))
         wa_sb = held([P, 2, H // 2], I32, "wa_sb")
         nc.sync.dma_start(wa_sb[:], wa_words.rearrange("a p n -> p a n").bitcast(I32))
 
-        pages = [held([P, T2], F32, "page%d" % i) for i in range(2)]
+        pages = [held([P, T2], F32, "page%d" % i) for i in range(3)]
+        pages.append(placed([P, T2], F32, "page3", AT_PAGE3))
+
+        def clear(i):
+            nc.vector.memset(pages[i][:].bitcast(I32), 0)
+
         ident = held([P, P], F32, "ident")
         make_identity(nc, ident[:])
-        for i in range(2):
-            nc.vector.memset(pages[i][:].bitcast(I32), 0)
+        clear(0)
+        clear(1)
         neg_usual = held([P, 4], F32, "neg_usual")
         nc.scalar.activation(neg_usual[:], usual_sb[:], ACT.Identity, scale=-1.0)
 
-        gathered_sc = placed([P, S], U8, "gathered_sc", AT_GATHERED)
-        nc.vector.tensor_copy(gathered_sc[:], tab_sc[:].indirect(offs_sb[:]))
-        nc.vector.tensor_copy(staged[:, :S].bitcast(I32), gathered_sc[:].bitcast(I32))
-
-        def move(a, r):
-            nc.sync.dma_start(planes[a][r:P:32, :].bitcast(I32), staged[8 * r + 4 * a : P : 32, :].bitcast(I32))
-
-        wb_raw1 = placed([P, 4 * H], F32, "wb_raw1", AT_WB1)[:]
-        wd_raw = placed([P, 4 * N], F32, "wd_raw", AT_WD)[:]
-        wgo_sb = placed([P, S], F32, "wgo_sb", AT_WGO)[:]
-        moves = [(a, r) for a in range(2) for r in range(4)]
-        for a, r in moves[:3]:
-            move(a, r)
-        load_words(1)
-        for a, r in moves[3:]:
-            move(a, r)
-        nc.sync.dma_start(wb_raw1, wb_rows[1])
-        nc.sync.dma_start(wd_raw, wd.rearrange("(p j) c -> p (j c)", j=4))
-        nc.sync.dma_start(wgo_sb, wgo)
-
-        picked_words = [held([P, S], U32, "picked_words%d" % a) for a in range(2)]
-        nc.vector.tensor_copy(picked_words[0][:], tab_w[0][:].bitcast(U32).indirect(offs_sb[:]))
-        for i, at in ((2, AT_PAGE2), (3, AT_PAGE3)):
-            pages.append(placed([P, T2], F32, "page%d" % i, at))
-            nc.vector.memset(pages[i][:].bitcast(I32), 0)
-        for half in range(2):
-            nc.vector.tensor_copy(
-                picked_words[1][:, HALF * half : HALF * (half + 1)],
-                tab_w[1][:].bitcast(U32).indirect(offs_sb[:, HALF // 16 * half : HALF // 16 * (half + 1)]),
-            )
-
-        wb_raw = [wb_raw0[:], wb_raw1]
-        neg_wb_bf = [held([P, 4 * H], BF16, "neg_wb_bf%d" % a) for a in range(2)]
+        neg_wb_bf = [placed([P, 4 * H], BF16, "neg_wb_bf%d" % a, at) for a, at in enumerate((AT_WB_BF0, AT_WB_BF1))]
         neg_wb_q = [held([P, H], U32, "neg_wb_q%d" % a) for a in range(2)]
         neg_wb_sc = [held([P, H], U8, "neg_wb_sc%d" % a) for a in range(2)]
 
@@ -148,20 +126,50 @@ def tile_list_skill_disagreement_marks_kernel(
         def quantise_wb(a):
             nc.vector.quantize_mx(out=neg_wb_q[a][:].bitcast(FP8X4), scales=neg_wb_sc[a][:], in_=neg_wb_bf[a][:])
 
+        picked_words = [held([P, S], U32, "picked_words%d" % a) for a in range(2)]
+
+        def gather_words(a, j0, j1):
+            nc.vector.tensor_copy(
+                picked_words[a][:, j0:j1], tab_w[a][:].bitcast(U32).indirect(offs_sb[:, j0 // 16 : j1 // 16])
+            )
+
+        gathered_sc = placed([P, S], U8, "gathered_sc", AT_GATHERED)
+        nc.vector.tensor_copy(gathered_sc[:], tab_sc[:].indirect(offs_sb[:]))
+        nc.scalar.dma_start(staged[0:P:8, ROW : ROW + S].bitcast(I32), gathered_sc[4:P:8, :].bitcast(I32))
         nc.scalar.activation(*walk(0, 0, H), ACT.Copy, scale=-1.0)
+        clear(2)
+        nc.vector.tensor_copy(staged[:, :S].bitcast(I32), gathered_sc[:].bitcast(I32))
+        clear(3)
+        for r in range(4):
+            nc.scalar.dma_start(plane[r:P:32, :].bitcast(I32), staged[8 * r : P : 32, :].bitcast(I32))
+
+        wd_raw = placed([P, 4 * N], F32, "wd_raw", AT_WD)[:]
+        nc.sync.dma_start(wd_raw, wd.rearrange("(p j) c -> p (j c)", j=4))
+        wgo_sb = placed([P, S], F32, "wgo_sb", AT_WGO)[:]
+        nc.sync.dma_start(wgo_sb, wgo)
+
+        gather_words(0, 0, S)
         quantise_wb(0)
+        gather_words(1, 0, S // 2)
+        gather_words(1, S // 2, S)
+        nc.scalar.activation(*walk(1, 0, SCALAR_COLS), ACT.Copy, scale=-1.0)
+        nc.vector.tensor_scalar(*walk(1, SCALAR_COLS, H), -1.0, 0.0, ALU.mult, ALU.add)
+        quantise_wb(1)
 
         def wc_mx(a, c0=0, c1=H):
-            return wc_sb[:, a, c0:c1].bitcast(FP8X4), planes[a][:, S + c0 : S + c1]
+            return wc_sb[:, a, c0:c1].bitcast(FP8X4), plane[:, ROW * a + S + c0 : ROW * a + S + c1]
 
         def wa_mx(a, c0=0, c1=H):
-            return wa_sb[:, a, c0 // 2 : c1 // 2].bitcast(FP4X4), planes[a][:, S + H + c0 : S + H + c1]
+            return wa_sb[:, a, c0 // 2 : c1 // 2].bitcast(FP4X4), plane[:, ROW * a + S + H + c0 : ROW * a + S + H + c1]
 
         def neg_wb_mx(a, c0=0, c1=H):
             return neg_wb_q[a][:, c0:c1].bitcast(FP8X4), neg_wb_sc[a][:, c0:c1]
 
         def picked_mx(a, k):
-            return picked_words[a][:, P * k : P * (k + 1)].bitcast(FP8X4), planes[a][:, P * k : P * (k + 1)]
+            return (
+                picked_words[a][:, P * k : P * (k + 1)].bitcast(FP8X4),
+                plane[:, ROW * a + P * k : ROW * a + P * (k + 1)],
+            )
 
         def mx_pass(acc, stationary, moving, start, stop):
             nc.tensor.matmul_mx(
@@ -169,49 +177,17 @@ def tile_list_skill_disagreement_marks_kernel(
                 start=start, stop=stop,
             )
 
-        def bank_tile(bank):
-            return psum.tile([P, H], F32, name="acc", tag=bank, bufs=BANKS[bank])
+        free_banks, bank_of = list(range(BANKS)), {}
+
+        def bank_tile(k, name, shape=(P, H)):
+            bank_of[k, name] = free_banks.pop(0)
+            return psum.tile(list(shape), F32, name="%s_%s" % (name, k), offset=BANK_BYTES * bank_of[k, name])
+
+        def give_back(k, name):
+            free_banks.append(bank_of.pop((k, name)))
 
         def by_slot(acc):
             return acc[:].rearrange("p (m t) -> p t m", t=4)
-
-        def product(k, bank, *weights):
-            acc = bank_tile(bank)
-            passes = [(a, weight) for weight in weights for a in range(2)]
-            for n, (a, weight) in enumerate(passes):
-                mx_pass(acc[:], picked_mx(a, k), weight(a), n == 0, n == len(passes) - 1)
-            return by_slot(acc)
-
-        def mostly_less_b(k, weight):
-            acc = bank_tile("mm")
-            for a in range(2):
-                mx_pass(acc[:], picked_mx(a, k), weight(a), a == 0, False)
-            for c0, c1 in ((0, H // 2), (H // 2, SHARED)):
-                for a in range(2):
-                    mx_pass(acc[:, c0:c1], picked_mx(a, k), neg_wb_mx(a, c0, c1), False, a == 1 and c1 == SHARED)
-            return by_slot(acc)
-
-        def product_by_rows(k, weight, name):
-            acc = bank_tile("mm")
-            for a in range(2):
-                for i in range(4):
-                    mx_pass(
-                        acc[:, P * i : P * (i + 1)], weight(a, P * i, P * (i + 1)), picked_mx(a, k),
-                        a == 0 and i == 0, a == 1 and i == 3,
-                    )
-            rows_sb = term(name)
-            nc.scalar.copy(rows_sb[:], acc[:])
-            return rows_sb
-
-        def turned_sum(first, second):
-            acc = bank_tile("mm")
-            for e, rows_sb in enumerate((first, second)):
-                for i in range(4):
-                    nc.tensor.matmul(
-                        acc[:, P * i : P * (i + 1)], rows_sb[:, P * i : P * (i + 1)], ident[:],
-                        start=(e == 0 and i == 0), stop=(e == 1 and i == 3), is_transpose=True,
-                    )
-            return by_slot(acc)
 
         def slots(ap):
             return ap.rearrange("p (t m) -> p t m", t=4)
@@ -219,104 +195,167 @@ def tile_list_skill_disagreement_marks_kernel(
         def relu_neg(dst, src):
             nc.scalar.activation(dst, src, ACT.Relu, scale=-1.0)
 
-        c_sb, d_sb, summands, by_rows = {}, {}, {}, {}
+        sums, open_sums, sb = {}, {}, {}
 
-        def take_d(k, d_ps):
-            d_sb[k], rd = term("d"), term("rd")
-            nc.scalar.copy(slots(d_sb[k][:]), d_ps)
-            relu_neg(slots(rd[:]), d_ps)
-            summands[k] = [rd]
+        def begin(k, name, passes):
+            open_sums[k, name] = bank_tile(k, name)
+            for n, (a, weight) in enumerate(passes):
+                mx_pass(open_sums[k, name][:], picked_mx(a, k), weight(a), n == 0, False)
 
-        def row_part(k, n):
-            weight, name = ((neg_wb_mx, "nb"), (wc_mx, "c"), (wa_mx, "u"))[n]
-            by_rows.setdefault(k, []).append(product_by_rows(k, weight, name))
+        def finish(k, name, passes):
+            acc = open_sums.pop((k, name))
+            for n, (a, weight) in enumerate(passes):
+                mx_pass(acc[:], picked_mx(a, k), weight(a), False, n == len(passes) - 1)
+            sums[k, name] = by_slot(acc)
 
-        def first_part(k):
-            if k < PLAIN:
-                bank = "h" if k == AHEAD - 1 else "mm"
-                c_sb[k] = placed([P, H], F32, "c%d" % k, AT_WB1 + 4 * H * k) if k < PLAIN else term("c")
-                d_sb[k], rd = term("d"), term("rd")
-                nc.scalar.copy(slots(c_sb[k][:]), product(k, bank, wc_mx))
-                nc.vector.tensor_tensor(slots(d_sb[k][:]), slots(c_sb[k][:]), product(k, bank, wa_mx), ALU.subtract)
-                relu_neg(rd[:], d_sb[k][:])
-                summands[k] = [rd]
-            elif k == PLAIN:
-                d_sb[k] = term("d")
-                nc.scalar.copy(slots(d_sb[k][:]), mostly_less_b(k, wc_mx))
-            elif k >= TURNED:
-                take_d(k, turned_sum(by_rows[k][0], by_rows[k][1]))
-            else:
-                take_d(k, product(k, "mm", wc_mx, neg_wb_mx))
+        def product(k, name, *weights):
+            passes = [(a, weight) for weight in weights for a in range(2)]
+            begin(k, name, passes[:1])
+            finish(k, name, passes[1:])
 
-        def second_part(k):
-            ru, top = term("ru"), term("top")
-            if k < PLAIN:
-                u = term("u")
-                nc.vector.tensor_tensor(slots(u[:]), product(k, "y" if k < AHEAD - 1 else "mm", neg_wb_mx), slots(c_sb[k][:]), ALU.add)
-                relu_neg(ru[:], u[:])
-                nc.vector.tensor_tensor(top[:], u[:], d_sb[k][:], ALU.max)
-            elif k == PLAIN:
-                cut = SHARED // 4
-                rest = bank_tile("mm")
+        def mostly_less_b(k, name, weight):
+            acc = bank_tile(k, name)
+            for a in range(2):
+                mx_pass(acc[:], picked_mx(a, k), weight(a), a == 0, False)
+            for c0, c1 in ((0, H // 2), (H // 2, SHARED)):
                 for a in range(2):
-                    mx_pass(rest[:, SHARED:], picked_mx(a, k), neg_wb_mx(a, SHARED, H), a == 0, a == 1)
-                u_ps = mostly_less_b(k, wa_mx)
-                d, u, rd = slots(d_sb[k][:]), slots(term("u")[:]), term("rd")
-                nc.vector.tensor_tensor(u[:, :, cut:], by_slot(rest)[:, :, cut:], d[:, :, cut:], ALU.add)
-                nc.vector.tensor_tensor(d[:, :, cut:], d[:, :, cut:], u_ps[:, :, cut:], ALU.subtract)
-                relu_neg(slots(ru[:])[:, :, :cut], u_ps[:, :, :cut])
-                relu_neg(slots(ru[:])[:, :, cut:], u[:, :, cut:])
-                relu_neg(rd[:], d_sb[k][:])
-                nc.vector.tensor_tensor(slots(top[:])[:, :, :cut], u_ps[:, :, :cut], d[:, :, :cut], ALU.max)
-                nc.vector.tensor_tensor(slots(top[:])[:, :, cut:], u[:, :, cut:], d[:, :, cut:], ALU.max)
-                summands[k] = [rd]
-            else:
-                if k >= TURNED:
-                    u_ps = turned_sum(by_rows[k][0], by_rows[k][2])
-                else:
-                    u_ps = product(k, "mm", wa_mx, neg_wb_mx)
-                relu_neg(slots(ru[:]), u_ps)
-                nc.vector.tensor_tensor(slots(top[:]), u_ps, slots(d_sb[k][:]), ALU.max)
-            summands[k].extend([ru, top])
+                    mx_pass(acc[:, c0:c1], picked_mx(a, k), neg_wb_mx(a, c0, c1), False, a == 1 and c1 == SHARED)
+            sums[k, name] = by_slot(acc)
+
+        def rest_of_b(k):
+            rest = bank_tile(k, "nb")
+            for a in range(2):
+                mx_pass(rest[:, SHARED:], picked_mx(a, k), neg_wb_mx(a, SHARED, H), a == 0, a == 1)
+            sums[k, "nb"] = by_slot(rest)
+
+        def by_rows(k, name, weight):
+            acc = open_sums[k, name] = bank_tile(k, name)
+            for a in range(2):
+                for i in range(4):
+                    mx_pass(
+                        acc[:, P * i : P * (i + 1)], weight(a, P * i, P * (i + 1)), picked_mx(a, k),
+                        a == 0 and i == 0, a == 1 and i == 3,
+                    )
+
+        def copy_rows(k, name):
+            sb[k, name + "_rows"] = term("rows")
+            nc.scalar.copy(sb[k, name + "_rows"][:], open_sums.pop((k, name))[:])
+            give_back(k, name)
+
+        def turned_sum(k, name, first, second):
+            acc = bank_tile(k, name)
+            for e, part in enumerate((first, second)):
+                for i in range(4):
+                    nc.tensor.matmul(
+                        acc[:, P * i : P * (i + 1)], sb[k, part + "_rows"][:, P * i : P * (i + 1)], ident[:],
+                        start=(e == 0 and i == 0), stop=(e == 1 and i == 3), is_transpose=True,
+                    )
+            sums[k, name] = by_slot(acc)
+
+        def copy_out(k, name):
+            sb[k, name] = term(name)
+            nc.scalar.copy(slots(sb[k, name][:]), sums[k, name])
+            if name == "c" or k == MOSTLY:
+                give_back(k, name)
+
+        def make_d(k):
+            sb[k, "d"] = term("d")
+            nc.vector.tensor_tensor(slots(sb[k, "d"][:]), slots(sb[k, "c"][:]), sums[k, "a"], ALU.subtract)
+            give_back(k, "a")
+
+        def make_u(k):
+            sb[k, "u"] = term("u")
+            nc.vector.tensor_tensor(slots(sb[k, "u"][:]), sums[k, "nb"], slots(sb[k, "c"][:]), ALU.add)
+            give_back(k, "nb")
+
+        def relu(k, name):
+            sb[k, "r" + name] = term("r" + name)
+            src = sums[k, name] if (k, name) in sums else slots(sb[k, name][:])
+            relu_neg(slots(sb[k, "r" + name][:]), src)
+            if name == "d" and (k, name) in sums:
+                give_back(k, name)
+
+        def make_top(k):
+            sb[k, "top"] = term("top")
+            u = slots(sb[k, "u"][:]) if (k, "u") in sb else sums[k, "u"]
+            nc.vector.tensor_tensor(slots(sb[k, "top"][:]), u, slots(sb[k, "d"][:]), ALU.max)
+            if (k, "u") in sums:
+                give_back(k, "u")
+
+        cut = SHARED // 4
+
+        def relu_shared(k):
+            sb[k, "ru"] = term("ru")
+            relu_neg(slots(sb[k, "ru"][:])[:, :, :cut], sums[k, "u"][:, :, :cut])
+
+        def mend_rest(k):
+            sb[k, "top"], sb[k, "u"] = term("top"), term("u")
+            d, u, top = slots(sb[k, "d"][:]), slots(sb[k, "u"][:]), slots(sb[k, "top"][:])
+            nc.vector.tensor_tensor(u[:, :, cut:], sums[k, "nb"][:, :, cut:], d[:, :, cut:], ALU.add)
+            nc.vector.tensor_tensor(top[:, :, :cut], sums[k, "u"][:, :, :cut], d[:, :, :cut], ALU.max)
+            nc.vector.tensor_tensor(d[:, :, cut:], d[:, :, cut:], sums[k, "u"][:, :, cut:], ALU.subtract)
+            give_back(k, "nb")
+            give_back(k, "u")
+
+        def top_of_rest(k):
+            d, u, top = slots(sb[k, "d"][:]), slots(sb[k, "u"][:]), slots(sb[k, "top"][:])
+            nc.vector.tensor_tensor(top[:, :, cut:], u[:, :, cut:], d[:, :, cut:], ALU.max)
+
+        def relu_rest(k):
+            sb[k, "rd"] = term("rd")
+            relu_neg(slots(sb[k, "ru"][:])[:, :, cut:], slots(sb[k, "u"][:])[:, :, cut:])
+            relu_neg(sb[k, "rd"][:], sb[k, "d"][:])
 
         h_q = held([P, S], U32, "h_q")
         h_sc = held([P, S], U8, "h_sc")
+        h_ps, h_bf = {}, {}
 
         def turn(k):
-            h_ps = psum.tile([P, 4, P], F32, name="h_ps", tag="h", bufs=BANKS["h"])
-            for e, summand in enumerate(summands[k]):
+            h_ps[k] = bank_tile(k, "h", (P, 4, P))
+            for e, name in enumerate(LAST_FIRST[k == MOSTLY or (2 if k > MOSTLY else 0)]):
                 for t in range(4):
                     nc.tensor.matmul(
-                        h_ps[:, t, :], slots(summand[:])[:, t, :], ident[:],
+                        h_ps[k][:, t, :], slots(sb[k, name][:])[:, t, :], ident[:],
                         start=(e == 0 and t == 0), stop=(e == 2 and t == 3), is_transpose=True,
                     )
-            h_bf = ring.tile([P, 4 * P], BF16, name="h_bf", align_bytes=64)
-            nc.scalar.copy(h_bf[:].rearrange("p (j t) -> p j t", t=4), h_ps[:].rearrange("p t j -> p j t"))
+
+        def round_h(k):
+            if k == 0:
+                h_bf[k] = placed([P, 4 * P], BF16, "h_bf0", AT_H0)
+            else:
+                h_bf[k] = ring.tile([P, 4 * P], BF16, name="h_bf", align_bytes=64)
+            nc.scalar.copy(h_bf[k][:].rearrange("p (j t) -> p j t", t=4), h_ps[k][:].rearrange("p t j -> p j t"))
+            give_back(k, "h")
+
+        def quantise_h(k):
             nc.vector.quantize_mx(
-                out=h_q[:, P * k : P * (k + 1)].bitcast(FP8X4), scales=h_sc[:, P * k : P * (k + 1)], in_=h_bf[:]
+                out=h_q[:, P * k : P * (k + 1)].bitcast(FP8X4), scales=h_sc[:, P * k : P * (k + 1)], in_=h_bf[k][:]
             )
 
-        wd_bf = held([P, 4, P, 4], BF16, "wd_bf")
         wd_q = held([P, N], U32, "wd_q")
         wd_sc = held([P, N], U8, "wd_sc")
+        wd_bf = {}
 
-        def prepare_wd(i0, i1):
-            (nc.vector.tensor_copy if i0 == 0 else nc.scalar.copy)(
-                wd_bf[:, i0:i1].rearrange("p i m j -> p m i j"),
-                wd_raw.rearrange("p (j m i) -> p m i j", j=4, i=4)[:, :, i0:i1, :],
+        def round_wd(i0):
+            shape = [P, 2, P, 4]
+            wd_bf[i0] = held(shape, BF16, "wd_bf0") if i0 == 0 else placed(shape, BF16, "wd_bf1", AT_WD_BF1)
+            nc.scalar.copy(
+                wd_bf[i0][:].rearrange("p i m j -> p m i j"),
+                wd_raw.rearrange("p (j m i) -> p m i j", j=4, i=4)[:, :, i0 : i0 + 2, :],
             )
+
+        def quantise_wd(i0):
             nc.vector.quantize_mx(
-                out=wd_q[:, P * i0 : P * i1].bitcast(FP8X4),
-                scales=wd_sc[:, P * i0 : P * i1],
-                in_=wd_bf[:, i0:i1].rearrange("p i m j -> p (i m j)"),
+                out=wd_q[:, P * i0 : P * (i0 + 2)].bitcast(FP8X4),
+                scales=wd_sc[:, P * i0 : P * (i0 + 2)],
+                in_=wd_bf[i0][:].rearrange("p i m j -> p (i m j)"),
             )
 
         rows = out.rearrange("(p i) t -> i p t", i=4)
 
-        def place(pieces):
+        def marks(pieces):
             width = sum(P * (k1 - k0) for i, k0, k1 in pieces)
-            y_ps = psum.tile([P, width], F32, name="y_ps", tag="y", bufs=BANKS["y"])
-            y_sb = ring.tile([P, width], F32, name="y_sb", align_bytes=64)
+            y_ps = bank_tile("%d_%d_%d" % pieces[0], "y", (P, width))
             starts = [sum(P * (k1 - k0) for i, k0, k1 in pieces[:n]) for n in range(len(pieces))]
             for at, (i, k0, k1) in zip(starts, pieces):
                 for k in range(k0, k1, 2):
@@ -330,10 +369,20 @@ def tile_list_skill_disagreement_marks_kernel(
                         start=True,
                         stop=True,
                     )
-            for at, (i, k0, k1) in zip(starts, pieces):
+            return y_ps, list(zip(starts, pieces))
+
+        def less_usual(made):
+            y_ps, pieces = made
+            y_sb = ring.tile(list(y_ps.shape), F32, name="y_sb", align_bytes=64)
+            for at, (i, k0, k1) in pieces:
                 col = slice(at, at + P * (k1 - k0))
                 nc.scalar.activation(y_sb[:, col], y_ps[:, col], ACT.Identity, bias=neg_usual[:, i : i + 1])
-            for at, (i, k0, k1) in zip(starts, pieces):
+            give_back("%d_%d_%d" % pieces[0][1], "y")
+            return y_sb, pieces
+
+        def scatter(made):
+            y_sb, pieces = made
+            for at, (i, k0, k1) in pieces:
                 j0, j1 = P * k0, P * k1
                 nc.vector.tensor_tensor(
                     pages[i][:].indirect(offs2_sb[:, j0 // 16 : j1 // 16]),
@@ -347,48 +396,125 @@ def tile_list_skill_disagreement_marks_kernel(
                     for queue, c0 in ((nc.sync, 0), (nc.scalar, T2 // 2)):
                         queue.dma_start(rows[i][:, c0 : c0 + T2 // 2], pages[i][:, c0 : c0 + T2 // 2])
 
-        nc.scalar.activation(*walk(1, 0, SCALAR_COLS), ACT.Copy, scale=-1.0)
-        nc.vector.tensor_scalar(*walk(1, SCALAR_COLS, H), -1.0, 0.0, ALU.mult, ALU.add)
-        quantise_wb(1)
-        first_part(0)
-        first_part(1)
-        second_part(0)
-        first_part(2)
-        second_part(1)
-        prepare_wd(0, 2)
-        second_part(2)
+        def place(pieces):
+            scatter(less_usual(marks(pieces)))
+
+        def to_h(k):
+            turn(k)
+            round_h(k)
+            quantise_h(k)
+
+        for k in range(3):
+            begin(k, "nb", [(0, neg_wb_mx)])
+        product(0, "c", wc_mx)
+        copy_out(0, "c")
+        product(1, "c", wc_mx)
+        copy_out(1, "c")
+        product(0, "a", wa_mx)
+        finish(0, "nb", [(1, neg_wb_mx)])
+        make_d(0)
+        make_u(0)
+        relu(0, "d")
+        product(1, "a", wa_mx)
+        finish(1, "nb", [(1, neg_wb_mx)])
+        make_d(1)
+        relu(0, "u")
+        make_top(0)
+        product(2, "c", wc_mx)
+        copy_out(2, "c")
+        make_u(1)
+        product(2, "a", wa_mx)
+        finish(2, "nb", [(1, neg_wb_mx)])
+        round_wd(0)
         turn(0)
-        prepare_wd(2, 4)
-        first_part(3)
-        second_part(3)
+        make_d(2)
+        make_top(1)
+        round_h(0)
+        relu(1, "d")
+        relu(1, "u")
+        make_u(2)
+        quantise_wd(0)
+        product(3, "c", wc_mx)
+        product(3, "a", wa_mx)
+        product(3, "nb", neg_wb_mx)
+        quantise_h(0)
+        make_top(2)
+        made = less_usual(marks([(0, 0, 1), (1, 0, 1)]))
+        copy_out(3, "c")
         turn(1)
-        place([(0, 0, 1), (1, 0, 1)])
-        first_part(4)
-        second_part(4)
+        round_wd(2)
+        scatter(made)
+        round_h(1)
+        quantise_wd(2)
+        make_d(3)
+        make_u(3)
+        quantise_h(1)
+        make_top(3)
+        relu(2, "d")
+        relu(2, "u")
+        mostly_less_b(4, "d", wc_mx)
+        rest_of_b(4)
+        mostly_less_b(4, "u", wa_mx)
+        place([(2, 0, 1), (3, 0, 1)])
+        copy_out(4, "d")
+        relu_shared(4)
         turn(2)
-        place([(2, 0, 2), (3, 0, 2)])
-        row_part(6, 0)
-        first_part(5)
-        row_part(6, 1)
+        round_h(2)
+        made = less_usual(marks([(i, 1, 2) for i in range(4)]))
+        mend_rest(4)
+        quantise_h(2)
+        top_of_rest(4)
+        scatter(made)
+        product(5, "d", wc_mx, neg_wb_mx)
+        product(5, "u", wa_mx, neg_wb_mx)
+        relu(3, "d")
+        relu(3, "u")
         turn(3)
-        place([(0, 1, 3), (1, 1, 3)])
-        second_part(5)
-        row_part(6, 2)
+        relu_rest(4)
+        copy_out(5, "d")
+        relu(5, "d")
+        round_h(3)
+        relu(5, "u")
+        made = less_usual(marks([(i, 2, 3) for i in range(4)]))
+        quantise_h(3)
+        make_top(5)
+        scatter(made)
+        product(6, "d", wc_mx, neg_wb_mx)
         turn(4)
-        row_part(7, 0)
-        place([(2, 2, 4), (3, 2, 4)])
-        first_part(6)
-        second_part(6)
-        row_part(7, 1)
-        row_part(7, 2)
+        round_h(4)
+        product(6, "u", wa_mx, neg_wb_mx)
+        copy_out(6, "d")
+        relu(6, "d")
+        relu(6, "u")
+        made = less_usual(marks([(i, 3, 4) for i in range(4)]))
+        quantise_h(4)
+        make_top(6)
+        scatter(made)
         turn(5)
-        place([(0, 3, 5), (1, 3, 5)])
-        first_part(7)
-        second_part(7)
+        round_h(5)
+        for name, weight in (("nb", neg_wb_mx), ("c", wc_mx), ("a", wa_mx)):
+            by_rows(7, name, weight)
+            copy_rows(7, name)
+        made = marks([(i, 4, 5) for i in range(3)])
+        turned_sum(7, "d", "nb", "c")
+        turned_sum(7, "u", "nb", "a")
+        copy_out(7, "d")
+        relu(7, "u")
+        made = less_usual(made)
+        quantise_h(5)
+        make_top(7)
+        scatter(made)
         turn(6)
-        place([(2, 4, 6), (1, 5, 6)])
+        relu(7, "d")
+        round_h(6)
+        made = less_usual(marks([(1, 5, 6), (2, 5, 6)]))
         turn(7)
-        place([(0, 5, 7)])
+        quantise_h(6)
+        scatter(made)
+        round_h(7)
+        made = less_usual(marks([(0, 5, 7)]))
+        quantise_h(7)
+        scatter(made)
         place([(0, 7, 8), (1, 6, 8)])
         place([(2, 6, 8)])
         place([(3, 4, 8)])

@@ -22,21 +22,27 @@ TILES = S // P
 SHARED = 3 * H // 4
 ROW = S + 2 * H
 EDGE = 64
-SCALAR_COLS = 352
+SCALAR_COLS = 192
 BANKS, BANK_BYTES = 8, 2048
 MOSTLY = 4
 DEPTH = 4
 
-AT_WB_BF0 = 0
-AT_TAB_SC = AT_WB_BF0 + 8 * H - EDGE
-AT_PAGE3 = AT_TAB_SC + T - EDGE
-AT_GATHERED = AT_PAGE3 + 4 * T2
-AT_WB_BF1 = AT_GATHERED + S - EDGE
-AT_WGO = AT_WB_BF1 + 8 * H
-AT_STAGED = AT_WGO + 4 * S - EDGE
+AT_TAB1 = 0
+AT_TAB_SC = AT_TAB1 + 4 * T - EDGE
+AT_TAB0 = AT_TAB_SC + T
+AT_PAGE1 = AT_TAB0 + 4 * T - EDGE
+AT_PAGE2 = AT_PAGE1 + 4 * T2
+AT_WB_BF1 = AT_PAGE2 + 4 * T2 - EDGE
+AT_PAGE3 = AT_WB_BF1 + 8 * H - EDGE
+AT_WB1 = AT_PAGE3 + 4 * T2
+AT_GATHERED = AT_WB1 + 16 * H - EDGE
+AT_WC = AT_GATHERED + S - EDGE
+AT_WA = AT_WC + 8 * H
+AT_STAGED = AT_WA + 4 * H - EDGE
 AT_WD = AT_STAGED + 2 * ROW - EDGE
 AT_H0 = AT_WD + 16 * N
 AT_WD_BF1 = AT_H0 + 8 * P - EDGE
+AT_WGO = AT_TAB1
 LAST_FIRST = (("ru", "rd", "top"), ("rd", "ru", "top"), ("top", "ru", "rd"))
 
 
@@ -84,36 +90,29 @@ def tile_list_skill_disagreement_marks_kernel(
         nc.sync.dma_start(usual_sb[:], usual.rearrange("(p i) -> p i", i=4))
         nc.sync.dma_start(tab_sc[0:P:4, :].bitcast(I32), tab_scales.bitcast(I32).rearrange("a q t -> q a t"))
 
-        tab_w = [held([P, T], I32, "tab_w%d" % a) for a in range(2)]
+        tab_w = [placed([P, T], I32, "tab_w0", AT_TAB0), placed([P, T], I32, "tab_w1", AT_TAB1)]
         wb_rows = wb.rearrange("(a p j) c -> a p (j c)", a=2, j=4)
-        wb_raw = [held([P, 4 * H], F32, "wb_raw%d" % a)[:] for a in range(2)]
+        wb_raw = [held([P, 4 * H], F32, "wb_raw0")[:], placed([P, 4 * H], F32, "wb_raw1", AT_WB1)[:]]
 
         def load_words(a):
             nc.sync.dma_start(tab_w[a][:], tab_words[a].rearrange("p t i -> p (t i)").bitcast(I32))
 
-        nc.sync.dma_start(wb_raw[0], wb_rows[0])
         load_words(0)
-        load_words(1)
-        nc.sync.dma_start(wb_raw[1], wb_rows[1])
-        wc_sb = held([P, 2, H], I32, "wc_sb")
-        nc.sync.dma_start(wc_sb[:], wc_words.rearrange("a p e i -> p a (e i)").bitcast(I32))
-        wa_sb = held([P, 2, H // 2], I32, "wa_sb")
-        nc.sync.dma_start(wa_sb[:], wa_words.rearrange("a p n -> p a n").bitcast(I32))
+        nc.sync.dma_start(wb_raw[0], wb_rows[0])
 
-        pages = [held([P, T2], F32, "page%d" % i) for i in range(3)]
-        pages.append(placed([P, T2], F32, "page3", AT_PAGE3))
+        pages = [held([P, T2], F32, "page0")]
+        pages.extend(placed([P, T2], F32, "page%d" % (i + 1), at) for i, at in enumerate((AT_PAGE1, AT_PAGE2, AT_PAGE3)))
 
-        def clear(i):
-            nc.vector.memset(pages[i][:].bitcast(I32), 0)
+        def clear(engine, i):
+            engine.memset(pages[i][:].bitcast(I32), 0)
 
         ident = held([P, P], F32, "ident")
         make_identity(nc, ident[:])
-        clear(0)
-        clear(1)
+        clear(nc.vector, 0)
         neg_usual = held([P, 4], F32, "neg_usual")
         nc.scalar.activation(neg_usual[:], usual_sb[:], ACT.Identity, scale=-1.0)
 
-        neg_wb_bf = [placed([P, 4 * H], BF16, "neg_wb_bf%d" % a, at) for a, at in enumerate((AT_WB_BF0, AT_WB_BF1))]
+        neg_wb_bf = [held([P, 4 * H], BF16, "neg_wb_bf0"), placed([P, 4 * H], BF16, "neg_wb_bf1", AT_WB_BF1)]
         neg_wb_q = [held([P, H], U32, "neg_wb_q%d" % a) for a in range(2)]
         neg_wb_sc = [held([P, H], U8, "neg_wb_sc%d" % a) for a in range(2)]
 
@@ -135,26 +134,33 @@ def tile_list_skill_disagreement_marks_kernel(
 
         gathered_sc = placed([P, S], U8, "gathered_sc", AT_GATHERED)
         nc.vector.tensor_copy(gathered_sc[:], tab_sc[:].indirect(offs_sb[:]))
-        nc.scalar.dma_start(staged[0:P:8, ROW : ROW + S].bitcast(I32), gathered_sc[4:P:8, :].bitcast(I32))
+        nc.sync.dma_start(staged[0:P:8, ROW : ROW + S].bitcast(I32), gathered_sc[4:P:8, :].bitcast(I32))
+        load_words(1)
         nc.scalar.activation(*walk(0, 0, H), ACT.Copy, scale=-1.0)
-        clear(2)
         nc.vector.tensor_copy(staged[:, :S].bitcast(I32), gathered_sc[:].bitcast(I32))
-        clear(3)
         for r in range(4):
-            nc.scalar.dma_start(plane[r:P:32, :].bitcast(I32), staged[8 * r : P : 32, :].bitcast(I32))
+            nc.sync.dma_start(plane[r:P:32, :].bitcast(I32), staged[8 * r : P : 32, :].bitcast(I32))
 
+        nc.sync.dma_start(wb_raw[1], wb_rows[1])
+        wc_sb = placed([P, 2, H], I32, "wc_sb", AT_WC)
+        nc.sync.dma_start(wc_sb[:], wc_words.rearrange("a p e i -> p a (e i)").bitcast(I32))
+        wa_sb = placed([P, 2, H // 2], I32, "wa_sb", AT_WA)
+        nc.sync.dma_start(wa_sb[:], wa_words.rearrange("a p n -> p a n").bitcast(I32))
         wd_raw = placed([P, 4 * N], F32, "wd_raw", AT_WD)[:]
         nc.sync.dma_start(wd_raw, wd.rearrange("(p j) c -> p (j c)", j=4))
-        wgo_sb = placed([P, S], F32, "wgo_sb", AT_WGO)[:]
-        nc.sync.dma_start(wgo_sb, wgo)
 
         gather_words(0, 0, S)
+        clear(nc.vector, 1)
         quantise_wb(0)
         gather_words(1, 0, S // 2)
         gather_words(1, S // 2, S)
+        wgo_sb = placed([P, S], F32, "wgo_sb", AT_WGO)[:]
+        nc.sync.dma_start(wgo_sb, wgo)
         nc.scalar.activation(*walk(1, 0, SCALAR_COLS), ACT.Copy, scale=-1.0)
         nc.vector.tensor_scalar(*walk(1, SCALAR_COLS, H), -1.0, 0.0, ALU.mult, ALU.add)
         quantise_wb(1)
+        clear(nc.gpsimd, 2)
+        clear(nc.gpsimd, 3)
 
         def wc_mx(a, c0=0, c1=H):
             return wc_sb[:, a, c0:c1].bitcast(FP8X4), plane[:, ROW * a + S + c0 : ROW * a + S + c1]

@@ -22,28 +22,25 @@ TILES = S // P
 SHARED = 3 * H // 4
 ROW = S + 2 * H
 EDGE = 64
-SCALAR_COLS = 192
-BANKS, BANK_BYTES = 8, 2048
-MOSTLY = 4
+BANKS = {"mm": 4, "h": 2, "y": 2}
+PLAIN = 3
+TURNED = 6
+AHEAD = 3
 DEPTH = 4
 
 AT_TAB1 = 0
 AT_TAB_SC = AT_TAB1 + 4 * T - EDGE
-AT_TAB0 = AT_TAB_SC + T
+AT_WA = AT_TAB_SC + T - EDGE
+AT_TAB0 = AT_WA + 4 * H
 AT_PAGE1 = AT_TAB0 + 4 * T - EDGE
 AT_PAGE2 = AT_PAGE1 + 4 * T2
 AT_WB_BF1 = AT_PAGE2 + 4 * T2 - EDGE
 AT_PAGE3 = AT_WB_BF1 + 8 * H - EDGE
-AT_WB1 = AT_PAGE3 + 4 * T2
+AT_WGO = AT_PAGE3 + 4 * T2
+AT_WB1 = AT_WGO + 4 * S - EDGE
+AT_BEHIND_CAST = AT_WB1 + EDGE
 AT_GATHERED = AT_WB1 + 16 * H - EDGE
-AT_WC = AT_GATHERED + S - EDGE
-AT_WA = AT_WC + 8 * H
-AT_STAGED = AT_WA + 4 * H - EDGE
-AT_WD = AT_STAGED + 2 * ROW - EDGE
-AT_H0 = AT_WD + 16 * N
-AT_WD_BF1 = AT_H0 + 8 * P - EDGE
-AT_WGO = AT_TAB1
-LAST_FIRST = (("ru", "rd", "top"), ("rd", "ru", "top"), ("top", "ru", "rd"))
+AT_WD = AT_GATHERED + S - EDGE
 
 
 def tile_list_skill_disagreement_marks_kernel(
@@ -55,7 +52,7 @@ def tile_list_skill_disagreement_marks_kernel(
         keep = ctx.enter_context(tc.tile_pool(name="keep", bufs=1))
         ring = ctx.enter_context(tc.tile_pool(name="ring", bufs=DEPTH))
         arena = ctx.enter_context(tc.tile_pool(name="arena", bufs=1))
-        psum = ctx.enter_context(tc.psum_pool(name="psum", bufs=1))
+        psum = ctx.enter_context(tc.psum_pool(name="psum", bufs=2))
 
         def placed(shape, dtype, name, offset):
             return arena.tile(shape, dtype, name=name, offset=offset, align_bytes=64)
@@ -71,7 +68,7 @@ def tile_list_skill_disagreement_marks_kernel(
         tab_sc = placed([P, T], U8, "tab_sc", AT_TAB_SC)
         nc.vector.memset(tab_sc[:].bitcast(I32), 0)
         plane = held([P, 2 * ROW], U8, "plane")
-        staged = placed([P, 2 * ROW], U8, "staged", AT_STAGED)
+        staged = held([P, 2 * ROW], U8, "staged")
         zero = held([P, 1], U32, "zero")
         nc.vector.memset(zero[:], 0)
         nc.scalar.copy(plane[:].bitcast(U32), zero[:].to_broadcast([P, 2 * ROW // 4]))
@@ -99,6 +96,8 @@ def tile_list_skill_disagreement_marks_kernel(
 
         load_words(0)
         nc.sync.dma_start(wb_raw[0], wb_rows[0])
+        wc_sb = held([P, 2, H], I32, "wc_sb")
+        nc.sync.dma_start(wc_sb[:], wc_words.rearrange("a p e i -> p a (e i)").bitcast(I32))
 
         pages = [held([P, T2], F32, "page0")]
         pages.extend(placed([P, T2], F32, "page%d" % (i + 1), at) for i, at in enumerate((AT_PAGE1, AT_PAGE2, AT_PAGE3)))
@@ -136,29 +135,26 @@ def tile_list_skill_disagreement_marks_kernel(
         nc.vector.tensor_copy(gathered_sc[:], tab_sc[:].indirect(offs_sb[:]))
         nc.sync.dma_start(staged[0:P:8, ROW : ROW + S].bitcast(I32), gathered_sc[4:P:8, :].bitcast(I32))
         load_words(1)
+        wa_sb = placed([P, 2, H // 2], I32, "wa_sb", AT_WA)
+        nc.sync.dma_start(wa_sb[:], wa_words.rearrange("a p n -> p a n").bitcast(I32))
         nc.scalar.activation(*walk(0, 0, H), ACT.Copy, scale=-1.0)
         nc.vector.tensor_copy(staged[:, :S].bitcast(I32), gathered_sc[:].bitcast(I32))
         for r in range(4):
             nc.sync.dma_start(plane[r:P:32, :].bitcast(I32), staged[8 * r : P : 32, :].bitcast(I32))
 
         nc.sync.dma_start(wb_raw[1], wb_rows[1])
-        wc_sb = placed([P, 2, H], I32, "wc_sb", AT_WC)
-        nc.sync.dma_start(wc_sb[:], wc_words.rearrange("a p e i -> p a (e i)").bitcast(I32))
-        wa_sb = placed([P, 2, H // 2], I32, "wa_sb", AT_WA)
-        nc.sync.dma_start(wa_sb[:], wa_words.rearrange("a p n -> p a n").bitcast(I32))
         wd_raw = placed([P, 4 * N], F32, "wd_raw", AT_WD)[:]
         nc.sync.dma_start(wd_raw, wd.rearrange("(p j) c -> p (j c)", j=4))
 
         gather_words(0, 0, S)
         clear(nc.vector, 1)
+        gather_words(1, 0, AHEAD * P)
         quantise_wb(0)
-        gather_words(1, 0, S // 2)
-        gather_words(1, S // 2, S)
+        gather_words(1, AHEAD * P, S)
+        nc.vector.tensor_scalar(*walk(1, 0, H), -1.0, 0.0, ALU.mult, ALU.add)
+        quantise_wb(1)
         wgo_sb = placed([P, S], F32, "wgo_sb", AT_WGO)[:]
         nc.sync.dma_start(wgo_sb, wgo)
-        nc.scalar.activation(*walk(1, 0, SCALAR_COLS), ACT.Copy, scale=-1.0)
-        nc.vector.tensor_scalar(*walk(1, SCALAR_COLS, H), -1.0, 0.0, ALU.mult, ALU.add)
-        quantise_wb(1)
         clear(nc.gpsimd, 2)
         clear(nc.gpsimd, 3)
 
@@ -172,10 +168,7 @@ def tile_list_skill_disagreement_marks_kernel(
             return neg_wb_q[a][:, c0:c1].bitcast(FP8X4), neg_wb_sc[a][:, c0:c1]
 
         def picked_mx(a, k):
-            return (
-                picked_words[a][:, P * k : P * (k + 1)].bitcast(FP8X4),
-                plane[:, ROW * a + P * k : ROW * a + P * (k + 1)],
-            )
+            return picked_words[a][:, P * k : P * (k + 1)].bitcast(FP8X4), plane[:, ROW * a + P * k : ROW * a + P * (k + 1)]
 
         def mx_pass(acc, stationary, moving, start, stop):
             nc.tensor.matmul_mx(
@@ -183,17 +176,49 @@ def tile_list_skill_disagreement_marks_kernel(
                 start=start, stop=stop,
             )
 
-        free_banks, bank_of = list(range(BANKS)), {}
-
-        def bank_tile(k, name, shape=(P, H)):
-            bank_of[k, name] = free_banks.pop(0)
-            return psum.tile(list(shape), F32, name="%s_%s" % (name, k), offset=BANK_BYTES * bank_of[k, name])
-
-        def give_back(k, name):
-            free_banks.append(bank_of.pop((k, name)))
+        def bank_tile(bank):
+            return psum.tile([P, H], F32, name="acc", tag=bank, bufs=BANKS[bank])
 
         def by_slot(acc):
             return acc[:].rearrange("p (m t) -> p t m", t=4)
+
+        def product(k, bank, *weights):
+            acc = bank_tile(bank)
+            passes = [(a, weight) for weight in weights for a in range(2)]
+            for n, (a, weight) in enumerate(passes):
+                mx_pass(acc[:], picked_mx(a, k), weight(a), n == 0, n == len(passes) - 1)
+            return by_slot(acc)
+
+        def mostly_less_b(k, weight):
+            acc = bank_tile("mm")
+            for a in range(2):
+                mx_pass(acc[:], picked_mx(a, k), weight(a), a == 0, False)
+            for c0, c1 in ((0, H // 2), (H // 2, SHARED)):
+                for a in range(2):
+                    mx_pass(acc[:, c0:c1], picked_mx(a, k), neg_wb_mx(a, c0, c1), False, a == 1 and c1 == SHARED)
+            return by_slot(acc)
+
+        def product_by_rows(k, weight, name):
+            acc = bank_tile("mm")
+            for a in range(2):
+                for i in range(4):
+                    mx_pass(
+                        acc[:, P * i : P * (i + 1)], weight(a, P * i, P * (i + 1)), picked_mx(a, k),
+                        a == 0 and i == 0, a == 1 and i == 3,
+                    )
+            rows_sb = term(name)
+            nc.scalar.copy(rows_sb[:], acc[:])
+            return rows_sb
+
+        def turned_sum(first, second):
+            acc = bank_tile("mm")
+            for e, rows_sb in enumerate((first, second)):
+                for i in range(4):
+                    nc.tensor.matmul(
+                        acc[:, P * i : P * (i + 1)], rows_sb[:, P * i : P * (i + 1)], ident[:],
+                        start=(e == 0 and i == 0), stop=(e == 1 and i == 3), is_transpose=True,
+                    )
+            return by_slot(acc)
 
         def slots(ap):
             return ap.rearrange("p (t m) -> p t m", t=4)
@@ -201,167 +226,105 @@ def tile_list_skill_disagreement_marks_kernel(
         def relu_neg(dst, src):
             nc.scalar.activation(dst, src, ACT.Relu, scale=-1.0)
 
-        sums, open_sums, sb = {}, {}, {}
+        c_sb, d_sb, summands, by_rows = {}, {}, {}, {}
 
-        def begin(k, name, passes):
-            open_sums[k, name] = bank_tile(k, name)
-            for n, (a, weight) in enumerate(passes):
-                mx_pass(open_sums[k, name][:], picked_mx(a, k), weight(a), n == 0, False)
+        def take_d(k, d_ps):
+            d_sb[k], rd = term("d"), term("rd")
+            nc.scalar.copy(slots(d_sb[k][:]), d_ps)
+            relu_neg(slots(rd[:]), d_ps)
+            summands[k] = [rd]
 
-        def finish(k, name, passes):
-            acc = open_sums.pop((k, name))
-            for n, (a, weight) in enumerate(passes):
-                mx_pass(acc[:], picked_mx(a, k), weight(a), False, n == len(passes) - 1)
-            sums[k, name] = by_slot(acc)
+        def row_part(k, n):
+            weight, name = ((neg_wb_mx, "nb"), (wc_mx, "c"), (wa_mx, "u"))[n]
+            by_rows.setdefault(k, []).append(product_by_rows(k, weight, name))
 
-        def product(k, name, *weights):
-            passes = [(a, weight) for weight in weights for a in range(2)]
-            begin(k, name, passes[:1])
-            finish(k, name, passes[1:])
+        def first_part(k):
+            if k < PLAIN:
+                bank = "h" if k == AHEAD - 1 else "mm"
+                c_sb[k] = term("c")
+                d_sb[k] = placed([P, H], F32, "d%d" % k, AT_BEHIND_CAST + 4 * H * (k - 1)) if k else term("d")
+                rd = term("rd")
+                nc.scalar.copy(slots(c_sb[k][:]), product(k, bank, wc_mx))
+                nc.vector.tensor_tensor(slots(d_sb[k][:]), slots(c_sb[k][:]), product(k, bank, wa_mx), ALU.subtract)
+                relu_neg(rd[:], d_sb[k][:])
+                summands[k] = [rd]
+            elif k == PLAIN:
+                d_sb[k] = term("d")
+                nc.scalar.copy(slots(d_sb[k][:]), mostly_less_b(k, wc_mx))
+            elif k >= TURNED:
+                take_d(k, turned_sum(by_rows[k][0], by_rows[k][1]))
+            else:
+                take_d(k, product(k, "mm", wc_mx, neg_wb_mx))
 
-        def mostly_less_b(k, name, weight):
-            acc = bank_tile(k, name)
-            for a in range(2):
-                mx_pass(acc[:], picked_mx(a, k), weight(a), a == 0, False)
-            for c0, c1 in ((0, H // 2), (H // 2, SHARED)):
+        def second_part(k):
+            ru, top = term("ru"), term("top")
+            if k < PLAIN:
+                u = term("u")
+                nc.vector.tensor_tensor(slots(u[:]), product(k, "y" if k < AHEAD - 1 else "mm", neg_wb_mx), slots(c_sb[k][:]), ALU.add)
+                relu_neg(ru[:], u[:])
+                nc.vector.tensor_tensor(top[:], u[:], d_sb[k][:], ALU.max)
+            elif k == PLAIN:
+                cut = SHARED // 4
+                rest = bank_tile("mm")
                 for a in range(2):
-                    mx_pass(acc[:, c0:c1], picked_mx(a, k), neg_wb_mx(a, c0, c1), False, a == 1 and c1 == SHARED)
-            sums[k, name] = by_slot(acc)
-
-        def rest_of_b(k):
-            rest = bank_tile(k, "nb")
-            for a in range(2):
-                mx_pass(rest[:, SHARED:], picked_mx(a, k), neg_wb_mx(a, SHARED, H), a == 0, a == 1)
-            sums[k, "nb"] = by_slot(rest)
-
-        def by_rows(k, name, weight):
-            acc = open_sums[k, name] = bank_tile(k, name)
-            for a in range(2):
-                for i in range(4):
-                    mx_pass(
-                        acc[:, P * i : P * (i + 1)], weight(a, P * i, P * (i + 1)), picked_mx(a, k),
-                        a == 0 and i == 0, a == 1 and i == 3,
-                    )
-
-        def copy_rows(k, name):
-            sb[k, name + "_rows"] = term("rows")
-            nc.scalar.copy(sb[k, name + "_rows"][:], open_sums.pop((k, name))[:])
-            give_back(k, name)
-
-        def turned_sum(k, name, first, second):
-            acc = bank_tile(k, name)
-            for e, part in enumerate((first, second)):
-                for i in range(4):
-                    nc.tensor.matmul(
-                        acc[:, P * i : P * (i + 1)], sb[k, part + "_rows"][:, P * i : P * (i + 1)], ident[:],
-                        start=(e == 0 and i == 0), stop=(e == 1 and i == 3), is_transpose=True,
-                    )
-            sums[k, name] = by_slot(acc)
-
-        def copy_out(k, name):
-            sb[k, name] = term(name)
-            nc.scalar.copy(slots(sb[k, name][:]), sums[k, name])
-            if name == "c" or k == MOSTLY:
-                give_back(k, name)
-
-        def make_d(k):
-            sb[k, "d"] = term("d")
-            nc.vector.tensor_tensor(slots(sb[k, "d"][:]), slots(sb[k, "c"][:]), sums[k, "a"], ALU.subtract)
-            give_back(k, "a")
-
-        def make_u(k):
-            sb[k, "u"] = term("u")
-            nc.vector.tensor_tensor(slots(sb[k, "u"][:]), sums[k, "nb"], slots(sb[k, "c"][:]), ALU.add)
-            give_back(k, "nb")
-
-        def relu(k, name):
-            sb[k, "r" + name] = term("r" + name)
-            src = sums[k, name] if (k, name) in sums else slots(sb[k, name][:])
-            relu_neg(slots(sb[k, "r" + name][:]), src)
-            if name == "d" and (k, name) in sums:
-                give_back(k, name)
-
-        def make_top(k):
-            sb[k, "top"] = term("top")
-            u = slots(sb[k, "u"][:]) if (k, "u") in sb else sums[k, "u"]
-            nc.vector.tensor_tensor(slots(sb[k, "top"][:]), u, slots(sb[k, "d"][:]), ALU.max)
-            if (k, "u") in sums:
-                give_back(k, "u")
-
-        cut = SHARED // 4
-
-        def relu_shared(k):
-            sb[k, "ru"] = term("ru")
-            relu_neg(slots(sb[k, "ru"][:])[:, :, :cut], sums[k, "u"][:, :, :cut])
-
-        def mend_rest(k):
-            sb[k, "top"], sb[k, "u"] = term("top"), term("u")
-            d, u, top = slots(sb[k, "d"][:]), slots(sb[k, "u"][:]), slots(sb[k, "top"][:])
-            nc.vector.tensor_tensor(u[:, :, cut:], sums[k, "nb"][:, :, cut:], d[:, :, cut:], ALU.add)
-            nc.vector.tensor_tensor(top[:, :, :cut], sums[k, "u"][:, :, :cut], d[:, :, :cut], ALU.max)
-            nc.vector.tensor_tensor(d[:, :, cut:], d[:, :, cut:], sums[k, "u"][:, :, cut:], ALU.subtract)
-            give_back(k, "nb")
-            give_back(k, "u")
-
-        def top_of_rest(k):
-            d, u, top = slots(sb[k, "d"][:]), slots(sb[k, "u"][:]), slots(sb[k, "top"][:])
-            nc.vector.tensor_tensor(top[:, :, cut:], u[:, :, cut:], d[:, :, cut:], ALU.max)
-
-        def relu_rest(k):
-            sb[k, "rd"] = term("rd")
-            relu_neg(slots(sb[k, "ru"][:])[:, :, cut:], slots(sb[k, "u"][:])[:, :, cut:])
-            relu_neg(sb[k, "rd"][:], sb[k, "d"][:])
+                    mx_pass(rest[:, SHARED:], picked_mx(a, k), neg_wb_mx(a, SHARED, H), a == 0, a == 1)
+                u_ps = mostly_less_b(k, wa_mx)
+                d, u, rd = slots(d_sb[k][:]), slots(term("u")[:]), term("rd")
+                nc.vector.tensor_tensor(u[:, :, cut:], by_slot(rest)[:, :, cut:], d[:, :, cut:], ALU.add)
+                nc.vector.tensor_tensor(d[:, :, cut:], d[:, :, cut:], u_ps[:, :, cut:], ALU.subtract)
+                relu_neg(slots(ru[:])[:, :, :cut], u_ps[:, :, :cut])
+                relu_neg(slots(ru[:])[:, :, cut:], u[:, :, cut:])
+                relu_neg(rd[:], d_sb[k][:])
+                nc.vector.tensor_tensor(slots(top[:])[:, :, :cut], u_ps[:, :, :cut], d[:, :, :cut], ALU.max)
+                nc.vector.tensor_tensor(slots(top[:])[:, :, cut:], u[:, :, cut:], d[:, :, cut:], ALU.max)
+                summands[k] = [rd]
+            else:
+                if k >= TURNED:
+                    u_ps = turned_sum(by_rows[k][0], by_rows[k][2])
+                else:
+                    u_ps = product(k, "mm", wa_mx, neg_wb_mx)
+                relu_neg(slots(ru[:]), u_ps)
+                nc.vector.tensor_tensor(slots(top[:]), u_ps, slots(d_sb[k][:]), ALU.max)
+            summands[k].extend([ru, top])
 
         h_q = held([P, S], U32, "h_q")
         h_sc = held([P, S], U8, "h_sc")
-        h_ps, h_bf = {}, {}
 
         def turn(k):
-            h_ps[k] = bank_tile(k, "h", (P, 4, P))
-            for e, name in enumerate(LAST_FIRST[k == MOSTLY or (2 if k > MOSTLY else 0)]):
+            h_ps = psum.tile([P, 4, P], F32, name="h_ps", tag="h", bufs=BANKS["h"])
+            for e, summand in enumerate(summands[k]):
                 for t in range(4):
                     nc.tensor.matmul(
-                        h_ps[k][:, t, :], slots(sb[k, name][:])[:, t, :], ident[:],
+                        h_ps[:, t, :], slots(summand[:])[:, t, :], ident[:],
                         start=(e == 0 and t == 0), stop=(e == 2 and t == 3), is_transpose=True,
                     )
-
-        def round_h(k):
-            if k == 0:
-                h_bf[k] = placed([P, 4 * P], BF16, "h_bf0", AT_H0)
-            else:
-                h_bf[k] = ring.tile([P, 4 * P], BF16, name="h_bf", align_bytes=64)
-            nc.scalar.copy(h_bf[k][:].rearrange("p (j t) -> p j t", t=4), h_ps[k][:].rearrange("p t j -> p j t"))
-            give_back(k, "h")
-
-        def quantise_h(k):
+            h_bf = ring.tile([P, 4 * P], BF16, name="h_bf", align_bytes=64)
+            nc.scalar.copy(h_bf[:].rearrange("p (j t) -> p j t", t=4), h_ps[:].rearrange("p t j -> p j t"))
             nc.vector.quantize_mx(
-                out=h_q[:, P * k : P * (k + 1)].bitcast(FP8X4), scales=h_sc[:, P * k : P * (k + 1)], in_=h_bf[k][:]
+                out=h_q[:, P * k : P * (k + 1)].bitcast(FP8X4), scales=h_sc[:, P * k : P * (k + 1)], in_=h_bf[:]
             )
 
+        wd_bf = held([P, 4, P, 4], BF16, "wd_bf")
         wd_q = held([P, N], U32, "wd_q")
         wd_sc = held([P, N], U8, "wd_sc")
-        wd_bf = {}
 
-        def round_wd(i0):
-            shape = [P, 2, P, 4]
-            wd_bf[i0] = held(shape, BF16, "wd_bf0") if i0 == 0 else placed(shape, BF16, "wd_bf1", AT_WD_BF1)
+        def prepare_wd(i0, i1):
             nc.scalar.copy(
-                wd_bf[i0][:].rearrange("p i m j -> p m i j"),
-                wd_raw.rearrange("p (j m i) -> p m i j", j=4, i=4)[:, :, i0 : i0 + 2, :],
+                wd_bf[:, i0:i1].rearrange("p i m j -> p m i j"),
+                wd_raw.rearrange("p (j m i) -> p m i j", j=4, i=4)[:, :, i0:i1, :],
             )
-
-        def quantise_wd(i0):
             nc.vector.quantize_mx(
-                out=wd_q[:, P * i0 : P * (i0 + 2)].bitcast(FP8X4),
-                scales=wd_sc[:, P * i0 : P * (i0 + 2)],
-                in_=wd_bf[i0][:].rearrange("p i m j -> p (i m j)"),
+                out=wd_q[:, P * i0 : P * i1].bitcast(FP8X4),
+                scales=wd_sc[:, P * i0 : P * i1],
+                in_=wd_bf[:, i0:i1].rearrange("p i m j -> p (i m j)"),
             )
 
         rows = out.rearrange("(p i) t -> i p t", i=4)
 
-        def marks(pieces):
+        def place(pieces):
             width = sum(P * (k1 - k0) for i, k0, k1 in pieces)
-            y_ps = bank_tile("%d_%d_%d" % pieces[0], "y", (P, width))
+            y_ps = psum.tile([P, width], F32, name="y_ps", tag="y", bufs=BANKS["y"])
+            y_sb = ring.tile([P, width], F32, name="y_sb", align_bytes=64)
             starts = [sum(P * (k1 - k0) for i, k0, k1 in pieces[:n]) for n in range(len(pieces))]
             for at, (i, k0, k1) in zip(starts, pieces):
                 for k in range(k0, k1, 2):
@@ -375,20 +338,10 @@ def tile_list_skill_disagreement_marks_kernel(
                         start=True,
                         stop=True,
                     )
-            return y_ps, list(zip(starts, pieces))
-
-        def less_usual(made):
-            y_ps, pieces = made
-            y_sb = ring.tile(list(y_ps.shape), F32, name="y_sb", align_bytes=64)
-            for at, (i, k0, k1) in pieces:
+            for at, (i, k0, k1) in zip(starts, pieces):
                 col = slice(at, at + P * (k1 - k0))
                 nc.scalar.activation(y_sb[:, col], y_ps[:, col], ACT.Identity, bias=neg_usual[:, i : i + 1])
-            give_back("%d_%d_%d" % pieces[0][1], "y")
-            return y_sb, pieces
-
-        def scatter(made):
-            y_sb, pieces = made
-            for at, (i, k0, k1) in pieces:
+            for at, (i, k0, k1) in zip(starts, pieces):
                 j0, j1 = P * k0, P * k1
                 nc.vector.tensor_tensor(
                     pages[i][:].indirect(offs2_sb[:, j0 // 16 : j1 // 16]),
@@ -402,125 +355,45 @@ def tile_list_skill_disagreement_marks_kernel(
                     for queue, c0 in ((nc.sync, 0), (nc.scalar, T2 // 2)):
                         queue.dma_start(rows[i][:, c0 : c0 + T2 // 2], pages[i][:, c0 : c0 + T2 // 2])
 
-        def place(pieces):
-            scatter(less_usual(marks(pieces)))
-
-        def to_h(k):
-            turn(k)
-            round_h(k)
-            quantise_h(k)
-
-        for k in range(3):
-            begin(k, "nb", [(0, neg_wb_mx)])
-        product(0, "c", wc_mx)
-        copy_out(0, "c")
-        product(1, "c", wc_mx)
-        copy_out(1, "c")
-        product(0, "a", wa_mx)
-        finish(0, "nb", [(1, neg_wb_mx)])
-        make_d(0)
-        make_u(0)
-        relu(0, "d")
-        product(1, "a", wa_mx)
-        finish(1, "nb", [(1, neg_wb_mx)])
-        make_d(1)
-        relu(0, "u")
-        make_top(0)
-        product(2, "c", wc_mx)
-        copy_out(2, "c")
-        make_u(1)
-        product(2, "a", wa_mx)
-        finish(2, "nb", [(1, neg_wb_mx)])
-        round_wd(0)
+        first_part(0)
+        first_part(1)
+        first_part(2)
+        second_part(0)
+        second_part(1)
+        prepare_wd(0, 2)
+        second_part(2)
         turn(0)
-        make_d(2)
-        make_top(1)
-        round_h(0)
-        relu(1, "d")
-        relu(1, "u")
-        make_u(2)
-        quantise_wd(0)
-        product(3, "c", wc_mx)
-        product(3, "a", wa_mx)
-        product(3, "nb", neg_wb_mx)
-        quantise_h(0)
-        make_top(2)
-        made = less_usual(marks([(0, 0, 1), (1, 0, 1)]))
-        copy_out(3, "c")
+        prepare_wd(2, 4)
+        first_part(3)
+        second_part(3)
         turn(1)
-        round_wd(2)
-        scatter(made)
-        round_h(1)
-        quantise_wd(2)
-        make_d(3)
-        make_u(3)
-        quantise_h(1)
-        make_top(3)
-        relu(2, "d")
-        relu(2, "u")
-        mostly_less_b(4, "d", wc_mx)
-        rest_of_b(4)
-        mostly_less_b(4, "u", wa_mx)
-        place([(2, 0, 1), (3, 0, 1)])
-        copy_out(4, "d")
-        relu_shared(4)
+        place([(0, 0, 1), (1, 0, 1)])
+        first_part(4)
+        second_part(4)
         turn(2)
-        round_h(2)
-        made = less_usual(marks([(i, 1, 2) for i in range(4)]))
-        mend_rest(4)
-        quantise_h(2)
-        top_of_rest(4)
-        scatter(made)
-        product(5, "d", wc_mx, neg_wb_mx)
-        product(5, "u", wa_mx, neg_wb_mx)
-        relu(3, "d")
-        relu(3, "u")
+        place([(2, 0, 2), (3, 0, 2)])
+        row_part(6, 0)
+        first_part(5)
+        row_part(6, 1)
         turn(3)
-        relu_rest(4)
-        copy_out(5, "d")
-        relu(5, "d")
-        round_h(3)
-        relu(5, "u")
-        made = less_usual(marks([(i, 2, 3) for i in range(4)]))
-        quantise_h(3)
-        make_top(5)
-        scatter(made)
-        product(6, "d", wc_mx, neg_wb_mx)
+        place([(0, 1, 3), (1, 1, 3)])
+        second_part(5)
+        row_part(6, 2)
         turn(4)
-        round_h(4)
-        product(6, "u", wa_mx, neg_wb_mx)
-        copy_out(6, "d")
-        relu(6, "d")
-        relu(6, "u")
-        made = less_usual(marks([(i, 3, 4) for i in range(4)]))
-        quantise_h(4)
-        make_top(6)
-        scatter(made)
+        row_part(7, 0)
+        place([(2, 2, 4), (3, 2, 4)])
+        first_part(6)
+        second_part(6)
+        row_part(7, 1)
+        row_part(7, 2)
         turn(5)
-        round_h(5)
-        for name, weight in (("nb", neg_wb_mx), ("c", wc_mx), ("a", wa_mx)):
-            by_rows(7, name, weight)
-            copy_rows(7, name)
-        made = marks([(i, 4, 5) for i in range(3)])
-        turned_sum(7, "d", "nb", "c")
-        turned_sum(7, "u", "nb", "a")
-        copy_out(7, "d")
-        relu(7, "u")
-        made = less_usual(made)
-        quantise_h(5)
-        make_top(7)
-        scatter(made)
+        place([(0, 3, 5), (1, 3, 5)])
+        first_part(7)
+        second_part(7)
         turn(6)
-        relu(7, "d")
-        round_h(6)
-        made = less_usual(marks([(1, 5, 6), (2, 5, 6)]))
+        place([(2, 4, 6), (1, 5, 6)])
         turn(7)
-        quantise_h(6)
-        scatter(made)
-        round_h(7)
-        made = less_usual(marks([(0, 5, 7)]))
-        quantise_h(7)
-        scatter(made)
+        place([(0, 5, 7)])
         place([(0, 7, 8), (1, 6, 8)])
         place([(2, 6, 8)])
         place([(3, 4, 8)])

@@ -28,15 +28,14 @@ TURNED = 6
 AHEAD = 3
 DEPTH = 4
 
-AT_TAB1 = 0
+AT_PAGE3 = 0
+AT_TAB1 = AT_PAGE3 + 4 * T2 - EDGE
 AT_TAB_SC = AT_TAB1 + 4 * T - EDGE
 AT_WA = AT_TAB_SC + T - EDGE
-AT_TAB0 = AT_WA + 4 * H
+AT_PAGE2 = AT_WA + 4 * H
+AT_TAB0 = AT_PAGE2 + 4 * T2 - EDGE
 AT_PAGE1 = AT_TAB0 + 4 * T - EDGE
-AT_PAGE2 = AT_PAGE1 + 4 * T2
-AT_WB_BF1 = AT_PAGE2 + 4 * T2 - EDGE
-AT_PAGE3 = AT_WB_BF1 + 8 * H - EDGE
-AT_WGO = AT_PAGE3 + 4 * T2
+AT_WGO = AT_PAGE1 + 4 * T2
 AT_WB1 = AT_WGO + 4 * S - EDGE
 AT_BEHIND_CAST = AT_WB1 + EDGE
 AT_GATHERED = AT_WB1 + 16 * H - EDGE
@@ -102,16 +101,16 @@ def tile_list_skill_disagreement_marks_kernel(
         pages = [held([P, T2], F32, "page0")]
         pages.extend(placed([P, T2], F32, "page%d" % (i + 1), at) for i, at in enumerate((AT_PAGE1, AT_PAGE2, AT_PAGE3)))
 
-        def clear(engine, i):
-            engine.memset(pages[i][:].bitcast(I32), 0)
+        def clear(i):
+            nc.vector.memset(pages[i][:].bitcast(I32), 0)
 
         ident = held([P, P], F32, "ident")
         make_identity(nc, ident[:])
-        clear(nc.vector, 0)
+        clear(0)
         neg_usual = held([P, 4], F32, "neg_usual")
         nc.scalar.activation(neg_usual[:], usual_sb[:], ACT.Identity, scale=-1.0)
 
-        neg_wb_bf = [held([P, 4 * H], BF16, "neg_wb_bf0"), placed([P, 4 * H], BF16, "neg_wb_bf1", AT_WB_BF1)]
+        neg_wb_bf = [held([P, 4 * H], BF16, "neg_wb_bf%d" % a) for a in range(2)]
         neg_wb_q = [held([P, H], U32, "neg_wb_q%d" % a) for a in range(2)]
         neg_wb_sc = [held([P, H], U8, "neg_wb_sc%d" % a) for a in range(2)]
 
@@ -147,16 +146,16 @@ def tile_list_skill_disagreement_marks_kernel(
         nc.sync.dma_start(wd_raw, wd.rearrange("(p j) c -> p (j c)", j=4))
 
         gather_words(0, 0, S)
-        clear(nc.vector, 1)
+        clear(1)
+        clear(2)
         gather_words(1, 0, AHEAD * P)
         quantise_wb(0)
         gather_words(1, AHEAD * P, S)
+        clear(3)
         nc.vector.tensor_scalar(*walk(1, 0, H), -1.0, 0.0, ALU.mult, ALU.add)
         quantise_wb(1)
         wgo_sb = placed([P, S], F32, "wgo_sb", AT_WGO)[:]
         nc.sync.dma_start(wgo_sb, wgo)
-        clear(nc.gpsimd, 2)
-        clear(nc.gpsimd, 3)
 
         def wc_mx(a, c0=0, c1=H):
             return wc_sb[:, a, c0:c1].bitcast(FP8X4), plane[:, ROW * a + S + c0 : ROW * a + S + c1]

@@ -28,18 +28,20 @@ TURNED = 6
 AHEAD = 3
 DEPTH = 4
 
-AT_PAGE3 = 0
-AT_TAB1 = AT_PAGE3 + 4 * T2 - EDGE
-AT_TAB_SC = AT_TAB1 + 4 * T - EDGE
-AT_WA = AT_TAB_SC + T - EDGE
-AT_PAGE2 = AT_WA + 4 * H
+AT_PAGE2 = 0
 AT_TAB0 = AT_PAGE2 + 4 * T2 - EDGE
-AT_PAGE1 = AT_TAB0 + 4 * T - EDGE
-AT_WGO = AT_PAGE1 + 4 * T2
+AT_PAGE3 = AT_TAB0 + 4 * T - EDGE
+AT_WGO = AT_PAGE3 + 4 * T2
 AT_WB1 = AT_WGO + 4 * S - EDGE
 AT_BEHIND_CAST = AT_WB1 + EDGE
 AT_GATHERED = AT_WB1 + 16 * H - EDGE
-AT_WD = AT_GATHERED + S - EDGE
+GATHERED_BYTES = 4 * H + 2 * EDGE
+AT_TAB1 = AT_GATHERED + GATHERED_BYTES - EDGE
+AT_STAGED = AT_TAB1 + 4 * T
+AT_WD = AT_STAGED + ROW - EDGE
+AT_WA = AT_GATHERED + EDGE
+AT_TAB_SC = AT_WD + 16 * N
+AT_PICKED0 = AT_TAB_SC + T - EDGE
 
 
 def tile_list_skill_disagreement_marks_kernel(
@@ -66,16 +68,16 @@ def tile_list_skill_disagreement_marks_kernel(
         offs2_sb = lists.tile([P, S // 16], U16, name="offs2_sb")
         tab_sc = placed([P, T], U8, "tab_sc", AT_TAB_SC)
         nc.vector.memset(tab_sc[:].bitcast(I32), 0)
-        plane = held([P, 2 * ROW], U8, "plane")
-        staged = held([P, 2 * ROW], U8, "staged")
+        planes = [held([P, ROW], U8, "plane%d" % a) for a in range(2)]
+        staged = placed([P, ROW], U8, "staged", AT_STAGED)
         zero = held([P, 1], U32, "zero")
         nc.vector.memset(zero[:], 0)
-        nc.scalar.copy(plane[:].bitcast(U32), zero[:].to_broadcast([P, 2 * ROW // 4]))
+        for plane in planes:
+            nc.scalar.copy(plane[:].bitcast(U32), zero[:].to_broadcast([P, ROW // 4]))
 
         def load_weight_scales(c0, src):
             nc.sync.dma_start(
-                staged[0:P:8, :].bitcast(I32).rearrange("q (a c) -> q a c", a=2)[:, :, c0 // 4 : (c0 + H) // 4],
-                src.bitcast(I32).rearrange("a q t -> q a t"),
+                staged[0:P:4, c0 : c0 + H].bitcast(I32), src.bitcast(I32).rearrange("a q t -> q a t")
             )
 
         nc.sync.dma_start(offs_sb[:], offs)
@@ -98,8 +100,8 @@ def tile_list_skill_disagreement_marks_kernel(
         wc_sb = held([P, 2, H], I32, "wc_sb")
         nc.sync.dma_start(wc_sb[:], wc_words.rearrange("a p e i -> p a (e i)").bitcast(I32))
 
-        pages = [held([P, T2], F32, "page0")]
-        pages.extend(placed([P, T2], F32, "page%d" % (i + 1), at) for i, at in enumerate((AT_PAGE1, AT_PAGE2, AT_PAGE3)))
+        pages = [held([P, T2], F32, "page%d" % i) for i in range(2)]
+        pages.extend(placed([P, T2], F32, "page%d" % (i + 2), at) for i, at in enumerate((AT_PAGE2, AT_PAGE3)))
 
         def clear(i):
             nc.vector.memset(pages[i][:].bitcast(I32), 0)
@@ -107,6 +109,7 @@ def tile_list_skill_disagreement_marks_kernel(
         ident = held([P, P], F32, "ident")
         make_identity(nc, ident[:])
         clear(0)
+        clear(1)
         neg_usual = held([P, 4], F32, "neg_usual")
         nc.scalar.activation(neg_usual[:], usual_sb[:], ACT.Identity, scale=-1.0)
 
@@ -123,51 +126,55 @@ def tile_list_skill_disagreement_marks_kernel(
         def quantise_wb(a):
             nc.vector.quantize_mx(out=neg_wb_q[a][:].bitcast(FP8X4), scales=neg_wb_sc[a][:], in_=neg_wb_bf[a][:])
 
-        picked_words = [held([P, S], U32, "picked_words%d" % a) for a in range(2)]
+        picked_words = [placed([P, S], U32, "picked_words0", AT_PICKED0), held([P, S], U32, "picked_words1")]
 
         def gather_words(a, j0, j1):
             nc.vector.tensor_copy(
                 picked_words[a][:, j0:j1], tab_w[a][:].bitcast(U32).indirect(offs_sb[:, j0 // 16 : j1 // 16])
             )
 
-        gathered_sc = placed([P, S], U8, "gathered_sc", AT_GATHERED)
-        nc.vector.tensor_copy(gathered_sc[:], tab_sc[:].indirect(offs_sb[:]))
-        nc.sync.dma_start(staged[0:P:8, ROW : ROW + S].bitcast(I32), gathered_sc[4:P:8, :].bitcast(I32))
+        gathered_sc = placed([P, GATHERED_BYTES], U8, "gathered_sc", AT_GATHERED)[:, :S]
+        nc.vector.tensor_copy(gathered_sc, tab_sc[:].indirect(offs_sb[:]))
+        nc.vector.tensor_copy(staged[:, :S].bitcast(I32), gathered_sc.bitcast(I32))
+
+        def move_scales(a):
+            for r in range(4):
+                nc.sync.dma_start(
+                    planes[a][r:P:32, :].bitcast(I32), staged[8 * r + 4 * a : P : 32, :].bitcast(I32)
+                )
+
+        move_scales(0)
         load_words(1)
         wa_sb = placed([P, 2, H // 2], I32, "wa_sb", AT_WA)
         nc.sync.dma_start(wa_sb[:], wa_words.rearrange("a p n -> p a n").bitcast(I32))
+        move_scales(1)
         nc.scalar.activation(*walk(0, 0, H), ACT.Copy, scale=-1.0)
-        nc.vector.tensor_copy(staged[:, :S].bitcast(I32), gathered_sc[:].bitcast(I32))
-        for r in range(4):
-            nc.sync.dma_start(plane[r:P:32, :].bitcast(I32), staged[8 * r : P : 32, :].bitcast(I32))
-
         nc.sync.dma_start(wb_raw[1], wb_rows[1])
         wd_raw = placed([P, 4 * N], F32, "wd_raw", AT_WD)[:]
         nc.sync.dma_start(wd_raw, wd.rearrange("(p j) c -> p (j c)", j=4))
 
         gather_words(0, 0, S)
-        clear(1)
         clear(2)
+        clear(3)
         gather_words(1, 0, AHEAD * P)
         quantise_wb(0)
         gather_words(1, AHEAD * P, S)
-        clear(3)
         nc.vector.tensor_scalar(*walk(1, 0, H), -1.0, 0.0, ALU.mult, ALU.add)
         quantise_wb(1)
         wgo_sb = placed([P, S], F32, "wgo_sb", AT_WGO)[:]
         nc.sync.dma_start(wgo_sb, wgo)
 
         def wc_mx(a, c0=0, c1=H):
-            return wc_sb[:, a, c0:c1].bitcast(FP8X4), plane[:, ROW * a + S + c0 : ROW * a + S + c1]
+            return wc_sb[:, a, c0:c1].bitcast(FP8X4), planes[a][:, S + c0 : S + c1]
 
         def wa_mx(a, c0=0, c1=H):
-            return wa_sb[:, a, c0 // 2 : c1 // 2].bitcast(FP4X4), plane[:, ROW * a + S + H + c0 : ROW * a + S + H + c1]
+            return wa_sb[:, a, c0 // 2 : c1 // 2].bitcast(FP4X4), planes[a][:, S + H + c0 : S + H + c1]
 
         def neg_wb_mx(a, c0=0, c1=H):
             return neg_wb_q[a][:, c0:c1].bitcast(FP8X4), neg_wb_sc[a][:, c0:c1]
 
         def picked_mx(a, k):
-            return picked_words[a][:, P * k : P * (k + 1)].bitcast(FP8X4), plane[:, ROW * a + P * k : ROW * a + P * (k + 1)]
+            return picked_words[a][:, P * k : P * (k + 1)].bitcast(FP8X4), planes[a][:, P * k : P * (k + 1)]
 
         def mx_pass(acc, stationary, moving, start, stop):
             nc.tensor.matmul_mx(
@@ -183,31 +190,29 @@ def tile_list_skill_disagreement_marks_kernel(
 
         def product(k, bank, *weights):
             acc = bank_tile(bank)
-            passes = [(a, weight) for weight in weights for a in range(2)]
+            passes = [(a, weight) for weight in weights for a in ((0, 1) if k < AHEAD else (1, 0))]
             for n, (a, weight) in enumerate(passes):
                 mx_pass(acc[:], picked_mx(a, k), weight(a), n == 0, n == len(passes) - 1)
             return by_slot(acc)
 
         def mostly_less_b(k, weight):
             acc = bank_tile("mm")
-            for a in range(2):
-                mx_pass(acc[:], picked_mx(a, k), weight(a), a == 0, False)
+            for a in (1, 0):
+                mx_pass(acc[:], picked_mx(a, k), weight(a), a == 1, False)
             for c0, c1 in ((0, H // 2), (H // 2, SHARED)):
                 for a in range(2):
                     mx_pass(acc[:, c0:c1], picked_mx(a, k), neg_wb_mx(a, c0, c1), False, a == 1 and c1 == SHARED)
             return by_slot(acc)
 
-        def product_by_rows(k, weight, name):
+        def product_by_rows(k, weight):
             acc = bank_tile("mm")
-            for a in range(2):
+            for a in (1, 0):
                 for i in range(4):
                     mx_pass(
                         acc[:, P * i : P * (i + 1)], weight(a, P * i, P * (i + 1)), picked_mx(a, k),
-                        a == 0 and i == 0, a == 1 and i == 3,
+                        a == 1 and i == 0, a == 0 and i == 3,
                     )
-            rows_sb = term(name)
-            nc.scalar.copy(rows_sb[:], acc[:])
-            return rows_sb
+            return acc
 
         def turned_sum(first, second):
             acc = bank_tile("mm")
@@ -235,7 +240,19 @@ def tile_list_skill_disagreement_marks_kernel(
 
         def row_part(k, n):
             weight, name = ((neg_wb_mx, "nb"), (wc_mx, "c"), (wa_mx, "u"))[n]
-            by_rows.setdefault(k, []).append(product_by_rows(k, weight, name))
+            acc = product_by_rows(k, weight)
+            by_rows[k, name] = term(name)
+            nc.scalar.copy(by_rows[k, name][:], acc[:])
+            if name == "c" and k > TURNED:
+                by_rows[k, "nc"] = term("d")
+                nc.scalar.activation(by_rows[k, "nc"][:], acc[:], ACT.Copy, scale=-1.0)
+
+        def turned_term(k, first, second, sign, name):
+            part = term(name)
+            nc.scalar.activation(
+                slots(part[:]), turned_sum(by_rows[k, first], by_rows[k, second]), ACT.Relu, scale=sign
+            )
+            summands.setdefault(k, []).append(part)
 
         def first_part(k):
             if k < PLAIN:
@@ -250,12 +267,18 @@ def tile_list_skill_disagreement_marks_kernel(
             elif k == PLAIN:
                 d_sb[k] = term("d")
                 nc.scalar.copy(slots(d_sb[k][:]), mostly_less_b(k, wc_mx))
-            elif k >= TURNED:
-                take_d(k, turned_sum(by_rows[k][0], by_rows[k][1]))
+            elif k > TURNED:
+                turned_term(k, "nb", "c", 1.0, "rd")
+            elif k == TURNED:
+                take_d(k, turned_sum(by_rows[k, "nb"], by_rows[k, "c"]))
             else:
                 take_d(k, product(k, "mm", wc_mx, neg_wb_mx))
 
         def second_part(k):
+            if k > TURNED:
+                turned_term(k, "nb", "u", -1.0, "ru")
+                turned_term(k, "nc", "u", 1.0, "top")
+                return
             ru, top = term("ru"), term("top")
             if k < PLAIN:
                 u = term("u")
@@ -265,8 +288,8 @@ def tile_list_skill_disagreement_marks_kernel(
             elif k == PLAIN:
                 cut = SHARED // 4
                 rest = bank_tile("mm")
-                for a in range(2):
-                    mx_pass(rest[:, SHARED:], picked_mx(a, k), neg_wb_mx(a, SHARED, H), a == 0, a == 1)
+                for a in (1, 0):
+                    mx_pass(rest[:, SHARED:], picked_mx(a, k), neg_wb_mx(a, SHARED, H), a == 1, a == 0)
                 u_ps = mostly_less_b(k, wa_mx)
                 d, u, rd = slots(d_sb[k][:]), slots(term("u")[:]), term("rd")
                 nc.vector.tensor_tensor(u[:, :, cut:], by_slot(rest)[:, :, cut:], d[:, :, cut:], ALU.add)
@@ -278,8 +301,8 @@ def tile_list_skill_disagreement_marks_kernel(
                 nc.vector.tensor_tensor(slots(top[:])[:, :, cut:], u[:, :, cut:], d[:, :, cut:], ALU.max)
                 summands[k] = [rd]
             else:
-                if k >= TURNED:
-                    u_ps = turned_sum(by_rows[k][0], by_rows[k][2])
+                if k == TURNED:
+                    u_ps = turned_sum(by_rows[k, "nb"], by_rows[k, "u"])
                 else:
                     u_ps = product(k, "mm", wa_mx, neg_wb_mx)
                 relu_neg(slots(ru[:]), u_ps)

@@ -21,7 +21,7 @@ P = 128
 TILES = S // P
 SHARED = 3 * H // 4
 ROW = S + 2 * H
-EDGE = 64
+EDGE = 256
 BANKS = {"mm": 4, "h": 2, "y": 2}
 PLAIN = 3
 TURNED = 6
@@ -56,10 +56,10 @@ def tile_list_skill_disagreement_marks_kernel(
         psum = ctx.enter_context(tc.psum_pool(name="psum", bufs=2))
 
         def placed(shape, dtype, name, offset):
-            return arena.tile(shape, dtype, name=name, offset=offset, align_bytes=64)
+            return arena.tile(shape, dtype, name=name, offset=offset, align_bytes=EDGE)
 
         def held(shape, dtype, name):
-            return keep.tile(shape, dtype, name=name, align_bytes=64)
+            return keep.tile(shape, dtype, name=name, align_bytes=EDGE)
 
         def term(name):
             return ring.tile([P, H], F32, name=name, align_bytes=64)

from contextlib import ExitStack

import concourse.mybir as mybir
from concourse.masks import make_identity

K, H, N, T, S, T2 = 1024, 512, 512, 2048, 1024, 2048
FLOPS = 3 * 2 * K * H * S + 2 * H * N * S

F32 = mybir.dt.float32
BF16 = mybir.dt.bfloat16
I32 = mybir.dt.int32
U32 = mybir.dt.uint32
U16 = mybir.dt.uint16
U8 = mybir.dt.uint8
FP8X4 = mybir.dt.float8_e4m3fn_x4
FP4X4 = mybir.dt.float4_e2m1fn_x4
ALU = mybir.AluOpType
ACT = mybir.ActivationFunctionType

P = 128
TILES = S // P
SHARED = 3 * H // 4
ROW = S + 2 * H
EDGE = 256
BANKS = {"mm": 4, "h": 2, "y": 2}
PLAIN = 3
TURNED = 6
AHEAD = 3
DEPTH = 4

AT_PAGE2 = 0
AT_TAB0 = AT_PAGE2 + 4 * T2 - EDGE
AT_PAGE3 = AT_TAB0 + 4 * T - EDGE
AT_WGO = AT_PAGE3 + 4 * T2
AT_WB1 = AT_WGO + 4 * S - EDGE
AT_BEHIND_CAST = AT_WB1 + EDGE
AT_GATHERED = AT_WB1 + 16 * H - EDGE
GATHERED_BYTES = 4 * H + 2 * EDGE
AT_TAB1 = AT_GATHERED + GATHERED_BYTES - EDGE
AT_STAGED = AT_TAB1 + 4 * T
AT_WD = AT_STAGED + ROW - EDGE
AT_WA = AT_GATHERED + EDGE
AT_TAB_SC = AT_WD + 16 * N
AT_PICKED0 = AT_TAB_SC + T - EDGE


def tile_list_skill_disagreement_marks_kernel(
    tc, tab_words, tab_scales, offs, wa_words, wa_scales, wb, wc_words, wc_scales, wd, usual, wgo, offs2, out
):
    nc = tc.nc
    with ExitStack() as ctx:
        lists = ctx.enter_context(tc.tile_pool(name="lists", bufs=1))
        keep = ctx.enter_context(tc.tile_pool(name="keep", bufs=1))
        ring = ctx.enter_context(tc.tile_pool(name="ring", bufs=DEPTH))
        arena = ctx.enter_context(tc.tile_pool(name="arena", bufs=1))
        psum = ctx.enter_context(tc.psum_pool(name="psum", bufs=2))

        def placed(shape, dtype, name, offset):
            return arena.tile(shape, dtype, name=name, offset=offset, align_bytes=EDGE)

        def held(shape, dtype, name):
            return keep.tile(shape, dtype, name=name, align_bytes=EDGE)

        def term(name):
            return ring.tile([P, H], F32, name=name, align_bytes=64)

        offs_sb = lists.tile([P, S // 16], U16, name="offs_sb")
        offs2_sb = lists.tile([P, S // 16], U16, name="offs2_sb")
        tab_sc = placed([P, T], U8, "tab_sc", AT_TAB_SC)
        nc.vector.memset(tab_sc[:].bitcast(I32), 0)
        planes = [held([P, ROW], U8, "plane%d" % a) for a in range(2)]
        staged = placed([P, ROW], U8, "staged", AT_STAGED)
        zero = held([P, 1], U32, "zero")
        nc.vector.memset(zero[:], 0)
        for plane in planes:
            nc.scalar.copy(plane[:].bitcast(U32), zero[:].to_broadcast([P, ROW // 4]))

        def load_weight_scales(c0, src):
            nc.sync.dma_start(
                staged[0:P:4, c0 : c0 + H].bitcast(I32), src.bitcast(I32).rearrange("a q t -> q a t")
            )

        nc.sync.dma_start(offs_sb[:], offs)
        load_weight_scales(S, wc_scales)
        load_weight_scales(S + H, wa_scales)
        nc.sync.dma_start(offs2_sb[:], offs2)
        usual_sb = held([P, 4], F32, "usual_sb")
        nc.sync.dma_start(usual_sb[:], usual.rearrange("(p i) -> p i", i=4))
        nc.sync.dma_start(tab_sc[0:P:4, :].bitcast(I32), tab_scales.bitcast(I32).rearrange("a q t -> q a t"))

        tab_w = [placed([P, T], I32, "tab_w0", AT_TAB0), placed([P, T], I32, "tab_w1", AT_TAB1)]
        wb_rows = wb.rearrange("(a p j) c -> a p (j c)", a=2, j=4)
        wb_raw = [held([P, 4 * H], F32, "wb_raw0")[:], placed([P, 4 * H], F32, "wb_raw1", AT_WB1)[:]]

        def load_words(a):
            nc.sync.dma_start(tab_w[a][:], tab_words[a].rearrange("p t i -> p (t i)").bitcast(I32))

        load_words(0)
        nc.sync.dma_start(wb_raw[0], wb_rows[0])
        wc_sb = held([P, 2, H], I32, "wc_sb")
        nc.sync.dma_start(wc_sb[:], wc_words.rearrange("a p e i -> p a (e i)").bitcast(I32))

        pages = [held([P, T2], F32, "page%d" % i) for i in range(2)]
        pages.extend(placed([P, T2], F32, "page%d" % (i + 2), at) for i, at in enumerate((AT_PAGE2, AT_PAGE3)))

        def clear(i):
            nc.vector.memset(pages[i][:].bitcast(I32), 0)

        ident = held([P, P], F32, "ident")
        make_identity(nc, ident[:])
        clear(0)
        clear(1)
        neg_usual = held([P, 4], F32, "neg_usual")
        nc.scalar.activation(neg_usual[:], usual_sb[:], ACT.Identity, scale=-1.0)

        neg_wb_bf = [held([P, 4 * H], BF16, "neg_wb_bf%d" % a) for a in range(2)]
        neg_wb_q = [held([P, H], U32, "neg_wb_q%d" % a) for a in range(2)]
        neg_wb_sc = [held([P, H], U8, "neg_wb_sc%d" % a) for a in range(2)]

        def walk(a, c0, c1):
            return (
                neg_wb_bf[a][:, 4 * c0 : 4 * c1].rearrange("p (c j) -> p c j", j=4),
                wb_raw[a].rearrange("p (j c) -> p c j", j=4)[:, c0:c1, :],
            )

        def quantise_wb(a):
            nc.vector.quantize_mx(out=neg_wb_q[a][:].bitcast(FP8X4), scales=neg_wb_sc[a][:], in_=neg_wb_bf[a][:])

        picked_words = [placed([P, S], U32, "picked_words0", AT_PICKED0), held([P, S], U32, "picked_words1")]

        def gather_words(a, j0, j1):
            nc.vector.tensor_copy(
                picked_words[a][:, j0:j1], tab_w[a][:].bitcast(U32).indirect(offs_sb[:, j0 // 16 : j1 // 16])
            )

        gathered_sc = placed([P, GATHERED_BYTES], U8, "gathered_sc", AT_GATHERED)[:, :S]
        nc.vector.tensor_copy(gathered_sc, tab_sc[:].indirect(offs_sb[:]))
        nc.vector.tensor_copy(staged[:, :S].bitcast(I32), gathered_sc.bitcast(I32))

        def move_scales(a):
            for r in range(4):
                nc.sync.dma_start(
                    planes[a][r:P:32, :].bitcast(I32), staged[8 * r + 4 * a : P : 32, :].bitcast(I32)
                )

        move_scales(0)
        load_words(1)
        wa_sb = placed([P, 2, H // 2], I32, "wa_sb", AT_WA)
        nc.sync.dma_start(wa_sb[:], wa_words.rearrange("a p n -> p a n").bitcast(I32))
        move_scales(1)
        nc.scalar.activation(*walk(0, 0, H), ACT.Copy, scale=-1.0)
        nc.sync.dma_start(wb_raw[1], wb_rows[1])
        wd_raw = placed([P, 4 * N], F32, "wd_raw", AT_WD)[:]
        nc.sync.dma_start(wd_raw, wd.rearrange("(p j) c -> p (j c)", j=4))

        gather_words(0, 0, S)
        clear(2)
        clear(3)
        gather_words(1, 0, AHEAD * P)
        quantise_wb(0)
        gather_words(1, AHEAD * P, S)
        nc.vector.tensor_scalar(*walk(1, 0, H), -1.0, 0.0, ALU.mult, ALU.add)
        quantise_wb(1)
        wgo_sb = placed([P, S], F32, "wgo_sb", AT_WGO)[:]
        nc.sync.dma_start(wgo_sb, wgo)

        def wc_mx(a, c0=0, c1=H):
            return wc_sb[:, a, c0:c1].bitcast(FP8X4), planes[a][:, S + c0 : S + c1]

        def wa_mx(a, c0=0, c1=H):
            return wa_sb[:, a, c0 // 2 : c1 // 2].bitcast(FP4X4), planes[a][:, S + H + c0 : S + H + c1]

        def neg_wb_mx(a, c0=0, c1=H):
            return neg_wb_q[a][:, c0:c1].bitcast(FP8X4), neg_wb_sc[a][:, c0:c1]

        def picked_mx(a, k):
            return picked_words[a][:, P * k : P * (k + 1)].bitcast(FP8X4), planes[a][:, P * k : P * (k + 1)]

        def mx_pass(acc, stationary, moving, start, stop):
            nc.tensor.matmul_mx(
                out=acc, lhsT=stationary[0], lhsT_scale=stationary[1], rhs=moving[0], rhs_scale=moving[1],
                start=start, stop=stop,
            )

        def bank_tile(bank):
            return psum.tile([P, H], F32, name="acc", tag=bank, bufs=BANKS[bank])

        def by_slot(acc):
            return acc[:].rearrange("p (m t) -> p t m", t=4)

        def product(k, bank, *weights):
            acc = bank_tile(bank)
            passes = [(a, weight) for weight in weights for a in ((0, 1) if k < AHEAD else (1, 0))]
            for n, (a, weight) in enumerate(passes):
                mx_pass(acc[:], picked_mx(a, k), weight(a), n == 0, n == len(passes) - 1)
            return by_slot(acc)

        def mostly_less_b(k, weight):
            acc = bank_tile("mm")
            for a in (1, 0):
                mx_pass(acc[:], picked_mx(a, k), weight(a), a == 1, False)
            for c0, c1 in ((0, H // 2), (H // 2, SHARED)):
                for a in range(2):
                    mx_pass(acc[:, c0:c1], picked_mx(a, k), neg_wb_mx(a, c0, c1), False, a == 1 and c1 == SHARED)
            return by_slot(acc)

        def product_by_rows(k, weight):
            acc = bank_tile("mm")
            for a in (1, 0):
                for i in range(4):
                    mx_pass(
                        acc[:, P * i : P * (i + 1)], weight(a, P * i, P * (i + 1)), picked_mx(a, k),
                        a == 1 and i == 0, a == 0 and i == 3,
                    )
            return acc

        def turned_sum(first, second):
            acc = bank_tile("mm")
            for e, rows_sb in enumerate((first, second)):
                for i in range(4):
                    nc.tensor.matmul(
                        acc[:, P * i : P * (i + 1)], rows_sb[:, P * i : P * (i + 1)], ident[:],
                        start=(e == 0 and i == 0), stop=(e == 1 and i == 3), is_transpose=True,
                    )
            return by_slot(acc)

        def slots(ap):
            return ap.rearrange("p (t m) -> p t m", t=4)

        def relu_neg(dst, src):
            nc.scalar.activation(dst, src, ACT.Relu, scale=-1.0)

        c_sb, d_sb, summands, by_rows = {}, {}, {}, {}

        def take_d(k, d_ps):
            d_sb[k], rd = term("d"), term("rd")
            nc.scalar.copy(slots(d_sb[k][:]), d_ps)
            relu_neg(slots(rd[:]), d_ps)
            summands[k] = [rd]

        def row_part(k, n):
            weight, name = ((neg_wb_mx, "nb"), (wc_mx, "c"), (wa_mx, "u"))[n]
            acc = product_by_rows(k, weight)
            by_rows[k, name] = term(name)
            nc.scalar.copy(by_rows[k, name][:], acc[:])
            if name == "c" and k > TURNED:
                by_rows[k, "nc"] = term("d")
                nc.scalar.activation(by_rows[k, "nc"][:], acc[:], ACT.Copy, scale=-1.0)

        def turned_term(k, first, second, sign, name):
            part = term(name)
            nc.scalar.activation(
                slots(part[:]), turned_sum(by_rows[k, first], by_rows[k, second]), ACT.Relu, scale=sign
            )
            summands.setdefault(k, []).append(part)

        def first_part(k):
            if k < PLAIN:
                bank = "h" if k == AHEAD - 1 else "mm"
                c_sb[k] = term("c")
                d_sb[k] = placed([P, H], F32, "d%d" % k, AT_BEHIND_CAST + 4 * H * (k - 1)) if k else term("d")
                rd = term("rd")
                nc.scalar.copy(slots(c_sb[k][:]), product(k, bank, wc_mx))
                nc.vector.tensor_tensor(slots(d_sb[k][:]), slots(c_sb[k][:]), product(k, bank, wa_mx), ALU.subtract)
                relu_neg(rd[:], d_sb[k][:])
                summands[k] = [rd]
            elif k == PLAIN:
                d_sb[k] = term("d")
                nc.scalar.copy(slots(d_sb[k][:]), mostly_less_b(k, wc_mx))
            elif k > TURNED:
                turned_term(k, "nb", "c", 1.0, "rd")
            elif k == TURNED:
                take_d(k, turned_sum(by_rows[k, "nb"], by_rows[k, "c"]))
            else:
                take_d(k, product(k, "mm", wc_mx, neg_wb_mx))

        def second_part(k):
            if k > TURNED:
                turned_term(k, "nb", "u", -1.0, "ru")
                turned_term(k, "nc", "u", 1.0, "top")
                return
            ru, top = term("ru"), term("top")
            if k < PLAIN:
                u = term("u")
                nc.vector.tensor_tensor(slots(u[:]), product(k, "y" if k < AHEAD - 1 else "mm", neg_wb_mx), slots(c_sb[k][:]), ALU.add)
                relu_neg(ru[:], u[:])
                nc.vector.tensor_tensor(top[:], u[:], d_sb[k][:], ALU.max)
            elif k == PLAIN:
                cut = SHARED // 4
                rest = bank_tile("mm")
                for a in (1, 0):
                    mx_pass(rest[:, SHARED:], picked_mx(a, k), neg_wb_mx(a, SHARED, H), a == 1, a == 0)
                u_ps = mostly_less_b(k, wa_mx)
                d, u, rd = slots(d_sb[k][:]), slots(term("u")[:]), term("rd")
                nc.vector.tensor_tensor(u[:, :, cut:], by_slot(rest)[:, :, cut:], d[:, :, cut:], ALU.add)
                nc.vector.tensor_tensor(d[:, :, cut:], d[:, :, cut:], u_ps[:, :, cut:], ALU.subtract)
                relu_neg(slots(ru[:])[:, :, :cut], u_ps[:, :, :cut])
                relu_neg(slots(ru[:])[:, :, cut:], u[:, :, cut:])
                relu_neg(rd[:], d_sb[k][:])
                nc.vector.tensor_tensor(slots(top[:])[:, :, :cut], u_ps[:, :, :cut], d[:, :, :cut], ALU.max)
                nc.vector.tensor_tensor(slots(top[:])[:, :, cut:], u[:, :, cut:], d[:, :, cut:], ALU.max)
                summands[k] = [rd]
            else:
                if k == TURNED:
                    u_ps = turned_sum(by_rows[k, "nb"], by_rows[k, "u"])
                else:
                    u_ps = product(k, "mm", wa_mx, neg_wb_mx)
                relu_neg(slots(ru[:]), u_ps)
                nc.vector.tensor_tensor(slots(top[:]), u_ps, slots(d_sb[k][:]), ALU.max)
            summands[k].extend([ru, top])

        h_q = held([P, S], U32, "h_q")
        h_sc = held([P, S], U8, "h_sc")

        def turn(k):
            h_ps = psum.tile([P, 4, P], F32, name="h_ps", tag="h", bufs=BANKS["h"])
            for e, summand in enumerate(summands[k]):
                for t in range(4):
                    nc.tensor.matmul(
                        h_ps[:, t, :], slots(summand[:])[:, t, :], ident[:],
                        start=(e == 0 and t == 0), stop=(e == 2 and t == 3), is_transpose=True,
                    )
            h_bf = ring.tile([P, 4 * P], BF16, name="h_bf", align_bytes=64)
            nc.scalar.copy(h_bf[:].rearrange("p (j t) -> p j t", t=4), h_ps[:].rearrange("p t j -> p j t"))
            nc.vector.quantize_mx(
                out=h_q[:, P * k : P * (k + 1)].bitcast(FP8X4), scales=h_sc[:, P * k : P * (k + 1)], in_=h_bf[:]
            )

        wd_bf = held([P, 4, P, 4], BF16, "wd_bf")
        wd_q = held([P, N], U32, "wd_q")
        wd_sc = held([P, N], U8, "wd_sc")

        def prepare_wd(i0, i1):
            nc.scalar.copy(
                wd_bf[:, i0:i1].rearrange("p i m j -> p m i j"),
                wd_raw.rearrange("p (j m i) -> p m i j", j=4, i=4)[:, :, i0:i1, :],
            )
            nc.vector.quantize_mx(
                out=wd_q[:, P * i0 : P * i1].bitcast(FP8X4),
                scales=wd_sc[:, P * i0 : P * i1],
                in_=wd_bf[:, i0:i1].rearrange("p i m j -> p (i m j)"),
            )

        rows = out.rearrange("(p i) t -> i p t", i=4)

        def place(pieces):
            width = sum(P * (k1 - k0) for i, k0, k1 in pieces)
            y_ps = psum.tile([P, width], F32, name="y_ps", tag="y", bufs=BANKS["y"])
            y_sb = ring.tile([P, width], F32, name="y_sb", align_bytes=64)
            starts = [sum(P * (k1 - k0) for i, k0, k1 in pieces[:n]) for n in range(len(pieces))]
            for at, (i, k0, k1) in zip(starts, pieces):
                for k in range(k0, k1, 2):
                    j0, j1 = P * k, P * min(k + 2, k1)
                    nc.tensor.matmul_mx(
                        out=y_ps[:, at + j0 - P * k0 : at + j1 - P * k0],
                        lhsT=wd_q[:, P * i : P * (i + 1)].bitcast(FP8X4),
                        lhsT_scale=wd_sc[:, P * i : P * (i + 1)],
                        rhs=h_q[:, j0:j1].bitcast(FP8X4),
                        rhs_scale=h_sc[:, j0:j1],
                        start=True,
                        stop=True,
                    )
            for at, (i, k0, k1) in zip(starts, pieces):
                col = slice(at, at + P * (k1 - k0))
                nc.scalar.activation(y_sb[:, col], y_ps[:, col], ACT.Identity, bias=neg_usual[:, i : i + 1])
            for at, (i, k0, k1) in zip(starts, pieces):
                j0, j1 = P * k0, P * k1
                nc.vector.tensor_tensor(
                    pages[i][:].indirect(offs2_sb[:, j0 // 16 : j1 // 16]),
                    y_sb[:, at : at + j1 - j0],
                    wgo_sb[:, j0:j1],
                    ALU.mult,
                )
                if k1 == TILES and i < 3:
                    nc.sync.dma_start(rows[i], pages[i][:])
                elif k1 == TILES:
                    for queue, c0 in ((nc.sync, 0), (nc.scalar, T2 // 2)):
                        queue.dma_start(rows[i][:, c0 : c0 + T2 // 2], pages[i][:, c0 : c0 + T2 // 2])

        first_part(0)
        first_part(1)
        first_part(2)
        second_part(0)
        second_part(1)
        prepare_wd(0, 2)
        second_part(2)
        turn(0)
        prepare_wd(2, 4)
        first_part(3)
        second_part(3)
        turn(1)
        place([(0, 0, 1), (1, 0, 1)])
        first_part(4)
        second_part(4)
        turn(2)
        place([(2, 0, 2), (3, 0, 2)])
        row_part(6, 0)
        first_part(5)
        row_part(6, 1)
        turn(3)
        place([(0, 1, 3), (1, 1, 3)])
        second_part(5)
        row_part(6, 2)
        turn(4)
        row_part(7, 0)
        place([(2, 2, 4), (3, 2, 4)])
        first_part(6)
        second_part(6)
        row_part(7, 1)
        row_part(7, 2)
        turn(5)
        place([(0, 3, 5), (1, 3, 5)])
        first_part(7)
        second_part(7)
        turn(6)
        place([(2, 4, 6), (1, 5, 6)])
        turn(7)
        place([(0, 5, 7)])
        place([(0, 7, 8), (1, 6, 8)])
        place([(2, 6, 8)])
        place([(3, 4, 8)])
